import numpy as np, ml_dtypes
CORES = [9,25,41,57]
N = 4
import mx_ref
BF = ml_dtypes.bfloat16
def pick(q, e):
    c = np.concatenate([q[0].reshape(128, -1, 4), np.zeros((128, 1, 4), np.uint8)], axis=1); s = np.concatenate([q[1], np.ones((16, 1), np.uint8)], axis=1)
    return (np.ascontiguousarray(c[:, e].reshape(128, -1)), np.ascontiguousarray(s[:, e]))
def join(*qs):
    return (np.concatenate([q[0] for q in qs], axis=1), np.concatenate([q[1] for q in qs], axis=1))
def put(q, e, v):
    c, s = q[0].reshape(128, -1, 4).copy(), q[1].copy(); c[:, e] = v[0].reshape(128, -1, 4); s[:, e] = v[1]
    return (c.reshape(128, -1), s)
def pk(c, s):
    return (np.ascontiguousarray(c), mx_ref.live(s))
def emit(q):
    return q[0], q[1]
def packed(v, rng):
    q = [mx_ref.quantize(np.ascontiguousarray(v[r])) for r in range(N)]
    return np.stack([a for a, b in q]), np.stack([mx_ref.plane(b, rng) for a, b in q])
def tile(rs):
    return np.stack(rs, axis=2).reshape(128, -1).astype(BF)
def f(rng, *shape):
    return mx_ref.flush((rng.standard_normal(shape, dtype=np.float32) * np.exp2(rng.integers(-2, 3, shape[:-1] + (1,)))).astype(BF))
def wide(rng, *shape, cols=0):
    v = rng.standard_normal(shape, dtype=np.float32) * np.exp2(rng.integers(-12, 13, shape)).astype(np.float32)
    if cols: v *= np.repeat(np.exp2(rng.integers(-cols, cols + 1, shape[:-2] + (1, shape[-1] // 4))) * (rng.random(shape[:-2] + (1, shape[-1] // 4)) > 0.0625), 4, axis=-1).astype(np.float32)
    return mx_ref.flush(v.astype(BF))
P, CAPP, LAST = 160, 64, 4
def times(t, v):
    return mx_ref.flush((t.astype(np.float32) * np.asarray(v, np.float32)).astype(BF))
def weights(rng, v):
    c, p = packed(times(f(rng, N, 128, 4096), v), rng)
    return {"wc": c, "ws": p}
def plain(rng):
    return {"x": f(rng, N, 128, 4 * P), "u": np.stack([f(rng, 128, 512)] * N), **weights(rng, 0.25)}
def tagged(rng, al, be, lo):
    d = plain(rng)
    x, u = np.array(d["x"]), np.array(d["u"])
    x[:, :24] = 0
    for p, v in ((0, al), (8, be), (16, lo)): x[:, p, ::4] = np.asarray(v, np.float32).astype(BF)
    u[:, :, :8] = 0
    u[:, 0, 0] = 2.0 ** 21
    u[:, 8, 4] = 2.0 ** 21
    u[:, 16, 4] = 1.0
    keep = ~np.isin(np.arange(1024) % 128, (0, 8, 16))
    return {"x": x, "u": u, **weights(rng, 0.25 * np.repeat(keep, 4))}
def setup_inputs(rng):
    return plain(rng)
def setup_inputs_ties(rng):
    return tagged(rng, rng.integers(-1, 1, (N, P)), rng.integers(-1, 1, (N, P)), np.zeros((N, P)))
def setup_inputs_near(rng):
    place = np.zeros((N, P), int) + np.arange(P)
    early = place < CAPP
    al = np.where(early, -((place + int(rng.integers(0, 2))) % 2), 4 * rng.integers(0, 2, (N, P)))
    lo = rng.integers(0, 8, (N, P))
    lo[0] = np.minimum(lo[0], 6)
    lo[1] = 7
    return tagged(rng, al, np.where(early, 0, 4), np.where(early, 0, lo))
def setup_inputs_crowd(rng):
    b = np.concatenate([[N - 1], rng.permutation(N - 2) + 1, [N]])
    a = np.where(np.roll(b, -1) > np.roll(b, -2), 16, -16)
    one = np.ones((1, P), int)
    a, b = a[:, None] * one, b[:, None] * one
    a[N - 3] = 16
    a[N - 2, P - 1] = -16
    a[N - 1, :CAPP - 1] = -16
    a[N - 1, P - 1] = -16
    b[N - 1, P - 1] = -16
    return tagged(rng, a, b, 0 * b)
def setup_inputs_huge(rng):
    d = plain(rng)
    sign = np.repeat(np.where(rng.random((N, 1, P)) < 0.25, -1.0, 1.0), 4, axis=2)
    u = np.array(d["u"])
    u[:, :, :8] = (-(1 + rng.random((128, 8))) * 2.0 ** 29).astype(np.float32).astype(BF)
    x = ((1 + rng.random((N, 128, 4 * P))) * 2.0 ** 27 * sign).astype(np.float32).astype(BF)
    return {"x": x, "u": u, **weights(rng, 0.125)}
def setup_inputs_spread(rng):
    return {**plain(rng), "x": wide(rng, N, 128, 4 * P, cols=6)}
def check_inputs(d):
    b = []
    for k in ("x", "u"):
        v = np.abs(d[k].astype(np.float32))
        if not (np.isfinite(v).all() and ((v == 0) | (v >= 2.0 ** -30) & (v <= 2.0 ** 30)).all()): b.append("a value of " + k)
    v = d["u"].astype(np.float32)
    if (v != v[:1]).any(): b.append("u isn't the same on every rank")
    return b
def reference(x, u, wc, ws):
    y, sp = np.zeros((N, 128, (LAST - 1) * P), np.float32), np.zeros((N, 1, (LAST - 1) * P), np.float32)
    oc, osc = np.zeros((N, 128, 4 * P), np.uint8), np.zeros((N, 16, P), np.uint8)
    tu = [mx_ref.quantize(np.ascontiguousarray(u[r])) for r in range(N)]
    wt = [[pick(pk(wc[r], ws[r]), np.arange(128 * m, 128 * m + 128)) for m in range(8)] for r in range(N)]
    cell = {1: [mx_ref.quantize(np.ascontiguousarray(x[r])) for r in range(N)]}
    got = {1: [mx_ref.matmul(tu[r], cell[1][r]) for r in range(N)]}
    for w in range(2, LAST + 1):
        cell[w], got[w] = [], []
        for r in range(N):
            home = [(r + k) % N for k in range(w)]
            at = [(np.arange(P) + (r + k) // N) % P for k in range(w)]
            score = np.stack([got[k][r][0] + got[w - k][home[k]][1][at[k]] for k in range(1, w)]) + np.float32(0)
            best = 1 + np.argmax(score, axis=0)
            slots, left, right = [], [], []
            for k in range(1, w):
                e = np.flatnonzero(best == k)[:CAPP]
                sp[r, 0, (w - 2) * P + e] = k
                fill = np.full(CAPP - len(e), -1)
                slots.append(np.concatenate([e, fill]))
                left.append(pick(cell[k][r], slots[-1]))
                right.append(pick(cell[w - k][home[k]], np.concatenate([at[k][e], fill])))
            a, b = join(*left), join(*right)
            z = [np.maximum(mx_ref.matmul(wt[r][t], a) + mx_ref.matmul(wt[r][4 + t], b), np.float32(0)) * np.float32(0.05) for t in range(4)]
            new = mx_ref.quantize(np.ascontiguousarray(tile(z)))
            e = np.concatenate(slots)
            used = np.flatnonzero(e >= 0)
            cell[w].append(put(cell[w - 1][r], e[used], pick(new, used)))
            got[w].append(mx_ref.matmul(tu[r], cell[w][r]))
            y[r, :, (w - 2) * P:(w - 1) * P] = got[w][r]
    for r in range(N): oc[r], osc[r] = emit(cell[LAST][r])
    return {"y": y, "oc": oc, "osc": osc, "sp": sp}

@@ -1,0 +1,509 @@
+from concourse.mybir import dt, AluOpType, ActivationFunctionType
+
+P, CAPP = 160, 64
+NL = P - CAPP
+X0 = NL - 2
+NX = P - X0
+V0 = P - 128
+BIG, GATE = 1.0e29, 2.0 ** 80
+CODE, PLANE, F, BF, I32, U16 = "float8_e4m3fn_x4", "uint8", "float32", "bfloat16", "int32", "uint16"
+C2, CB, CA, C1, CE = 0, 256, 512, 768, 1024
+N1, N12, N2, N3, WN = 704, 864, 930, 1090, 1156
+HB = NX + NL
+
+
+def _pair(name, n):
+    return {name + "q": ("sbuf", [128, n], CODE), name + "s": ("sbuf", [128, n], PLANE)}
+
+
+def _f(dtype, **kw):
+    return {k: ("sbuf", [128, n], dtype) for k, n in kw.items()}
+
+
+SCRATCH = {}
+for _n, _w in (("wt", 1024), ("uu", 128), ("uab", 256), ("win", CE + 2 * NL), ("wn", WN), ("pool", P), ("pland", P),
+               ("left", P), ("w4", 672), ("c4", P)):
+    SCRATCH.update(_pair(_n, _w))
+SCRATCH.update(_f(BF, hx=648, h2=648, hu=512, huab=1024, he=4 * (HB + P), h3x=512, h4=640, ones=128, keep=192,
+                  m2r=P, cum=NL, mb=256, sb=256))
+SCRATCH.update(_f(F, tmod=192, msk=192, spw=688, a1r=P, s1r=NL, s2r=P, ma=416, sa=416, mc=192, sc=192, md=80, sd=80,
+                  me=192, se=192, mf=P, sf=P, fx=32, fy=32, junk=64, s1x=NX, wr=P, ysb=3 * P, spr=3 * P, cst=8, cle=48,
+                  cgt=48, msg1=36, land1=18, land3=18, msg2=15, land2=15))
+SMALL, _at = {}, [0]
+for _n, _w in dict(d0=40, d1=40, e0=20, u6=10, wg=P + 16, s3=10, cr=80, qf=1, q3=1, pw=10, pw5=10, ph=6, k63=6, k64=6,
+                   jw=10, jc=10, o2=10, d32=6, d12=6, da=6, gx=6, t0=10, t1=10, t2=10, t3=10, t4=10, t5=10, uw=10,
+                   dw=10, xm=6, th1=6, th2=6, gg=12, xx=12, yy=12, b3w=12, gt=12, zz=12, ab=12, j16=16, sg=16, nn=1,
+                   nr=1, nq=1, n4=1, f4=4, f5=4, u0=6, u1=6, u3=6, s2p=10, thr=10, s1p=10, so=40,
+                   v0=10, v1=10, v2=10, v3=10, v4=10, v5=10, v6=10, e1=20, eo=20).items():
+    SMALL[_n] = (_at[0], _w)
+    _at[0] += _w
+SCRATCH.update(_f(F, small=_at[0]))
+SCRATCH.update(_f(I32, qi=1, qj=1, ci=10, cj=10))
+SCRATCH.update(_f(U16, off3=10, offp=10, offl=10, offk=10, off4=10, offs=10, offt=10))
+for _b in range(8):
+    SCRATCH["ps%d" % _b] = ("psum", [128, 512], F)
+ARR = ["an1q", "an1s", "an2q", "an2s", "an3q", "an3s", "an12q", "an12s", "am1", "am2", "am3", "apq", "aps"]
+SEMAPHORES = ["cg"] + ARR + ["sent"] + ["d%d" % i for i in range(16)] + ["cv", "cs", "ct"]
+
+
+def rank_program(g, core, T, topo):
+    rank = T.rank_of(core)
+    if rank is None:
+        return
+    n = len(T.cores)
+    A, ACT = AluOpType, ActivationFunctionType
+    eng = {"v": g.vector, "s": g.scalar, "t": g.tensor, "g": g, "y": g.sync}
+    own = {"v": "cv", "s": "cs", "t": "ct", "g": "cg"}
+    count = {k: 0 for k in SEMAPHORES}
+    known = {q: {} for q in eng}
+    clock = {}
+    log = {}
+    dmas = [0]
+
+    def R(name, a=0, b=None, s=1):
+        if name in SMALL:
+            at, w = SMALL[name]
+            return ("small", at + a, at + (w if b is None else b), s)
+        return (name, a, SCRATCH[name][1][1] if b is None else b, s)
+
+    def ap(r):
+        return T[r[0]][:, r[1]:r[2]] if r[3] == 1 else T[r[0]][:, r[1]:r[2]:r[3]]
+
+    def wait(q, ev):
+        if known[q].get(ev[0], 0) >= ev[1]:
+            return
+        eng[q].wait_ge(T.sem[ev[0]], ev[1])
+        for k, v in list(clock.get(ev, {}).items()) + [ev]:
+            if known[q].get(k, 0) < v:
+                known[q][k] = v
+
+    def order(q, reads, writes):
+        need = {}
+        for rs, wr in ((reads, False), (writes, True)):
+            for r in rs:
+                bank = r[0].startswith("ps")
+                for (a, b, st, ev, w, oq) in log.get(r[0], []):
+                    if bank:
+                        if oq == q:
+                            continue
+                    elif b <= r[1] or a >= r[2] or (st > 1 and st == r[3] and (a - r[1]) % st) or not (w or wr):
+                        continue
+                    need[ev[0]] = max(need.get(ev[0], 0), ev[1])
+        for k in sorted(need, key=lambda k: k == own.get(q)):
+            wait(q, (k, need[k]))
+
+    def note(q, tag, ev, reads, writes):
+        clock[ev] = dict(known[q])
+        for rs, wr in ((reads, False), (writes, True)):
+            for r in rs:
+                log.setdefault(r[0], []).append((r[1], r[2], r[3], ev, wr, tag))
+
+    def op(q, fn, reads, writes):
+        order(q, reads, writes)
+        count[own[q]] += 1
+        fn().then_inc(T.sem[own[q]], 1)
+        note(q, q, (own[q], count[own[q]]), reads, writes)
+
+    def dma(q, out, in_, reads, writes):
+        order(q, reads, writes)
+        s = "d%d" % dmas[0]
+        dmas[0] += 1
+        count[s] = 16
+        eng[q].dma_start(out, in_).then_inc(T.sem[s], 16)
+        note(q, "dma", (s, 16), reads, writes)
+
+    def peer(k):
+        return T.cores[(rank + k) % n]
+
+    def view(r):
+        return ap(r).bitcast(dt.uint8) if SCRATCH[r[0]][2] == CODE else ap(r)
+
+    def send(k, dst, src, sem):
+        order("g", [src], [])
+        to = peer(k)
+        rid, pid = topo.addr(to)[:2]
+        g.remote_dma(view(dst), view(src), T.sem[sem], T.sem.sent, pid, rid, topo.mask(core, to))
+        count["sent"] += len(topo.engines(core, to))
+
+    def lands(k, r, sem):
+        count[sem] = len(topo.engines(peer(k), core))
+        log.setdefault(r[0], []).append((r[1], r[2], 1, (sem, count[sem]), True, "far"))
+
+    def isr(x):
+        return isinstance(x, tuple)
+
+    def val(x):
+        return ap(x) if isr(x) else x
+
+    def tt(o, a, b, alu):
+        op("v", lambda: g.vector.tensor_tensor(ap(o), ap(a), ap(b), alu), [a, b], [o])
+
+    def ts(o, a, s1, op0, s2=None, op1=None):
+        rd = [a] + [x for x in (s1, s2) if isr(x)]
+        if op1 is None:
+            op("v", lambda: g.vector.tensor_scalar(ap(o), ap(a), val(s1), None, op0), rd, [o])
+        else:
+            op("v", lambda: g.vector.tensor_scalar(ap(o), ap(a), val(s1), val(s2), op0, op1), rd, [o])
+
+    def act(o, a, scale=None, bias=None, func=ACT.Identity, total=None):
+        kw = {}
+        if scale is not None:
+            kw["scale"] = val(scale)
+        if bias is not None:
+            kw["bias"] = val(bias)
+        if total is not None:
+            kw["accum_out"] = ap(total)
+        op("s", lambda: g.scalar.activation(ap(o), ap(a), func, **kw), [a] + [x for x in (scale, bias) if isr(x)],
+           [o] + ([total] if total else []))
+
+    def cp(o, a, q="v"):
+        if q == "v":
+            op("v", lambda: g.vector.tensor_copy(ap(o), ap(a)), [a], [o])
+        else:
+            act(o, a, None, None, ACT.Copy)
+
+    def fill(o, c):
+        op("v", lambda: g.vector.memset(ap(o), c), [], [o])
+
+    def scan(o, a, b, op0=A.mult):
+        op("v", lambda: g.vector.tensor_tensor_scan(ap(o), ap(a), ap(b), 0.0, op0, A.add), [a, b], [o])
+
+    def iota(o, pattern, base=0, cm=0):
+        if SCRATCH[o[0]][2] == I32:
+            op("g", lambda: g.iota(ap(o), pattern, base, cm), [], [o])
+        else:
+            op("g", lambda: g.iota(ap(o), pattern, base, cm, allow_small_or_imprecise_dtypes=True), [], [o])
+
+    def quant(name, a, w, h, ha=0):
+        q, s, i = R(name + "q", a, a + w), R(name + "s", a, a + w), R(h, 4 * ha, 4 * (ha + w))
+        op("v", lambda: g.vector.quantize_mx(ap(q), ap(s), ap(i)), [i], [q, s])
+
+    def PS(bank, a, b):
+        return R("ps%d" % bank, a, b)
+
+    def mm(bank, st, sa, mv, ma, w, start=True, stop=True):
+        rd = [R(st + "q", sa, sa + 128), R(st + "s", sa, sa + 128), R(mv + "q", ma, ma + w), R(mv + "s", ma, ma + w)]
+        o = PS(bank, 0, w)
+        op("t", lambda: g.tensor.matmul_mx(ap(o), ap(rd[0]), ap(rd[1]), ap(rd[2]), ap(rd[3]), start, stop), rd, [o])
+
+    def relu(q, h, ha, t, bank, a, b):
+        o, i = R(h, 4 * ha + t, 4 * (ha + b - a), 4), PS(bank, a, b)
+        if q == "v":
+            ts(o, i, 0.0, A.max, 0.05, A.mult)
+        else:
+            act(o, i, 0.05, None, ACT.Relu)
+
+    def pick(dst, da, src, sa, sb, off):
+        o, i, l = R(dst + "q", da, da + P), R(src + "q", sa, sb), R(off)
+        op("v", lambda: g.vector.tensor_copy(ap(o).bitcast(dt.uint32), ap(i).bitcast(dt.uint32).indirect(ap(l))),
+           [i, l], [o])
+        o2, i2 = R(dst + "s", da, da + P), R(src + "s", sa, sb)
+        op("s", lambda: g.scalar.activation(ap(o2), ap(i2).indirect(ap(l)), ACT.Copy), [i2, l], [o2])
+
+    def gather(q, o, win, off):
+        l = R(off)
+        if q == "v":
+            op("v", lambda: g.vector.tensor_copy(ap(o), ap(win).indirect(ap(l))), [win, l], [o])
+        else:
+            op("s", lambda: g.scalar.activation(ap(o), ap(win).indirect(ap(l)), ACT.Copy), [win, l], [o])
+
+    def mask(buf, a, src, pos):
+        w = src[2] - src[1]
+        tt(R(buf, a, a + w), src, R("msk", pos % 16, pos % 16 + w), A.mult)
+
+    def squeeze(o, i, a, b):
+        scan(R(o, a, b), R("keep", 0, b - a), R(i, a, b))
+
+    def W(buf, a, c):
+        return R(buf, a + 15, a + 16 * c, 16 if c > 1 else 1)
+
+    def places(buf, a, bank):
+        cp(R(buf, a, a + CAPP), PS(bank, NL, P), "s")
+        cp(R(buf, a + CAPP, a + P), PS(bank, 0, NL), "s")
+
+    shift = {k: (((rank - k) % n) + k) // n for k in (1, 2, 3)}
+    d = shift[1]
+    BANKS = (5, 6, 7, 0)
+    jw = "jw" if d else "pw"
+
+    for k, a, w, s in ((1, N1, P, "an1"), (2, N2, P, "an2"), (3, N3, NX, "an3"), (1, N12, NX, "an12")):
+        lands(k, R("wnq", a, a + w), s + "q")
+        lands(k, R("wns", a, a + w), s + "s")
+    lands(-1, R("land1"), "am1")
+    lands(-1, R("land3"), "am3")
+    lands(1, R("land2"), "am2")
+    lands(1, R("plandq"), "apq")
+    lands(1, R("plands"), "aps")
+
+    dma("y", ap(R("hx", 0, 4 * NL)), T.x[:, 4 * CAPP:4 * P], [], [R("hx", 0, 4 * NL)])
+    dma("s", ap(R("hx", 4 * NL, 648)), T.x[:, 0:648 - 4 * NL], [], [R("hx", 4 * NL, 648)])
+    dma("y", ap(R("hu")), T.u[:, :], [], [R("hu")])
+    dma("y", view(R("wtq", 0, 512)), T.wc[:, 0:2048], [], [R("wtq", 0, 512)])
+    dma("y", ap(R("wts")), T.ws[:, :], [], [R("wts")])
+    dma("y", view(R("wtq", 512, 1024)), T.wc[:, 2048:4096], [], [R("wtq", 512, 1024)])
+
+    iota(R("qi"), [[0, 1]], 0, 1)
+    iota(R("t0"), [[16, 10]])
+    iota(R("j16"), [[1, 16]])
+    iota(R("tmod"), [[0, 12], [1, 16]])
+    iota(R("cst"), [[1, 8]])
+    fill(R("small", 0, SMALL["wg"][0] + 16), 0.0)
+    ts(R("qj"), R("qi"), 15, A.bitwise_and)
+    fill(R("small", SMALL["s3"][0], SMALL["qf"][0]), -BIG)
+    cp(R("qf"), R("qj"))
+    fill(R("ones"), 1.0)
+    ts(R("pw"), R("t0"), R("qf"), A.add)
+    fill(R("dw"), float(CB - CA + X0))
+    ts(R("xm"), R("pw", 0, 6), X0 - 0.5, A.is_gt)
+    if d:
+        ts(R("t1"), R("pw"), P - 1.5, A.is_gt, -float(P), A.mult)
+        act(R("jw"), R("pw"), 1.0, 1.0)
+        tt(R("jw"), R("jw"), R("t1"), A.add)
+    fill(R("d0", 33, 40, 2), 0.5)
+    ts(R("t2"), R(jw), X0 - 0.5, A.is_gt, float(N12 - X0 - N1), A.mult)
+    act(R("jc"), R(jw), 1.0, float(N1 - 512))
+    act(R("ph"), R("pw", 0, 6), 1.0, 0.5)
+    ts(R("keep"), R("tmod"), 0.0, A.not_equal)
+    tt(R("o2"), R("t2"), R("jc"), A.add)
+    ts(R("msk"), R("tmod"), R("qf"), A.is_equal)
+    act(R("sg"), R("j16"), -1.0, R("ph", 0, 1), ACT.Sign)
+    act(R("pw5"), R("pw"), 1.0 / 512)
+    act(R("uw"), R("pw"), 1.0, float(CA - X0))
+    act(R("d1", 21, 40, 2), R("pw"), 1.0 / 512)
+    cp(R("e1", 1, 8, 2), R("pw", 6, 10), "s")
+    cp(R("e1", 9, 20, 2), R("pw", 0, 6), "s")
+    act(R("q3"), R("qf"), 3.0)
+    act(R("k63"), R("pw", 0, 6), -1.0, CAPP - 1.0)
+    act(R("k64"), R("pw", 0, 6), -1.0, float(CAPP))
+    act(R("gx"), R("xm"), -BIG)
+    act(R("da"), R("xm"), -float(P), float(CA + NX))
+    act(R("d32"), R("t2", 0, 6), -1.0, float(N2 - N1))
+    act(R("d12"), R("t2", 0, 6), -1.0, float(512 - N1))
+    act(R("d0", 13, 20, 2), R("t2", 6, 10), -1.0, float(512 - N1))
+    cp(R("d1", 13, 20, 2), R("o2", 6, 10), "s")
+    for i in range(3):
+        act(R("cle", i, 48, 3), R("sg"), 256.0 ** i, None, ACT.Relu)
+        act(R("cgt", i, 48, 3), R("sg"), -256.0 ** i, None, ACT.Relu)
+
+    quant("win", C1, P + 2, "hx")
+    for k, a, w, at, s in ((1, N1, P, 0, "an1"), (2, N2, P, 0, "an2"), (3, N3, NX, X0, "an3")):
+        for x in "qs":
+            b = C1 + at + shift[k]
+            send(-k, R("wn" + x, a, a + w), R("win" + x, b, b + w), s + x)
+    for t in range(4):
+        mm(t, "wt", 128 * t, "win", C1, P, True, False)
+    for t in range(4):
+        ts(R("huab", t, 512, 4), R("ones"), R("hu", t, t + 1), A.mult)
+        act(R("huab", 512 + t, 1024, 4), R("ones"), 0.0, R("hu", 4 + t, 5 + t))
+    cp(R("h2", 0, 4 * NL), R("hx", 0, 4 * NL), "s")
+    cp(R("h2", 4 * P, 648), R("hx", 4 * P, 648), "s")
+    quant("uab", 0, 256, "huab")
+    mm(4, "uab", 0, "win", C1, P)
+    for t in range(3):
+        mm(5 + t, "wt", 128 * t, "win", C1, 128, True, False)
+    quant("uu", 0, 128, "hu")
+    mask("ma", 0, PS(4, 0, P), 0)
+    cp(R("a1r"), PS(4, 0, P), "s")
+    quant("wn", 0, P, "hx")
+    squeeze("sa", "ma", 0, P)
+    cp(R("msg1", 0, 10), W("sa", 0, 10), "s")
+
+    for t in range(4):
+        mm(t, "wt", 512 + 128 * t, "wn", N1, P, False, True)
+    mm(4, "uab", 128, "wn", N1, 128)
+    for t in range(4):
+        relu("s", "h2", NL, t, t, NL, P)
+    quant("win", C2, P + 2, "h2")
+    for x in "qs":
+        send(-1, R("wn" + x, N12, N12 + NX), R("win" + x, C2 + X0 + d, C2 + P + d), "an12" + x)
+    tt(R("s1r"), R("a1r", 0, NL), PS(4, 0, NL), A.add)
+    mask("ma", 256, PS(4, d, NL + d), 0)
+    if d:
+        mask("ma", 415, PS(4, 0, 1), 15)
+    for t in range(4):
+        relu("s", "he", NX, t, t, 0, NL)
+    mm(1, "uab", 0, "win", C2 + V0, 128)
+    mm(0, "wt", 384, "win", C1, 128, True, False)
+    mm(2, "uab", 128, "win", C2 + V0 + 2, 128)
+    mm(4, "uab", 128, "wn", N2, P)
+    for t, bank in enumerate(BANKS):
+        mm(bank, "wt", 512 + 128 * t, "wn", N2, 128, False, True)
+    cp(R("s1x", 0, CAPP), PS(1, CAPP, 128), "s")
+    for t, bank in enumerate(BANKS):
+        relu("s", "he", HB, t, bank, 0, NL)
+    mask("me", 0, PS(1, CAPP, 128), 0)
+    tt(R("s2r", NL, P), R("s1x", 0, CAPP), PS(4, NL, P), A.add)
+    tt(R("s2r", 0, NL), R("a1r", 0, NL), PS(4, 0, NL), A.add)
+    mask("me", 64, R("s2r", NL, P), 0)
+    tt(R("m2r", 0, NL), R("s2r", 0, NL), R("s1r"), A.is_gt)
+    squeeze("se", "me", 0, 128)
+    quant("win", CE, 2 * NL, "he", NX)
+    mm(3, "uab", 0, "win", CE, 2 * NL)
+    cp(R("msg1", 10, 18), W("se", 0, 8), "s")
+    send(1, R("land1"), R("msg1", 0, 18), "am1")
+    scan(R("cum"), R("ones", 0, NL), R("m2r", 0, NL))
+    mask("mb", NL, R("m2r", 0, NL), 0)
+    mask("mb", 0, R("cum"), 0)
+    mask("mc", 0, PS(3, 0, 2 * NL), 0)
+    squeeze("sb", "mb", 0, 2 * NL)
+    squeeze("sc", "mc", 0, 2 * NL)
+    cw, mw = W("sb", 0, 6), W("sb", NL, 6)
+    act(R("gg", 0, 6), mw, -BIG)
+    act(R("gg", 6, 12), mw, BIG, -BIG)
+    tt(R("u0"), R("ph"), cw, A.subtract)
+    tt(R("u1"), R("k64"), mw, A.mult)
+    tt(R("xx", 6, 12), R("msg1", 0, 6), R("gg", 0, 6), A.add)
+    tt(R("xx", 0, 6), R("msg1", 0, 6), R("gg", 6, 12), A.add)
+    tt(R("yy"), W("sc", 0, 12), R("gg"), A.add)
+    tt(R("msg1", 18, 24), R("u0"), R("u1"), A.add)
+    tt(R("msg1", 24, 36), R("yy"), R("xx"), A.max)
+    send(1, R("land3"), R("msg1", 18, 36), "am3")
+    iota(R("h3x", 0, 4 * (128 - NX)), [[0, 4 * (128 - NX)]])
+    for a, b, c in ((0, CB, 0), (CB, CA, 2), (CA, 688, 1)):
+        iota(R("spw", a, b), [[0, b - a]], c)
+    iota(R("spr", 0, CAPP), [[0, CAPP]], 1)
+    iota(R("spr", CAPP, P), [[0, NL]])
+
+    for t, bank in enumerate(BANKS):
+        mm(bank, "wt", 128 * t, "win", C2 + V0, 128, True, False)
+        mm(bank, "wt", 512 + 128 * t, "wn", N2 + V0, 128, False, True)
+    for t, bank in enumerate(BANKS):
+        relu("s", "he", HB + X0, t, bank, 128 - NX, 128)
+    for t, bank in enumerate(BANKS):
+        mm(bank, "wt", 128 * t, "win", C1 + V0, 128, True, False)
+    mm(3, "uu", 0, "win", C2, P)
+    mask("me", 128, PS(2, CAPP - 2 + d, 126 + d), 0)
+    mask("ma", P, PS(4, d, NL + d), 0)
+    tt(R("th1"), R("u0"), mw, A.add)
+    squeeze("se", "me", 128, 192)
+    squeeze("sa", "ma", P, 336)
+    tt(R("th2"), R("th1"), R("k63"), A.add)
+    quant("win", CB, P, "he", HB)
+    tt(R("b3w", 0, 6), W("sa", P, 6), R("gx"), A.add)
+
+    mm(1, "uab", 128, "wn", N12 + NX - 128, 128)
+    for t, bank in enumerate(BANKS):
+        mm(bank, "wt", 512 + 128 * t, "wn", N12 + NX - 128, 128, False, True)
+    for t, bank in enumerate(BANKS):
+        relu("s", "he", 0, t, bank, 128 - NX, 128)
+    tt(R("s1x"), R("a1r", X0, P), PS(1, 128 - NX, 128), A.add)
+    mask("ma", 256 + X0 - d, PS(1, 128 - NX, 128), X0 - d)
+    tt(R("m2r", X0, P), R("s2r", X0, P), R("s1x"), A.is_gt)
+    squeeze("sa", "ma", 336, 416)
+    act(R("junk"), R("m2r", NL, P), None, None, ACT.Identity, R("nn"))
+    cp(R("b3w", 6, 12), R("b3w", 0, 6), "s")
+    mask("mb", NL + X0, R("m2r", X0, P), X0)
+    quant("win", CA, HB, "he")
+    ts(R("t0", 0, 6), R("th1"), R("nn"), A.is_lt)
+    ts(R("t1", 0, 6), R("th2"), R("nn"), A.is_gt, float(CB), A.mult)
+    squeeze("sb", "mb", 176, 256)
+    tt(R("t0", 0, 6), R("t0", 0, 6), R("da"), A.mult)
+    tt(R("f4"), R("land1", 6, 10), W("se", 128, 4), A.add)
+    tt(R("dw", 0, 6), R("t1", 0, 6), R("t0", 0, 6), A.subtract)
+    tt(R("uw", 0, 6), R("t0", 0, 6), R("pw", 0, 6), A.add)
+    tt(R("t3"), R("dw"), W("sb", NL, 10), A.mult)
+    tt(R("f5"), R("f4"), R("land1", 14, 18), A.is_lt)
+    tt(R("t4"), R("t3"), R("uw"), A.add)
+    act(R("junk", 0, 4), R("f5"), None, None, ACT.Identity, R("n4"))
+    act(R("fx"), R("ones", 0, 32), R("n4"), None, ACT.Copy)
+    tt(R("s2p", 0, 6), R("land1", 0, 6), W("sa", 256, 6), A.add)
+    cp(R("off3"), R("t4"))
+    tt(R("s2p", 6, 10), R("land1", 10, 14), W("sa", 256 + NL, 4), A.add)
+    pick("wn", 512, "win", 0, CA + HB, "off3")
+    mm(2, "uab", 128, "wn", 512, P)
+    op("v", lambda: g.vector.transpose(ap(R("fy")), ap(R("fx"))), [R("fx")], [R("fy")])
+    act(R("junk", 0, 16), R("fy", 0, 16), -GATE, None, ACT.Identity, R("nr"))
+    act(R("junk", 16, 32), R("fy", 0, 16), GATE, None, ACT.Identity, R("nq"))
+    act(R("gt", 0, 6), R("land3", 0, 6), GATE, R("nr"), ACT.Relu)
+    act(R("gt", 6, 12), R("land3", 0, 6), -GATE, R("nq"), ACT.Relu)
+    tt(R("ab"), R("land3", 6, 18), R("b3w"), A.add)
+    mask("mf", 0, PS(2, d, P), 0)
+    if d:
+        mask("mf", P - 1, PS(2, 0, 1), 15)
+    tt(R("zz"), R("ab"), R("gt"), A.subtract)
+    squeeze("sf", "mf", 0, P)
+    tt(R("s3", 0, 6), R("zz", 0, 6), R("zz", 6, 12), A.max)
+    tt(R("s1p"), R("land1", 0, 10), W("sf", 0, 10), A.add)
+    tt(R("t5", 0, 6), R("s3", 0, 6), R("s2p", 0, 6), A.is_gt)
+    tt(R("thr"), R("s3"), R("s2p"), A.max)
+    tt(R("u3"), R("t5", 0, 6), R("d32"), A.mult)
+    act(R("d0", 21, 32, 2), R("t5", 0, 6), 0.5, 0.5)
+    tt(R("d1", 0, 20, 2), R("s1p"), R("thr"), A.is_ge)
+    tt(R("d1", 1, 12, 2), R("u3"), R("o2", 0, 6), A.add)
+    tt(R("d0", 1, 12, 2), R("d12"), R("u3"), A.subtract)
+    tt(R("d1", 20, 40, 2), R("s1p"), R("thr"), A.is_lt)
+    scan(R("so"), R("d0"), R("d1"))
+    tt(R("msg2", 10, 15), R("s1p", 5, 10), R("thr", 5, 10), A.max)
+    cp(R("offp"), R("so", 1, 20, 2))
+    cp(R("msg2", 0, 10), R("so", 21, 40, 2), "s")
+    pick("pool", 0, "wn", 512, WN, "offp")
+    send(-1, R("land2"), R("msg2"), "am2")
+    send(-1, R("plandq"), R("poolq"), "apq")
+    send(-1, R("plands"), R("pools"), "aps")
+
+    mm(1, "uab", 0, "wn", 512 + V0, 128)
+    mm(2, "uab", 128, "wn", N3 + NX - 128, 128)
+    for t, bank in enumerate(BANKS):
+        mm(bank, "wt", 128 * t, "wn", 512 + V0, 128, True, False)
+        mm(bank, "wt", 512 + 128 * t, "wn", N3 + NX - 128, 128, False, True)
+    mm(4, "uu", 0, "wn", 512, P)
+    cp(R("s1x"), PS(1, 128 - NX, 128), "s")
+    for t, bank in enumerate(BANKS):
+        relu("s", "h3x", 128 - NX, t, bank, 128 - NX, 128)
+    quant("wn", 256, P, "h2")
+    tt(R("cr", 80 - NX, 80), R("s1x"), PS(2, 128 - NX, 128), A.add)
+    cp(R("offs", 0, 4), R("t4", 6, 10))
+    mask("md", 0, R("cr"), 0)
+    cp(R("offs", 4, 10), R("t4", 0, 6))
+    squeeze("sd", "md", 0, 80)
+    pick("w4", 0, "win", 0, CA + HB, "off3")
+    quant("w4", 512 + V0, 128, "h3x")
+    places("ysb", 0, 3)
+    places("ysb", P, 4)
+
+    tt(R("u6", 5, 10), W("sd", 0, 5), R("land2", 10, 15), A.is_gt)
+    tt(R("v0"), R("land2", 0, 10), R("pw5"), A.subtract)
+    ts(R("offl"), R("land2", 0, 10), 512.0, A.mult)
+    tt(R("v1", 0, 4), R("v0", 6, 10), R("u6", 6, 10), A.max)
+    tt(R("v1", 4, 10), R("v0", 0, 6), R("u6", 0, 6), A.max)
+    pick("left", 0, "wn", 0, 512 + P, "offl")
+    ts(R("offk"), R("v1"), 2.0, A.mult, R("q3"), A.add)
+    for t in range(4):
+        mm(t, "wt", 128 * t, "left", 0, P, True, False)
+    for t in range(4):
+        mm(t, "wt", 512 + 128 * t, "pland", 0, P, False, True)
+    dma("y", T.y[:, 0:2 * P], ap(R("ysb", 0, 2 * P)), [R("ysb", 0, 2 * P), R("plands")], [])
+    ts(R("v3"), R("v1"), 0.25, A.is_lt, 1.0 / 65536, A.max)
+    gather("v", R("wr"), R("cle"), "offk")
+    gather("s", R("wg", 16, P + 16), R("cgt"), "offk")
+    ts(R("v4"), R("v1"), 0.75, A.is_lt, 1.0 / 256, A.mult)
+    scan(R("sf"), R("wg", 0, P), R("wr"), A.add)
+    tt(R("v2"), R("v3"), R("v4"), A.max)
+    act(R("e0", 1, 8, 2), R("u6", 6, 10), 256.0, 256.0)
+    act(R("e0", 9, 20, 2), R("u6", 0, 6), 256.0, 256.0)
+    act(R("v5"), R("v1"), 2.0, 1.0)
+    tt(R("v3"), W("sf", 0, 10), R("v2"), A.mult)
+    ts(R("ci"), R("v3"), -0.2, A.add)
+    ts(R("cj"), R("ci"), 255, A.bitwise_and)
+    ts(R("e1", 0, 20, 2), R("cj"), CAPP + 0.5, A.is_lt)
+    scan(R("eo"), R("e0"), R("e1"))
+    tt(R("v6"), R("v5"), R("e1", 0, 20, 2), A.mult)
+    cp(R("off4"), R("eo", 1, 20, 2))
+    cp(R("offt"), R("v6"))
+    for t in range(4):
+        relu("sssv"[t], "h4", 0, t, t, 0, P)
+    quant("w4", 256, P, "h4")
+    gather("s", R("spr", 2 * P, 3 * P), R("cst"), "offt")
+    pick("c4", 0, "w4", 0, 672, "off4")
+    gather("v", R("spr", P, 2 * P), R("spw"), "offs")
+    mm(4, "uu", 0, "c4", 0, P)
+    dma("y", T.oc[:, :], view(R("c4q")), [R("c4q")], [])
+    cp(R("ysb", 2 * P, 3 * P), PS(4, 0, P), "s")
+    dma("s", T.y[:, 2 * P:3 * P], ap(R("ysb", 2 * P, 3 * P)), [R("ysb", 2 * P, 3 * P)], [])
+    for k in range(4):
+        dma("y", T.osc[4 * k:4 * k + 4, :], T.c4s[32 * k:32 * k + 4, :], [R("c4s")], [])
+    dma("y", T.sp[0:1, :], T.spr[0:1, :], [R("spr")], [])
+
+    for k in SEMAPHORES:
+        if count[k]:
+            wait("g", (k, count[k]))

@@ -28,12 +28,12 @@ SCRATCH.update(_f(BF, hx=648, h2=648, hu=512, huab=1024, he=4 * (HB + P), h3x=51
                   m2r=P, cum=NL, mb=256, sb=256))
 SCRATCH.update(_f(F, tmod=192, msk=192, spw=688, a1r=P, s1r=NL, s2r=P, ma=416, sa=416, mc=192, sc=192, md=80, sd=80,
                   me=192, se=192, mf=P, sf=P, fx=32, fy=32, junk=64, s1x=NX, wr=P, ysb=3 * P, spr=3 * P, cst=8, cle=48,
-                  cgt=48, msg1=36, land1=18, land3=18, msg2=15, land2=15))
+                  cgt=48, msg1=14, msg3=18, land1=14, land3=18, msg2=15, land2=15))
 SMALL, _at = {}, [0]
-for _n, _w in dict(d0=40, d1=40, e0=20, u6=10, wg=P + 16, s3=10, cr=80, qf=1, q3=1, pw=10, pw5=10, ph=6, k63=6, k64=6,
-                   jw=10, jc=10, o2=10, d32=6, d12=6, da=6, gx=6, t0=10, t1=10, t2=10, t3=10, t4=10, t5=10, uw=10,
-                   dw=10, xm=6, th1=6, th2=6, gg=12, xx=12, yy=12, b3w=12, gt=12, zz=12, ab=12, j16=16, sg=16, nn=1,
-                   nr=1, nq=1, n4=1, f4=4, f5=4, u0=6, u1=6, u3=6, s2p=10, thr=10, s1p=10, so=40,
+for _n, _w in dict(d0=60, d1=60, c0=30, c1=30, e0=20, u6=10, wg=P + 16, s3=10, cr=80, qf=1, q3=1, pw=10, pw5=10, ph=6,
+                   k63=6, k64=6, jw=10, da=1, t0=10, t1=10, t2=10, xm=6, gg=12, xx=12, yy=12, b3w=12, gt=12,
+                   zz=12, ab=12, j16=16, sg=16, nn=1, nr=1, nq=1, n4=1, f4=4, f5=4, f6=4, u0=6, u1=6, s2p=10, thr=10,
+                   s1p=10, so=60, co=30, sh=16, th5=1, th6=6, k5=1, g5=1,
                    v0=10, v1=10, v2=10, v3=10, v4=10, v5=10, v6=10, e1=20, eo=20).items():
     SMALL[_n] = (_at[0], _w)
     _at[0] += _w
@@ -226,6 +226,11 @@ def rank_program(g, core, T, topo):
     BANKS = (5, 6, 7, 0)
     jw = "jw" if d else "pw"
 
+    def first_cells(k, a, w, at, s):
+        for x in "qs":
+            b = C1 + at + shift[k]
+            send(-k, R("wn" + x, a, a + w), R("win" + x, b, b + w), s + x)
+
     for k, a, w, s in ((1, N1, P, "an1"), (2, N2, P, "an2"), (3, N3, NX, "an3"), (1, N12, NX, "an12")):
         lands(k, R("wnq", a, a + w), s + "q")
         lands(k, R("wns", a, a + w), s + "s")
@@ -253,43 +258,40 @@ def rank_program(g, core, T, topo):
     cp(R("qf"), R("qj"))
     fill(R("ones"), 1.0)
     ts(R("pw"), R("t0"), R("qf"), A.add)
-    fill(R("dw"), float(CB - CA + X0))
+    fill(R("c0", 2, 30, 3), 1.0)
+    fill(R("c0", 19, 30, 3), float(CB - CA + X0))
+    fill(R("c1", 19, 30, 3), float(CA - X0))
     ts(R("xm"), R("pw", 0, 6), X0 - 0.5, A.is_gt)
     if d:
         ts(R("t1"), R("pw"), P - 1.5, A.is_gt, -float(P), A.mult)
         act(R("jw"), R("pw"), 1.0, 1.0)
         tt(R("jw"), R("jw"), R("t1"), A.add)
-    fill(R("d0", 33, 40, 2), 0.5)
+    fill(R("d0", 31, 60, 3), 0.5)
+    fill(R("d1", 31, 60, 3), 0.5)
     ts(R("t2"), R(jw), X0 - 0.5, A.is_gt, float(N12 - X0 - N1), A.mult)
-    act(R("jc"), R(jw), 1.0, float(N1 - 512))
     act(R("ph"), R("pw", 0, 6), 1.0, 0.5)
-    ts(R("keep"), R("tmod"), 0.0, A.not_equal)
-    tt(R("o2"), R("t2"), R("jc"), A.add)
-    ts(R("msk"), R("tmod"), R("qf"), A.is_equal)
     act(R("sg"), R("j16"), -1.0, R("ph", 0, 1), ACT.Sign)
     act(R("pw5"), R("pw"), 1.0 / 512)
-    act(R("uw"), R("pw"), 1.0, float(CA - X0))
-    act(R("d1", 21, 40, 2), R("pw"), 1.0 / 512)
+    act(R("sh"), R("j16"), -1.0, R("qf"), ACT.Sign)
+    act(R("d1", 32, 60, 3), R("pw"), 1.0 / 512)
+    cp(R("c1", 2, 30, 3), R("pw"), "s")
     cp(R("e1", 1, 8, 2), R("pw", 6, 10), "s")
     cp(R("e1", 9, 20, 2), R("pw", 0, 6), "s")
     act(R("q3"), R("qf"), 3.0)
     act(R("k63"), R("pw", 0, 6), -1.0, CAPP - 1.0)
     act(R("k64"), R("pw", 0, 6), -1.0, float(CAPP))
-    act(R("gx"), R("xm"), -BIG)
-    act(R("da"), R("xm"), -float(P), float(CA + NX))
-    act(R("d32"), R("t2", 0, 6), -1.0, float(N2 - N1))
-    act(R("d12"), R("t2", 0, 6), -1.0, float(512 - N1))
-    act(R("d0", 13, 20, 2), R("t2", 6, 10), -1.0, float(512 - N1))
-    cp(R("d1", 13, 20, 2), R("o2", 6, 10), "s")
-    for i in range(3):
-        act(R("cle", i, 48, 3), R("sg"), 256.0 ** i, None, ACT.Relu)
-        act(R("cgt", i, 48, 3), R("sg"), -256.0 ** i, None, ACT.Relu)
+    act(R("g5"), R("xm", 5, 6), -BIG)
+    act(R("da"), R("xm", 5, 6), -float(P), float(CA + NX))
+    act(R("k5"), R("xm", 5, 6), float(P), -float(CA + NX + CB))
+    act(R("d0", 1, 18, 3), R("t2", 0, 6), -1.0, float(N2 - N1))
+    act(R("d1", 1, 30, 3), R("t2"), 1.0, float(N1 - 512))
+    cp(R("d1", 2, 30, 3), R(jw), "s")
 
     quant("win", C1, P + 2, "hx")
-    for k, a, w, at, s in ((1, N1, P, 0, "an1"), (2, N2, P, 0, "an2"), (3, N3, NX, X0, "an3")):
-        for x in "qs":
-            b = C1 + at + shift[k]
-            send(-k, R("wn" + x, a, a + w), R("win" + x, b, b + w), s + x)
+    first_cells(1, N1, P, 0, "an1")
+    first_cells(2, N2, P, 0, "an2")
+    ts(R("keep"), R("tmod"), 0.0, A.not_equal)
+    ts(R("msk"), R("tmod"), R("qf"), A.is_equal)
     for t in range(4):
         mm(t, "wt", 128 * t, "win", C1, P, True, False)
     for t in range(4):
@@ -304,65 +306,69 @@ def rank_program(g, core, T, topo):
     quant("uu", 0, 128, "hu")
     mask("ma", 0, PS(4, 0, P), 0)
     cp(R("a1r"), PS(4, 0, P), "s")
-    quant("wn", 0, P, "hx")
+    ts(R("sh"), R("sh"), 0.75, A.mult, 0.75, A.add)
     squeeze("sa", "ma", 0, P)
+    ts(R("sh"), R("sh"), 1.0, A.min)
     cp(R("msg1", 0, 10), W("sa", 0, 10), "s")
+    quant("wn", 0, P, "hx")
 
     for t in range(4):
         mm(t, "wt", 512 + 128 * t, "wn", N1, P, False, True)
-    mm(4, "uab", 128, "wn", N1, 128)
+    mm(4, "uab", 128, "wn", N1, P)
     for t in range(4):
         relu("s", "h2", NL, t, t, NL, P)
     quant("win", C2, P + 2, "h2")
     for x in "qs":
         send(-1, R("wn" + x, N12, N12 + NX), R("win" + x, C2 + X0 + d, C2 + P + d), "an12" + x)
+    mask("me", 64, PS(4, NL + d, P), 0)
     tt(R("s1r"), R("a1r", 0, NL), PS(4, 0, NL), A.add)
     mask("ma", 256, PS(4, d, NL + d), 0)
     if d:
         mask("ma", 415, PS(4, 0, 1), 15)
-    for t in range(4):
+        mask("me", 127, PS(4, 0, 1), 15)
+    for t in (1, 0, 2, 3):
         relu("s", "he", NX, t, t, 0, NL)
     mm(1, "uab", 0, "win", C2 + V0, 128)
     mm(0, "wt", 384, "win", C1, 128, True, False)
     mm(2, "uab", 128, "win", C2 + V0 + 2, 128)
+    mask("me", 0, PS(1, CAPP, 128), 0)
+    squeeze("se", "me", 0, 128)
+    cp(R("msg1", 10, 14), W("se", 0, 4))
+    send(1, R("land1"), R("msg1"), "am1")
     mm(4, "uab", 128, "wn", N2, P)
     for t, bank in enumerate(BANKS):
         mm(bank, "wt", 512 + 128 * t, "wn", N2, 128, False, True)
-    cp(R("s1x", 0, CAPP), PS(1, CAPP, 128), "s")
     for t, bank in enumerate(BANKS):
         relu("s", "he", HB, t, bank, 0, NL)
-    mask("me", 0, PS(1, CAPP, 128), 0)
-    tt(R("s2r", NL, P), R("s1x", 0, CAPP), PS(4, NL, P), A.add)
+    cp(R("s1x", 0, CAPP), PS(1, CAPP, 128), "s")
     tt(R("s2r", 0, NL), R("a1r", 0, NL), PS(4, 0, NL), A.add)
-    mask("me", 64, R("s2r", NL, P), 0)
     tt(R("m2r", 0, NL), R("s2r", 0, NL), R("s1r"), A.is_gt)
-    squeeze("se", "me", 0, 128)
-    quant("win", CE, 2 * NL, "he", NX)
-    mm(3, "uab", 0, "win", CE, 2 * NL)
-    cp(R("msg1", 10, 18), W("se", 0, 8), "s")
-    send(1, R("land1"), R("msg1", 0, 18), "am1")
     scan(R("cum"), R("ones", 0, NL), R("m2r", 0, NL))
     mask("mb", NL, R("m2r", 0, NL), 0)
+    quant("win", CE, 2 * NL, "he", NX)
+    mm(3, "uab", 0, "win", CE, 2 * NL)
     mask("mb", 0, R("cum"), 0)
-    mask("mc", 0, PS(3, 0, 2 * NL), 0)
+    tt(R("s2r", NL, P), R("s1x", 0, CAPP), PS(4, NL, P), A.add)
     squeeze("sb", "mb", 0, 2 * NL)
-    squeeze("sc", "mc", 0, 2 * NL)
+    mask("mc", 0, PS(3, 0, 2 * NL), 0)
     cw, mw = W("sb", 0, 6), W("sb", NL, 6)
+    m5 = W("sb", NL + 80, 1)
     act(R("gg", 0, 6), mw, -BIG)
     act(R("gg", 6, 12), mw, BIG, -BIG)
     tt(R("u0"), R("ph"), cw, A.subtract)
     tt(R("u1"), R("k64"), mw, A.mult)
+    squeeze("sc", "mc", 0, 2 * NL)
     tt(R("xx", 6, 12), R("msg1", 0, 6), R("gg", 0, 6), A.add)
     tt(R("xx", 0, 6), R("msg1", 0, 6), R("gg", 6, 12), A.add)
     tt(R("yy"), W("sc", 0, 12), R("gg"), A.add)
-    tt(R("msg1", 18, 24), R("u0"), R("u1"), A.add)
-    tt(R("msg1", 24, 36), R("yy"), R("xx"), A.max)
-    send(1, R("land3"), R("msg1", 18, 36), "am3")
+    tt(R("msg3", 0, 6), R("u0"), R("u1"), A.add)
+    tt(R("th5"), R("u0", 5, 6), m5, A.add)
+    tt(R("msg3", 6, 18), R("yy"), R("xx"), A.max)
+    send(1, R("land3"), R("msg3"), "am3")
+    first_cells(3, N3, NX, X0, "an3")
     iota(R("h3x", 0, 4 * (128 - NX)), [[0, 4 * (128 - NX)]])
     for a, b, c in ((0, CB, 0), (CB, CA, 2), (CA, 688, 1)):
         iota(R("spw", a, b), [[0, b - a]], c)
-    iota(R("spr", 0, CAPP), [[0, CAPP]], 1)
-    iota(R("spr", CAPP, P), [[0, NL]])
 
     for t, bank in enumerate(BANKS):
         mm(bank, "wt", 128 * t, "win", C2 + V0, 128, True, False)
@@ -374,12 +380,12 @@ def rank_program(g, core, T, topo):
     mm(3, "uu", 0, "win", C2, P)
     mask("me", 128, PS(2, CAPP - 2 + d, 126 + d), 0)
     mask("ma", P, PS(4, d, NL + d), 0)
-    tt(R("th1"), R("u0"), mw, A.add)
     squeeze("se", "me", 128, 192)
     squeeze("sa", "ma", P, 336)
-    tt(R("th2"), R("th1"), R("k63"), A.add)
     quant("win", CB, P, "he", HB)
-    tt(R("b3w", 0, 6), W("sa", P, 6), R("gx"), A.add)
+    act(R("c0", 1, 15, 3), W("sb", NL, 5), -float(CA + NX + CB), float(CA + NX))
+    act(R("c1", 1, 15, 3), W("sb", NL, 5), float(CB))
+    cp(R("th6", 0, 5), R("msg3", 0, 5), "s")
 
     mm(1, "uab", 128, "wn", N12 + NX - 128, 128)
     for t, bank in enumerate(BANKS):
@@ -391,31 +397,33 @@ def rank_program(g, core, T, topo):
     tt(R("m2r", X0, P), R("s2r", X0, P), R("s1x"), A.is_gt)
     squeeze("sa", "ma", 336, 416)
     act(R("junk"), R("m2r", NL, P), None, None, ACT.Identity, R("nn"))
-    cp(R("b3w", 6, 12), R("b3w", 0, 6), "s")
     mask("mb", NL + X0, R("m2r", X0, P), X0)
-    quant("win", CA, HB, "he")
-    ts(R("t0", 0, 6), R("th1"), R("nn"), A.is_lt)
-    ts(R("t1", 0, 6), R("th2"), R("nn"), A.is_gt, float(CB), A.mult)
-    squeeze("sb", "mb", 176, 256)
-    tt(R("t0", 0, 6), R("t0", 0, 6), R("da"), A.mult)
     tt(R("f4"), R("land1", 6, 10), W("se", 128, 4), A.add)
-    tt(R("dw", 0, 6), R("t1", 0, 6), R("t0", 0, 6), A.subtract)
-    tt(R("uw", 0, 6), R("t0", 0, 6), R("pw", 0, 6), A.add)
-    tt(R("t3"), R("dw"), W("sb", NL, 10), A.mult)
-    tt(R("f5"), R("f4"), R("land1", 14, 18), A.is_lt)
-    tt(R("t4"), R("t3"), R("uw"), A.add)
+    squeeze("sb", "mb", 176, 256)
+    tt(R("f6"), R("land1", 10, 14), W("se", 64, 4), A.add)
+    ts(R("th6", 5, 6), m5, R("k63", 5, 6), A.mult, R("th5"), A.add)
+    act(R("c0", 16, 17), m5, R("k5"), R("da"))
+    act(R("c1", 16, 17), m5, float(CB))
+    cp(R("c1", 18, 30, 3), W("sb", 2 * NL, 4), "s")
+    tt(R("f5"), R("f4"), R("f6"), A.is_lt)
     act(R("junk", 0, 4), R("f5"), None, None, ACT.Identity, R("n4"))
     act(R("fx"), R("ones", 0, 32), R("n4"), None, ACT.Copy)
+    for a in (0, 6):
+        cp(R("b3w", a, a + 5), W("sa", P, 5), "s")
+        act(R("b3w", a + 5, a + 6), W("sa", P + 80, 1), 1.0, R("g5"))
+    ts(R("c1", 0, 18, 3), R("th6"), R("nn"), A.is_lt)
+    quant("win", CA, HB, "he")
+    scan(R("co"), R("c0"), R("c1"))
     tt(R("s2p", 0, 6), R("land1", 0, 6), W("sa", 256, 6), A.add)
-    cp(R("off3"), R("t4"))
-    tt(R("s2p", 6, 10), R("land1", 10, 14), W("sa", 256 + NL, 4), A.add)
+    cp(R("off3"), R("co", 2, 30, 3))
+    op("v", lambda: g.vector.transpose(ap(R("fy")), ap(R("fx"))), [R("fx")], [R("fy")])
     pick("wn", 512, "win", 0, CA + HB, "off3")
     mm(2, "uab", 128, "wn", 512, P)
-    op("v", lambda: g.vector.transpose(ap(R("fy")), ap(R("fx"))), [R("fx")], [R("fy")])
     act(R("junk", 0, 16), R("fy", 0, 16), -GATE, None, ACT.Identity, R("nr"))
     act(R("junk", 16, 32), R("fy", 0, 16), GATE, None, ACT.Identity, R("nq"))
     act(R("gt", 0, 6), R("land3", 0, 6), GATE, R("nr"), ACT.Relu)
     act(R("gt", 6, 12), R("land3", 0, 6), -GATE, R("nq"), ACT.Relu)
+    tt(R("s2p", 6, 10), R("land1", 10, 14), W("sa", 256 + NL, 4), A.add)
     tt(R("ab"), R("land3", 6, 18), R("b3w"), A.add)
     mask("mf", 0, PS(2, d, P), 0)
     if d:
@@ -424,22 +432,21 @@ def rank_program(g, core, T, topo):
     squeeze("sf", "mf", 0, P)
     tt(R("s3", 0, 6), R("zz", 0, 6), R("zz", 6, 12), A.max)
     tt(R("s1p"), R("land1", 0, 10), W("sf", 0, 10), A.add)
-    tt(R("t5", 0, 6), R("s3", 0, 6), R("s2p", 0, 6), A.is_gt)
     tt(R("thr"), R("s3"), R("s2p"), A.max)
-    tt(R("u3"), R("t5", 0, 6), R("d32"), A.mult)
-    act(R("d0", 21, 32, 2), R("t5", 0, 6), 0.5, 0.5)
-    tt(R("d1", 0, 20, 2), R("s1p"), R("thr"), A.is_ge)
-    tt(R("d1", 1, 12, 2), R("u3"), R("o2", 0, 6), A.add)
-    tt(R("d0", 1, 12, 2), R("d12"), R("u3"), A.subtract)
-    tt(R("d1", 20, 40, 2), R("s1p"), R("thr"), A.is_lt)
-    scan(R("so"), R("d0"), R("d1"))
+    tt(R("d1", 0, 18, 3), R("s3", 0, 6), R("s2p", 0, 6), A.is_gt)
+    tt(R("d1", 30, 48, 3), R("s3", 0, 6), R("s2p", 0, 6), A.is_gt)
+    tt(R("d0", 2, 30, 3), R("s1p"), R("thr"), A.is_lt)
+    tt(R("d0", 32, 60, 3), R("s1p"), R("thr"), A.is_lt)
     tt(R("msg2", 10, 15), R("s1p", 5, 10), R("thr", 5, 10), A.max)
-    cp(R("offp"), R("so", 1, 20, 2))
-    cp(R("msg2", 0, 10), R("so", 21, 40, 2), "s")
-    pick("pool", 0, "wn", 512, WN, "offp")
+    scan(R("so"), R("d0"), R("d1"))
+    cp(R("offp"), R("so", 2, 30, 3))
+    cp(R("msg2", 0, 10), R("so", 32, 60, 3), "s")
+    pick("pool", 0, "wn", 512, N3, "offp")
     send(-1, R("land2"), R("msg2"), "am2")
     send(-1, R("plandq"), R("poolq"), "apq")
     send(-1, R("plands"), R("pools"), "aps")
+    iota(R("spr", 0, CAPP), [[0, CAPP]], 1)
+    iota(R("spr", CAPP, P), [[0, NL]])
 
     mm(1, "uab", 0, "wn", 512 + V0, 128)
     mm(2, "uab", 128, "wn", N3 + NX - 128, 128)
@@ -452,14 +459,20 @@ def rank_program(g, core, T, topo):
         relu("s", "h3x", 128 - NX, t, bank, 128 - NX, 128)
     quant("wn", 256, P, "h2")
     tt(R("cr", 80 - NX, 80), R("s1x"), PS(2, 128 - NX, 128), A.add)
-    cp(R("offs", 0, 4), R("t4", 6, 10))
+    cp(R("offs", 0, 4), R("co", 20, 30, 3))
     mask("md", 0, R("cr"), 0)
-    cp(R("offs", 4, 10), R("t4", 0, 6))
+    cp(R("offs", 4, 10), R("co", 2, 18, 3))
     squeeze("sd", "md", 0, 80)
+    act(R("cle", 0, 48, 3), R("sg"), 1.0, None, ACT.Relu)
+    act(R("cgt", 0, 48, 3), R("sg"), -1.0, None, ACT.Relu)
+    for i in (1, 2):
+        act(R("cle", i, 48, 3), R("sh"), 256.0 ** i)
+        act(R("cgt", i, 48, 3), R("sh"), -256.0 ** i, 256.0 ** i)
     pick("w4", 0, "win", 0, CA + HB, "off3")
     quant("w4", 512 + V0, 128, "h3x")
     places("ysb", 0, 3)
     places("ysb", P, 4)
+    gather("v", R("spr", P, 2 * P), R("spw"), "offs")
 
     tt(R("u6", 5, 10), W("sd", 0, 5), R("land2", 10, 15), A.is_gt)
     tt(R("v0"), R("land2", 0, 10), R("pw5"), A.subtract)
@@ -473,29 +486,29 @@ def rank_program(g, core, T, topo):
     for t in range(4):
         mm(t, "wt", 512 + 128 * t, "pland", 0, P, False, True)
     dma("y", T.y[:, 0:2 * P], ap(R("ysb", 0, 2 * P)), [R("ysb", 0, 2 * P), R("plands")], [])
-    ts(R("v3"), R("v1"), 0.25, A.is_lt, 1.0 / 65536, A.max)
+    step = 1.0 / 256 - 1.0 / 65536
+    act(R("v3"), R("v1"), -2.0, 1.0, ACT.Relu)
     gather("v", R("wr"), R("cle"), "offk")
     gather("s", R("wg", 16, P + 16), R("cgt"), "offk")
-    ts(R("v4"), R("v1"), 0.75, A.is_lt, 1.0 / 256, A.mult)
-    scan(R("sf"), R("wg", 0, P), R("wr"), A.add)
-    tt(R("v2"), R("v3"), R("v4"), A.max)
+    act(R("v4"), R("v1"), -2.0 * step, 2.0 * step + 1.0 / 65536)
     act(R("e0", 1, 8, 2), R("u6", 6, 10), 256.0, 256.0)
     act(R("e0", 9, 20, 2), R("u6", 0, 6), 256.0, 256.0)
     act(R("v5"), R("v1"), 2.0, 1.0)
-    tt(R("v3"), W("sf", 0, 10), R("v2"), A.mult)
-    ts(R("ci"), R("v3"), -0.2, A.add)
+    scan(R("sf"), R("wg", 0, P), R("wr"), A.add)
+    tt(R("v2"), R("v3"), R("v4"), A.max)
+    tt(R("ci"), W("sf", 0, 10), R("v2"), A.mult)
     ts(R("cj"), R("ci"), 255, A.bitwise_and)
     ts(R("e1", 0, 20, 2), R("cj"), CAPP + 0.5, A.is_lt)
     scan(R("eo"), R("e0"), R("e1"))
-    tt(R("v6"), R("v5"), R("e1", 0, 20, 2), A.mult)
+    relu("v", "h4", 0, 3, 3, 0, P)
     cp(R("off4"), R("eo", 1, 20, 2))
-    cp(R("offt"), R("v6"))
-    for t in range(4):
-        relu("sssv"[t], "h4", 0, t, t, 0, P)
+    for t in range(3):
+        relu("s", "h4", 0, t, t, 0, P)
     quant("w4", 256, P, "h4")
-    gather("s", R("spr", 2 * P, 3 * P), R("cst"), "offt")
+    tt(R("v6"), R("v5"), R("e1", 0, 20, 2), A.mult)
     pick("c4", 0, "w4", 0, 672, "off4")
-    gather("v", R("spr", P, 2 * P), R("spw"), "offs")
+    cp(R("offt"), R("v6"))
+    gather("v", R("spr", 2 * P, 3 * P), R("cst"), "offt")
     mm(4, "uu", 0, "c4", 0, P)
     dma("y", T.oc[:, :], view(R("c4q")), [R("c4q")], [])
     cp(R("ysb", 2 * P, 3 * P), PS(4, 0, P), "s")

@@ -5,11 +5,12 @@ NL = P - CAPP
 X0 = NL - 2
 NX = P - X0
 V0 = P - 128
-BIG, GATE = 1.0e29, 2.0 ** 80
+XW = 2 * NX + 2
+BIG = 1.0e29
 CODE, PLANE, F, BF, I32, U16 = "float8_e4m3fn_x4", "uint8", "float32", "bfloat16", "int32", "uint16"
-C2, CB, CA, C1, CE = 0, 256, 512, 768, 1024
-N1, N12, N2, N3, WN = 704, 864, 930, 1090, 1156
-HB = NX + NL
+CN, C1, C2, CL, CX, N4, S3, WIN = 64, 128, 352, 560, 752, 896, 1056, 1184
+C3, NE, N1, N2, N12, N3, WN = 512, 704, 768, 864, 1026, 1092, 1158
+D1L, D2L, D2X, D1X = CL - C1, CL + NL - C1, CX - X0 - C1, CX + NX + 2 - X0 - C1
 
 
 def _pair(name, n):
@@ -21,20 +22,20 @@ def _f(dtype, **kw):
 
 
 SCRATCH = {}
-for _n, _w in (("wt", 1024), ("uu", 128), ("uab", 256), ("win", CE + 2 * NL), ("wn", WN), ("pool", P), ("pland", P),
-               ("left", P), ("w4", 672), ("c4", P)):
+for _n, _w in (("wt", 1024), ("uu", 128), ("uab", 256), ("win", WIN), ("wn", WN), ("pool", P), ("pland", P),
+               ("left", P), ("c4", P)):
     SCRATCH.update(_pair(_n, _w))
-SCRATCH.update(_f(BF, hx=648, h2=648, hu=512, huab=1024, he=4 * (HB + P), h3x=512, h4=640, ones=128, keep=192,
-                  m2r=P, cum=NL, mb=256, sb=256))
-SCRATCH.update(_f(F, tmod=192, msk=192, spw=688, a1r=P, s1r=NL, s2r=P, ma=416, sa=416, mc=192, sc=192, md=80, sd=80,
-                  me=192, se=192, mf=P, sf=P, fx=32, fy=32, junk=64, s1x=NX, wr=P, ysb=3 * P, spr=3 * P, cst=8, cle=48,
-                  cgt=48, msg1=14, msg3=18, land1=14, land3=18, msg2=15, land2=15))
+SCRATCH.update(_f(BF, hx=896, h2=4 * XW, hu=512, hv=8, huab=1024, he=8 * NL, hc=4 * XW, h3x=512, h4=640, ones=128,
+                  keep=192, tmod=192, mr=256, mb=256, sb=256, spw=768))
+SCRATCH.update(_f(F, msk=192, mskx=NX, a1d=NL, sl=192, ax=XW, sx=XW, ma=416, sa=416, mc=192, sc=192, md=80, sd=80,
+                  me=64, se=64, mf=P, sf=P, junk=64, s1x=NX, wr=P, ysb=3 * P, spr=3 * P, cst=8, cle=48,
+                  cgt=48, msg1=14, msg3=6, land1=14, land3=6, msg2=20, land2=20))
 SMALL, _at = {}, [0]
-for _n, _w in dict(d0=60, d1=60, c0=30, c1=30, e0=20, u6=10, wg=P + 16, s3=10, cr=80, qf=1, q3=1, pw=10, pw5=10, ph=6,
-                   k63=6, k64=6, jw=10, da=1, t0=10, t1=10, t2=10, xm=6, gg=12, xx=12, yy=12, b3w=12, gt=12,
-                   zz=12, ab=12, j16=16, sg=16, nn=1, nr=1, nq=1, n4=1, f4=4, f5=4, f6=4, u0=6, u1=6, s2p=10, thr=10,
-                   s1p=10, so=60, co=30, sh=16, th5=1, th6=6, k5=1, g5=1,
-                   v0=10, v1=10, v2=10, v3=10, v4=10, v5=10, v6=10, e1=20, eo=20).items():
+for _n, _w in dict(d0=30, c0=24, c1=24, e0=30, e1=30, wg=P + 16, s3=10, cr=80, qf=1, q3=1, pw=10, pw5=10, ph=1,
+                   k63=1, k64=6, jw=10, t0=10, t1=10, t2=10, xm=1, gg=18, xx=12, yy=12, gt=12, a1w=12, a2f=10,
+                   zz=12, j16=16, sg=16, nn=1, u1=6, s2p=10, pe=4, s1p=10, da1=30, db1=30, so=30, sp=30, co=36, sh=16,
+                   th0=8, df=1, pb=1, az=12, g5=1, v0=5, u6=5, v1=10, v2=10, v3=10, v4=10, v5=10, v6=10,
+                   eo=30).items():
     SMALL[_n] = (_at[0], _w)
     _at[0] += _w
 SCRATCH.update(_f(F, small=_at[0]))
@@ -165,8 +166,8 @@ def rank_program(g, core, T, topo):
     def fill(o, c):
         op("v", lambda: g.vector.memset(ap(o), c), [], [o])
 
-    def scan(o, a, b, op0=A.mult):
-        op("v", lambda: g.vector.tensor_tensor_scan(ap(o), ap(a), ap(b), 0.0, op0, A.add), [a, b], [o])
+    def scan(o, a, b, op0=A.mult, op1=A.add):
+        op("v", lambda: g.vector.tensor_tensor_scan(ap(o), ap(a), ap(b), 0.0, op0, op1), [a, b], [o])
 
     def iota(o, pattern, base=0, cm=0):
         if SCRATCH[o[0]][2] == I32:
@@ -185,6 +186,14 @@ def rank_program(g, core, T, topo):
         rd = [R(st + "q", sa, sa + 128), R(st + "s", sa, sa + 128), R(mv + "q", ma, ma + w), R(mv + "s", ma, ma + w)]
         o = PS(bank, 0, w)
         op("t", lambda: g.tensor.matmul_mx(ap(o), ap(rd[0]), ap(rd[1]), ap(rd[2]), ap(rd[3]), start, stop), rd, [o])
+
+    def lefts(banks, mv, ma, w, which=range(4)):
+        for t in which:
+            mm(banks[t], "wt", 128 * t, mv, ma, w, True, False)
+
+    def rights(banks, mv, ma, w):
+        for t in range(4):
+            mm(banks[t], "wt", 512 + 128 * t, mv, ma, w, False, True)
 
     def relu(q, h, ha, t, bank, a, b):
         o, i = R(h, 4 * ha + t, 4 * (ha + b - a), 4), PS(bank, a, b)
@@ -217,40 +226,39 @@ def rank_program(g, core, T, topo):
     def W(buf, a, c):
         return R(buf, a + 15, a + 16 * c, 16 if c > 1 else 1)
 
-    def places(buf, a, bank):
-        cp(R(buf, a, a + CAPP), PS(bank, NL, P), "s")
-        cp(R(buf, a + CAPP, a + P), PS(bank, 0, NL), "s")
-
     shift = {k: (((rank - k) % n) + k) // n for k in (1, 2, 3)}
     d = shift[1]
-    BANKS = (5, 6, 7, 0)
+    last = (rank + 1) // n
     jw = "jw" if d else "pw"
+    x1 = 2 * last
+    x0 = 2 - x1
+    PE = P - x1
+    LO, HI, XB = (0, 1, 2, 3), (4, 5, 6, 7), (1, 2, 3, 0)
 
-    def first_cells(k, a, w, at, s):
+    def cells(k, buf, a, w, at, s, early=0, cut=0):
         for x in "qs":
-            b = C1 + at + shift[k]
-            send(-k, R("wn" + x, a, a + w), R("win" + x, b, b + w), s + x)
+            b = at + shift[k] - early
+            send(-k, R(buf + x, a - early, a + w - cut), R("win" + x, b, at + shift[k] + w - cut), s + x)
 
-    for k, a, w, s in ((1, N1, P, "an1"), (2, N2, P, "an2"), (3, N3, NX, "an3"), (1, N12, NX, "an12")):
-        lands(k, R("wnq", a, a + w), s + "q")
-        lands(k, R("wns", a, a + w), s + "s")
+    for k, buf, a, w, s in ((1, "wn", NE - last, P, "an1"), (2, "wn", N2 - last, P + last, "an2"),
+                            (3, "wn", N3, NX, "an3"), (1, "wn", N12 - 2, NX + 2, "an12")):
+        lands(k, R(buf + "q", a, a + w), s + "q")
+        lands(k, R(buf + "s", a, a + w), s + "s")
     lands(-1, R("land1"), "am1")
     lands(-1, R("land3"), "am3")
     lands(1, R("land2"), "am2")
     lands(1, R("plandq"), "apq")
     lands(1, R("plands"), "aps")
 
-    dma("y", ap(R("hx", 0, 4 * NL)), T.x[:, 4 * CAPP:4 * P], [], [R("hx", 0, 4 * NL)])
-    dma("s", ap(R("hx", 4 * NL, 648)), T.x[:, 0:648 - 4 * NL], [], [R("hx", 4 * NL, 648)])
-    dma("y", ap(R("hu")), T.u[:, :], [], [R("hu")])
-    dma("y", view(R("wtq", 0, 512)), T.wc[:, 0:2048], [], [R("wtq", 0, 512)])
+    dma("y", ap(R("hx", 0, 4 * P)), T.x[:, :], [], [R("hx", 0, 4 * P)])
+    dma("y", ap(R("hv")), T.u[:, 0:8], [], [R("hv")])
     dma("y", ap(R("wts")), T.ws[:, :], [], [R("wts")])
-    dma("y", view(R("wtq", 512, 1024)), T.wc[:, 2048:4096], [], [R("wtq", 512, 1024)])
+    dma("y", view(R("wtq")), T.wc[:, :], [], [R("wtq")])
 
     iota(R("qi"), [[0, 1]], 0, 1)
     iota(R("t0"), [[16, 10]])
-    iota(R("j16"), [[1, 16]])
     iota(R("tmod"), [[0, 12], [1, 16]])
+    iota(R("j16"), [[1, 16]])
     iota(R("cst"), [[1, 8]])
     fill(R("small", 0, SMALL["wg"][0] + 16), 0.0)
     ts(R("qj"), R("qi"), 15, A.bitwise_and)
@@ -258,260 +266,269 @@ def rank_program(g, core, T, topo):
     cp(R("qf"), R("qj"))
     fill(R("ones"), 1.0)
     ts(R("pw"), R("t0"), R("qf"), A.add)
-    fill(R("c0", 2, 30, 3), 1.0)
-    fill(R("c0", 19, 30, 3), float(CB - CA + X0))
-    fill(R("c1", 19, 30, 3), float(CA - X0))
-    ts(R("xm"), R("pw", 0, 6), X0 - 0.5, A.is_gt)
+    fill(R("h3x", 0, 4 * (128 - NX)), 0.0)
+    if last:
+        fill(R("he", 4 * X0, 4 * NL), 0.0)
+
+    quant("win", CN, P, "hx")
+    cells(1, "wn", NE, P, CN, "an1", d, d)
+    quant("win", CN + P, 128, "hx")
+    cells(2, "wn", N2, P, C1, "an2", int((rank - 2) % n == n - 1))
+    cp(R("hx", 4 * P, 4 * (P + CAPP)), R("hx", 0, 4 * CAPP), "s")
+    for t in range(4):
+        ts(R("huab", t, 512, 4), R("ones"), R("hv", t, t + 1), A.mult)
+        act(R("huab", 512 + t, 1024, 4), R("ones"), 0.0, R("hv", 4 + t, 5 + t))
+    ts(R("msk"), R("tmod"), R("qf"), A.is_equal)
+    quant("uab", 0, 256, "huab")
+    ts(R("keep"), R("tmod"), 0.0, A.not_equal)
+    cp(R("h2", 0, 8), R("hx", 4 * P - 8, 4 * P), "s")
+    cp(R("h2", 4 * NX, 4 * NX + 8), R("hx", 4 * CAPP, 4 * CAPP + 8), "s")
+    cp(R("h2", 4 * NX + 8, 4 * XW), R("hx", 4 * P - 8, 4 * (P + CAPP)), "s")
+    mm(7, "uab", 0, "win", C1, P)
+    lefts(LO, "win", CN, PE)
+    quant("wn", 0, P, "hx", CAPP)
+    mask("ma", 0, PS(7, 0, P), 0)
+    cp(R("a1d"), PS(7, 0, NL), "s")
+    lefts(HI, "win", C1, 128, (0, 1))
+    act(R("ph"), R("qf"), 1.0, 0.5)
+    act(R("sh"), R("j16"), -1.0, R("qf"), ACT.Sign)
+    act(R("sg"), R("j16"), -1.0, R("ph"), ACT.Sign)
+    act(R("pw5"), R("pw"), 1.0 / 512)
+    act(R("q3"), R("qf"), 3.0)
+    quant("wn", 256, 128, "hx", CAPP)
+    squeeze("sa", "ma", 0, P)
+    fill(R("c0", 2, 24, 3), 1.0)
+    fill(R("e0", 1, 30, 3), float(S3 - V0 - N4))
+    ts(R("mskx"), R("msk", X0 % 16, X0 % 16 + NX), float(D2X - D1X), A.mult)
     if d:
         ts(R("t1"), R("pw"), P - 1.5, A.is_gt, -float(P), A.mult)
         act(R("jw"), R("pw"), 1.0, 1.0)
         tt(R("jw"), R("jw"), R("t1"), A.add)
-    fill(R("d0", 31, 60, 3), 0.5)
-    fill(R("d1", 31, 60, 3), 0.5)
-    ts(R("t2"), R(jw), X0 - 0.5, A.is_gt, float(N12 - X0 - N1), A.mult)
-    act(R("ph"), R("pw", 0, 6), 1.0, 0.5)
-    act(R("sg"), R("j16"), -1.0, R("ph", 0, 1), ACT.Sign)
-    act(R("pw5"), R("pw"), 1.0 / 512)
-    act(R("sh"), R("j16"), -1.0, R("qf"), ACT.Sign)
-    act(R("d1", 32, 60, 3), R("pw"), 1.0 / 512)
-    cp(R("c1", 2, 30, 3), R("pw"), "s")
-    cp(R("e1", 1, 8, 2), R("pw", 6, 10), "s")
-    cp(R("e1", 9, 20, 2), R("pw", 0, 6), "s")
-    act(R("q3"), R("qf"), 3.0)
-    act(R("k63"), R("pw", 0, 6), -1.0, CAPP - 1.0)
-    act(R("k64"), R("pw", 0, 6), -1.0, float(CAPP))
-    act(R("g5"), R("xm", 5, 6), -BIG)
-    act(R("da"), R("xm", 5, 6), -float(P), float(CA + NX))
-    act(R("k5"), R("xm", 5, 6), float(P), -float(CA + NX + CB))
-    act(R("d0", 1, 18, 3), R("t2", 0, 6), -1.0, float(N2 - N1))
-    act(R("d1", 1, 30, 3), R("t2"), 1.0, float(N1 - 512))
-    cp(R("d1", 2, 30, 3), R(jw), "s")
-
-    quant("win", C1, P + 2, "hx")
-    first_cells(1, N1, P, 0, "an1")
-    first_cells(2, N2, P, 0, "an2")
-    ts(R("keep"), R("tmod"), 0.0, A.not_equal)
-    ts(R("msk"), R("tmod"), R("qf"), A.is_equal)
-    for t in range(4):
-        mm(t, "wt", 128 * t, "win", C1, P, True, False)
-    for t in range(4):
-        ts(R("huab", t, 512, 4), R("ones"), R("hu", t, t + 1), A.mult)
-        act(R("huab", 512 + t, 1024, 4), R("ones"), 0.0, R("hu", 4 + t, 5 + t))
-    cp(R("h2", 0, 4 * NL), R("hx", 0, 4 * NL), "s")
-    cp(R("h2", 4 * P, 648), R("hx", 4 * P, 648), "s")
-    quant("uab", 0, 256, "huab")
-    mm(4, "uab", 0, "win", C1, P)
-    for t in range(3):
-        mm(5 + t, "wt", 128 * t, "win", C1, 128, True, False)
-    quant("uu", 0, 128, "hu")
-    mask("ma", 0, PS(4, 0, P), 0)
-    cp(R("a1r"), PS(4, 0, P), "s")
+    if d or last:
+        ts(R("xm"), R("pw", 5, 6), X0 - 0.5, A.is_gt)
     ts(R("sh"), R("sh"), 0.75, A.mult, 0.75, A.add)
-    squeeze("sa", "ma", 0, P)
+    fill(R("db1"), 0.5)
+    ts(R("t2"), R(jw), X0 - 0.5, A.is_gt, float(N12 - X0 - N1), A.mult)
     ts(R("sh"), R("sh"), 1.0, A.min)
+    for a, b, c in ((0, D1L, 0.0), (D1L, D2L, 1.0), (D2L, CX + NX - C1, 2.0), (CX + NX - C1, 768, 1.0)):
+        fill(R("spw", a, b), c)
     cp(R("msg1", 0, 10), W("sa", 0, 10), "s")
-    quant("wn", 0, P, "hx")
-
-    for t in range(4):
-        mm(t, "wt", 512 + 128 * t, "wn", N1, P, False, True)
-    mm(4, "uab", 128, "wn", N1, P)
-    for t in range(4):
-        relu("s", "h2", NL, t, t, NL, P)
-    quant("win", C2, P + 2, "h2")
-    for x in "qs":
-        send(-1, R("wn" + x, N12, N12 + NX), R("win" + x, C2 + X0 + d, C2 + P + d), "an12" + x)
-    mask("me", 64, PS(4, NL + d, P), 0)
-    tt(R("s1r"), R("a1r", 0, NL), PS(4, 0, NL), A.add)
-    mask("ma", 256, PS(4, d, NL + d), 0)
+    for a in (0, 6):
+        cp(R("a1w", a, a + 6), W("sa", 0, 6), "s")
+    act(R("k64"), R("pw", 0, 6), -1.0, float(CAPP))
+    cp(R("c1", 8, 24, 3), R("pw", 0, 6), "s")
+    act(R("pe"), R("pw", 6, 10), 1.0, float(D1X))
     if d:
-        mask("ma", 415, PS(4, 0, 1), 15)
-        mask("me", 127, PS(4, 0, 1), 15)
-    for t in (1, 0, 2, 3):
-        relu("s", "he", NX, t, t, 0, NL)
-    mm(1, "uab", 0, "win", C2 + V0, 128)
-    mm(0, "wt", 384, "win", C1, 128, True, False)
-    mm(2, "uab", 128, "win", C2 + V0 + 2, 128)
-    mask("me", 0, PS(1, CAPP, 128), 0)
-    squeeze("se", "me", 0, 128)
-    cp(R("msg1", 10, 14), W("se", 0, 4))
-    send(1, R("land1"), R("msg1"), "am1")
-    mm(4, "uab", 128, "wn", N2, P)
-    for t, bank in enumerate(BANKS):
-        mm(bank, "wt", 512 + 128 * t, "wn", N2, 128, False, True)
-    for t, bank in enumerate(BANKS):
-        relu("s", "he", HB, t, bank, 0, NL)
-    cp(R("s1x", 0, CAPP), PS(1, CAPP, 128), "s")
-    tt(R("s2r", 0, NL), R("a1r", 0, NL), PS(4, 0, NL), A.add)
-    tt(R("m2r", 0, NL), R("s2r", 0, NL), R("s1r"), A.is_gt)
-    scan(R("cum"), R("ones", 0, NL), R("m2r", 0, NL))
-    mask("mb", NL, R("m2r", 0, NL), 0)
-    quant("win", CE, 2 * NL, "he", NX)
-    mm(3, "uab", 0, "win", CE, 2 * NL)
-    mask("mb", 0, R("cum"), 0)
-    tt(R("s2r", NL, P), R("s1x", 0, CAPP), PS(4, NL, P), A.add)
+        act(R("g5"), R("xm"), -BIG)
+    if last:
+        cp(R("mskx", 0, 2), R("msk", X0 % 16, X0 % 16 + 2), "s")
+        act(R("k63"), R("pw", 5, 6), -1.0, CAPP - 1.0)
+        act(R("c0", 1, 2), R("xm"), float(D1X - D1L), float(D1L))
+        act(R("c0", 4, 5), R("xm"), 0.0, -float(D2L))
+        act(R("c1", 4, 5), R("xm"), 0.0, float(D2L))
+        act(R("pb"), R("pw", 5, 6), 1.0, float(N4 - C1))
+        for a in (2, 5):
+            cp(R("c1", a, a + 1), R("pw", 5, 6), "s")
+    act(R("cle", 0, 48, 3), R("sg"), 1.0, None, ACT.Relu)
+    act(R("cgt", 0, 48, 3), R("sg"), -1.0, None, ACT.Relu)
+    for i in (1, 2):
+        act(R("cle", i, 48, 3), R("sh"), 256.0 ** i)
+        act(R("cgt", i, 48, 3), R("sh"), -256.0 ** i, 256.0 ** i)
+    act(R("da1", 0, 30, 3), R("t2"), 1.0, float(N1 - C3))
+    act(R("da1", 1, 30, 3), R("t2"), 0.0, -float(N2 - C3))
+    act(R("da1", 2, 30, 3), R(jw), 1.0, float(N2 - C3))
+    act(R("db1", 1, 30, 3), R("pw"), 0.0, -1.0)
+    act(R("db1", 2, 30, 3), R("pw"), 1.0 / 512, 1.0)
+
+    mm(7, "uab", 128, "wn", NE, PE)
+    rights(LO, "wn", NE, PE)
+    tt(R("sl", 0, NL - x1), PS(7, CAPP, PE), R("a1d", 0, NL - x1), A.add)
+    mask("ma", 256, PS(7, CAPP + d, PE), 0)
+    if d:
+        mask("ma", 415, PS(7, CAPP, CAPP + 1), 15)
+    squeeze("sa", "ma", 256, 336)
+    lefts(HI, "win", C1, 128, (2, 3))
+    for t in range(4):
+        relu("s", "h2", 2, t, t, 0, CAPP)
+    for t in range(4):
+        relu("s", "he", 0, t, t, CAPP, PE)
+    quant("win", C2, XW, "h2")
+    cells(1, "wn", N12 - 2, NX + 2, C2 - 2, "an12")
+    cells(3, "wn", N3, NX, C1 + X0, "an3")
+
+    mm(0, "uab", 128, "wn", N2 - x1, 128)
+    rights(HI, "wn", N2, 128)
+    mm(1, "uab", 0, "win", C2, XW)
+    tt(R("sl", NL, 2 * NL), PS(0, x1, NL + x1), R("a1d"), A.add)
+    if last:
+        tt(R("sl", X0, NL), PS(0, 0, 2), R("a1d", X0, NL), A.add)
+    tt(R("mr", NL, 2 * NL), R("sl", NL, 2 * NL), R("sl", 0, NL), A.is_gt)
+    for t in range(4):
+        relu("s", "he", NL, t, HI[t], 0, NL)
+    scan(R("mr", 0, NL), R("ones", 0, NL), R("mr", NL, 2 * NL), A.add, A.subtract)
+    mask("mb", NL, R("mr", NL, 2 * NL), 0)
+    mask("mb", 0, R("mr", 0, NL), 0)
+    quant("win", CL, 2 * NL, "he")
+    mask("ma", P, PS(0, d + x1, NL + d + x1), 0)
+    mask("me", 0, PS(1, 2, NX), 0)
+    cp(R("ax"), PS(1, 0, XW), "s")
+    lefts(XB, "win", C2, XW, (1, 2))
+    mm(5, "uab", 0, "win", CL, 2 * NL)
+    lefts(XB, "win", C2, XW, (3, 0))
     squeeze("sb", "mb", 0, 2 * NL)
-    mask("mc", 0, PS(3, 0, 2 * NL), 0)
+    squeeze("se", "me", 0, 64)
+    mm(4, "uab", 128, "wn", N2 + X0, XW)
+    rights(XB, "wn", N2 + X0, XW)
     cw, mw = W("sb", 0, 6), W("sb", NL, 6)
     m5 = W("sb", NL + 80, 1)
-    act(R("gg", 0, 6), mw, -BIG)
     act(R("gg", 6, 12), mw, BIG, -BIG)
-    tt(R("u0"), R("ph"), cw, A.subtract)
+    act(R("gg", 12, 18), mw, -BIG)
+    act(R("gg", 0, 6), mw, -BIG)
+    cp(R("msg1", 10, 14), W("se", 0, 4), "s")
+    send(1, R("land1"), R("msg1"), "am1")
+    dma("y", ap(R("hu")), T.u[:, :], [R("wns", N12, N3)], [R("hu")])
+    act(R("c0", 7, 24, 3), mw, -float(D1L + D2L), float(D1L))
+    act(R("c1", 7, 24, 3), mw, float(D2L))
+    if last:
+        act(R("th0", 0, 1), W("sb", 80, 1), 1.0, m5)
+        act(R("th0", 1, 2), R("th0", 0, 1), 1.0, R("k63"))
+    mask("mc", 0, PS(5, 0, 2 * NL), 0)
     tt(R("u1"), R("k64"), mw, A.mult)
     squeeze("sc", "mc", 0, 2 * NL)
-    tt(R("xx", 6, 12), R("msg1", 0, 6), R("gg", 0, 6), A.add)
-    tt(R("xx", 0, 6), R("msg1", 0, 6), R("gg", 6, 12), A.add)
-    tt(R("yy"), W("sc", 0, 12), R("gg"), A.add)
-    tt(R("msg3", 0, 6), R("u0"), R("u1"), A.add)
-    tt(R("th5"), R("u0", 5, 6), m5, A.add)
-    tt(R("msg3", 6, 18), R("yy"), R("xx"), A.max)
+    tt(R("th0", 2, 8), cw, R("u1"), A.add)
+    tt(R("xx"), R("a1w"), R("gg", 6, 18), A.add)
+
+    for t in (0, 1):
+        relu("s", "hc", 0, t, XB[t], 0, XW)
+    tt(R("sx"), PS(4, 0, XW), R("ax"), A.add)
+    tt(R("yy"), W("sc", 0, 12), R("gg", 0, 12), A.add)
+    tt(R("mr", NL + X0 + x0, 256), R("sx", x0, NX), R("sx", NX + 2 + x0, XW), A.is_gt)
+    tt(R("az"), R("yy"), R("xx"), A.max)
+    act(R("junk"), R("mr", 2 * NL, 256), None, None, ACT.Identity, R("nn"))
+    relu("s", "hc", 0, 2, XB[2], 0, XW)
+    tt(R("mb", NL + X0 + x0, 256), R("mr", NL + X0 + x0, 256), R("mskx", x0, NX), A.mult)
+    ts(R("c1", 6 - 3 * x1, 24, 3), R("th0", 2 - x1, 8), R("nn"), A.is_le)
+    squeeze("sb", "mb", 176 if last else 192, 256)
+    act(R("gt", 0, 6), R("c1", 6, 24, 3), BIG, -BIG)
+    act(R("gt", 6, 12), R("c1", 6, 24, 3), -BIG)
+    relu("s", "hc", 0, 3, XB[3], 0, XW)
+    scan(R("co", 6 - 3 * x1, 24), R("c0", 6 - 3 * x1, 24), R("c1", 6 - 3 * x1, 24))
+    tt(R("co", 26, 36, 3), W("sb", 2 * NL, 4), R("pe"), A.add)
+    if last:
+        tt(R("df"), R("co", 5, 6), R("co", 2, 3), A.subtract)
+    tt(R("zz"), R("az"), R("gt"), A.add)
+    if last:
+        ts(R("co", 23, 24), m5, R("df"), A.mult, R("co", 2, 3), A.add)
+        tt(R("msg3"), R("zz", 0, 6), R("zz", 6, 12), A.max)
+        cp(R("off3"), R("co", 8, 36, 3))
+    else:
+        cp(R("off3"), R("co", 8, 36, 3))
+        tt(R("msg3"), R("zz", 0, 6), R("zz", 6, 12), A.max)
     send(1, R("land3"), R("msg3"), "am3")
-    first_cells(3, N3, NX, X0, "an3")
-    iota(R("h3x", 0, 4 * (128 - NX)), [[0, 4 * (128 - NX)]])
-    for a, b, c in ((0, CB, 0), (CB, CA, 2), (CA, 688, 1)):
-        iota(R("spw", a, b), [[0, b - a]], c)
-
-    for t, bank in enumerate(BANKS):
-        mm(bank, "wt", 128 * t, "win", C2 + V0, 128, True, False)
-        mm(bank, "wt", 512 + 128 * t, "wn", N2 + V0, 128, False, True)
-    for t, bank in enumerate(BANKS):
-        relu("s", "he", HB + X0, t, bank, 128 - NX, 128)
-    for t, bank in enumerate(BANKS):
-        mm(bank, "wt", 128 * t, "win", C1 + V0, 128, True, False)
-    mm(3, "uu", 0, "win", C2, P)
-    mask("me", 128, PS(2, CAPP - 2 + d, 126 + d), 0)
-    mask("ma", P, PS(4, d, NL + d), 0)
-    squeeze("se", "me", 128, 192)
-    squeeze("sa", "ma", P, 336)
-    quant("win", CB, P, "he", HB)
-    act(R("c0", 1, 15, 3), W("sb", NL, 5), -float(CA + NX + CB), float(CA + NX))
-    act(R("c1", 1, 15, 3), W("sb", NL, 5), float(CB))
-    cp(R("th6", 0, 5), R("msg3", 0, 5), "s")
-
-    mm(1, "uab", 128, "wn", N12 + NX - 128, 128)
-    for t, bank in enumerate(BANKS):
-        mm(bank, "wt", 512 + 128 * t, "wn", N12 + NX - 128, 128, False, True)
-    for t, bank in enumerate(BANKS):
-        relu("s", "he", 0, t, bank, 128 - NX, 128)
-    tt(R("s1x"), R("a1r", X0, P), PS(1, 128 - NX, 128), A.add)
-    mask("ma", 256 + X0 - d, PS(1, 128 - NX, 128), X0 - d)
-    tt(R("m2r", X0, P), R("s2r", X0, P), R("s1x"), A.is_gt)
+    quant("win", CX, XW, "hc")
+    pick("wn", C3, "win", C1, CX + XW, "off3")
+    squeeze("sa", "ma", P, 256)
+    mask("ma", 256 + X0 - d, PS(4, NX + 2, XW), X0 - d)
+    mm(2, "uab", 128, "wn", C3, P)
+    mm(1, "uab", 0, "wn", C3 + V0, 128)
+    cp(R("a2f", 0, 6), R("land1", 0, 6), "s")
+    cp(R("a2f", 6, 10), R("land1", 10, 14), "s")
     squeeze("sa", "ma", 336, 416)
-    act(R("junk"), R("m2r", NL, P), None, None, ACT.Identity, R("nn"))
-    mask("mb", NL + X0, R("m2r", X0, P), X0)
-    tt(R("f4"), R("land1", 6, 10), W("se", 128, 4), A.add)
-    squeeze("sb", "mb", 176, 256)
-    tt(R("f6"), R("land1", 10, 14), W("se", 64, 4), A.add)
-    ts(R("th6", 5, 6), m5, R("k63", 5, 6), A.mult, R("th5"), A.add)
-    act(R("c0", 16, 17), m5, R("k5"), R("da"))
-    act(R("c1", 16, 17), m5, float(CB))
-    cp(R("c1", 18, 30, 3), W("sb", 2 * NL, 4), "s")
-    tt(R("f5"), R("f4"), R("f6"), A.is_lt)
-    act(R("junk", 0, 4), R("f5"), None, None, ACT.Identity, R("n4"))
-    act(R("fx"), R("ones", 0, 32), R("n4"), None, ACT.Copy)
-    for a in (0, 6):
-        cp(R("b3w", a, a + 5), W("sa", P, 5), "s")
-        act(R("b3w", a + 5, a + 6), W("sa", P + 80, 1), 1.0, R("g5"))
-    ts(R("c1", 0, 18, 3), R("th6"), R("nn"), A.is_lt)
-    quant("win", CA, HB, "he")
-    scan(R("co"), R("c0"), R("c1"))
-    tt(R("s2p", 0, 6), R("land1", 0, 6), W("sa", 256, 6), A.add)
-    cp(R("off3"), R("co", 2, 30, 3))
-    op("v", lambda: g.vector.transpose(ap(R("fy")), ap(R("fx"))), [R("fx")], [R("fy")])
-    pick("wn", 512, "win", 0, CA + HB, "off3")
-    mm(2, "uab", 128, "wn", 512, P)
-    act(R("junk", 0, 16), R("fy", 0, 16), -GATE, None, ACT.Identity, R("nr"))
-    act(R("junk", 16, 32), R("fy", 0, 16), GATE, None, ACT.Identity, R("nq"))
-    act(R("gt", 0, 6), R("land3", 0, 6), GATE, R("nr"), ACT.Relu)
-    act(R("gt", 6, 12), R("land3", 0, 6), -GATE, R("nq"), ACT.Relu)
-    tt(R("s2p", 6, 10), R("land1", 10, 14), W("sa", 256 + NL, 4), A.add)
-    tt(R("ab"), R("land3", 6, 18), R("b3w"), A.add)
+    if d:
+        act(W("sa", P + 80, 1), W("sa", P + 80, 1), 1.0, R("g5"))
+    cp(R("e1", 2, 12, 3), R("co", 26, 36, 3), "s")
+    cp(R("e1", 14, 30, 3), R("co", 8, 24, 3), "s")
+    cp(R("s1x"), PS(1, 128 - NX, 128), "s")
+    act(R("e1", 1, 12, 3), W("sb", 2 * NL, 4), -1.0, float(N4 - C1 - D1X))
+    act(R("e1", 13, 30 - 3 * last, 3), R("co", 7, 24 - 3 * last, 3), -1.0, float(N4 - C1))
+    if last:
+        act(R("e1", 28, 29), R("co", 23, 24), -1.0, R("pb"))
     mask("mf", 0, PS(2, d, P), 0)
     if d:
         mask("mf", P - 1, PS(2, 0, 1), 15)
-    tt(R("zz"), R("ab"), R("gt"), A.subtract)
+    tt(R("s2p"), R("a2f"), W("sa", 256, 10), A.add)
     squeeze("sf", "mf", 0, P)
-    tt(R("s3", 0, 6), R("zz", 0, 6), R("zz", 6, 12), A.max)
+    tt(R("s3", 0, 6), R("land3"), W("sa", P, 6), A.add)
     tt(R("s1p"), R("land1", 0, 10), W("sf", 0, 10), A.add)
-    tt(R("thr"), R("s3"), R("s2p"), A.max)
-    tt(R("d1", 0, 18, 3), R("s3", 0, 6), R("s2p", 0, 6), A.is_gt)
-    tt(R("d1", 30, 48, 3), R("s3", 0, 6), R("s2p", 0, 6), A.is_gt)
-    tt(R("d0", 2, 30, 3), R("s1p"), R("thr"), A.is_lt)
-    tt(R("d0", 32, 60, 3), R("s1p"), R("thr"), A.is_lt)
-    tt(R("msg2", 10, 15), R("s1p", 5, 10), R("thr", 5, 10), A.max)
-    scan(R("so"), R("d0"), R("d1"))
+    cp(R("offs"), R("e1", 2, 30, 3))
+    tt(R("msg2", 10, 20), R("s1p"), R("s2p"), A.max)
+    tt(R("d0", 1, 30, 3), R("s1p"), R("s2p"), A.is_lt)
+    tt(R("d0", 2, 30, 3), R("s3"), R("msg2", 10, 20), A.is_le)
+    scan(R("sp"), R("d0"), R("db1"))
+    scan(R("so"), R("d0"), R("da1"))
+    cp(R("msg2", 0, 10), R("sp", 2, 30, 3), "s")
     cp(R("offp"), R("so", 2, 30, 3))
-    cp(R("msg2", 0, 10), R("so", 32, 60, 3), "s")
-    pick("pool", 0, "wn", 512, N3, "offp")
+    pick("pool", 0, "wn", C3, N3, "offp")
     send(-1, R("land2"), R("msg2"), "am2")
     send(-1, R("plandq"), R("poolq"), "apq")
     send(-1, R("plands"), R("pools"), "aps")
     iota(R("spr", 0, CAPP), [[0, CAPP]], 1)
     iota(R("spr", CAPP, P), [[0, NL]])
 
-    mm(1, "uab", 0, "wn", 512 + V0, 128)
-    mm(2, "uab", 128, "wn", N3 + NX - 128, 128)
-    for t, bank in enumerate(BANKS):
-        mm(bank, "wt", 128 * t, "wn", 512 + V0, 128, True, False)
-        mm(bank, "wt", 512 + 128 * t, "wn", N3 + NX - 128, 128, False, True)
-    mm(4, "uu", 0, "wn", 512, P)
-    cp(R("s1x"), PS(1, 128 - NX, 128), "s")
-    for t, bank in enumerate(BANKS):
-        relu("s", "h3x", 128 - NX, t, bank, 128 - NX, 128)
-    quant("wn", 256, P, "h2")
-    tt(R("cr", 80 - NX, 80), R("s1x"), PS(2, 128 - NX, 128), A.add)
-    cp(R("offs", 0, 4), R("co", 20, 30, 3))
-    mask("md", 0, R("cr"), 0)
-    cp(R("offs", 4, 10), R("co", 2, 18, 3))
-    squeeze("sd", "md", 0, 80)
-    act(R("cle", 0, 48, 3), R("sg"), 1.0, None, ACT.Relu)
-    act(R("cgt", 0, 48, 3), R("sg"), -1.0, None, ACT.Relu)
-    for i in (1, 2):
-        act(R("cle", i, 48, 3), R("sh"), 256.0 ** i)
-        act(R("cgt", i, 48, 3), R("sh"), -256.0 ** i, 256.0 ** i)
-    pick("w4", 0, "win", 0, CA + HB, "off3")
-    quant("w4", 512 + V0, 128, "h3x")
-    places("ysb", 0, 3)
-    places("ysb", P, 4)
-    gather("v", R("spr", P, 2 * P), R("spw"), "offs")
+    mm(0, "uab", 128, "wn", N3 + NX - 128, 128)
+    lefts(HI, "wn", C3 + V0, 128)
+    rights(HI, "wn", N3 + NX - 128, 128)
+    quant("wn", 256 + X0, 128, "h2")
+    tt(R("cr", 80 - NX + x0, 80), R("s1x", x0, NX), PS(0, 128 - NX + x0, 128), A.add)
+    quant("uu", 0, 128, "hu")
+    mm(1, "uu", 0, "win", C1, 128)
+    mm(2, "uu", 0, "win", C2, 128)
+    mm(3, "uu", 0, "wn", C3, P)
+    for t in range(4):
+        relu("s", "h3x", 128 - NX, t, HI[t], 128 - NX, 128)
+    gather("s", R("spr", P, 2 * P), R("spw"), "offs")
+    c0 = 0 if last else 16
+    mask("md", c0, R("cr", c0, 80), 0)
+    quant("win", S3, 128, "h3x")
+    squeeze("sd", "md", c0, 80)
 
-    tt(R("u6", 5, 10), W("sd", 0, 5), R("land2", 10, 15), A.is_gt)
-    tt(R("v0"), R("land2", 0, 10), R("pw5"), A.subtract)
     ts(R("offl"), R("land2", 0, 10), 512.0, A.mult)
-    tt(R("v1", 0, 4), R("v0", 6, 10), R("u6", 6, 10), A.max)
-    tt(R("v1", 4, 10), R("v0", 0, 6), R("u6", 0, 6), A.max)
-    pick("left", 0, "wn", 0, 512 + P, "offl")
+    if last:
+        tt(R("u6"), W("sd", 0, 5), R("land2", 15, 20), A.is_gt)
+    else:
+        tt(R("e1", 0, 12, 3), W("sd", 16, 4), R("land2", 16, 20), A.is_gt)
+    pick("left", 0, "wn", 0, C3 + P, "offl")
+    lefts(HI, "left", 0, P)
+    rights(HI, "pland", 0, P)
+    if last:
+        cp(R("e1", 0, 12, 3), R("u6", 1, 5), "s")
+        cp(R("e1", 27, 28), R("u6", 0, 1), "s")
+    cp(R("ysb", CAPP, P), PS(1, 0, NL), "s")
+    cp(R("ysb", 0, CAPP), PS(2, 2, NX), "s")
+    nc = 6 - last
+    tt(R("v0"), R("land2", 5, 10), R("pw5", 5, 10), A.subtract)
+    tt(R("v1", 4, 4 + nc), R("land2", 0, nc), R("pw5", 0, nc), A.subtract)
+    tt(R("v1", 0, 4), R("v0", 1, 5), R("u6", 1, 5) if last else R("e1", 0, 12, 3), A.max)
+    if last:
+        tt(R("v1", 9, 10), R("v0", 0, 1), R("u6", 0, 1), A.max)
     ts(R("offk"), R("v1"), 2.0, A.mult, R("q3"), A.add)
-    for t in range(4):
-        mm(t, "wt", 128 * t, "left", 0, P, True, False)
-    for t in range(4):
-        mm(t, "wt", 512 + 128 * t, "pland", 0, P, False, True)
-    dma("y", T.y[:, 0:2 * P], ap(R("ysb", 0, 2 * P)), [R("ysb", 0, 2 * P), R("plands")], [])
     step = 1.0 / 256 - 1.0 / 65536
-    act(R("v3"), R("v1"), -2.0, 1.0, ACT.Relu)
     gather("v", R("wr"), R("cle"), "offk")
     gather("s", R("wg", 16, P + 16), R("cgt"), "offk")
+    act(R("v3"), R("v1"), -2.0, 1.0, ACT.Relu)
     act(R("v4"), R("v1"), -2.0 * step, 2.0 * step + 1.0 / 65536)
-    act(R("e0", 1, 8, 2), R("u6", 6, 10), 256.0, 256.0)
-    act(R("e0", 9, 20, 2), R("u6", 0, 6), 256.0, 256.0)
     act(R("v5"), R("v1"), 2.0, 1.0)
+    cp(R("ysb", P, P + CAPP), PS(3, NL, P), "s")
+    cp(R("ysb", P + CAPP, 2 * P), PS(3, 0, NL), "s")
+    dma("y", T.y[:, 0:2 * P], ap(R("ysb", 0, 2 * P)), [R("ysb", 0, 2 * P), R("plands")], [])
     scan(R("sf"), R("wg", 0, P), R("wr"), A.add)
     tt(R("v2"), R("v3"), R("v4"), A.max)
     tt(R("ci"), W("sf", 0, 10), R("v2"), A.mult)
     ts(R("cj"), R("ci"), 255, A.bitwise_and)
-    ts(R("e1", 0, 20, 2), R("cj"), CAPP + 0.5, A.is_lt)
+    ts(R("e0", 2, 30, 3), R("cj"), CAPP + 0.5, A.is_lt)
     scan(R("eo"), R("e0"), R("e1"))
-    relu("v", "h4", 0, 3, 3, 0, P)
-    cp(R("off4"), R("eo", 1, 20, 2))
+    tt(R("v6"), R("v5"), R("e0", 2, 30, 3), A.mult)
+    cp(R("off4"), R("eo", 2, 30, 3))
+    relu("v", "h4", 0, 3, HI[3], 0, P)
     for t in range(3):
-        relu("s", "h4", 0, t, t, 0, P)
-    quant("w4", 256, P, "h4")
-    tt(R("v6"), R("v5"), R("e1", 0, 20, 2), A.mult)
-    pick("c4", 0, "w4", 0, 672, "off4")
+        relu("s", "h4", 0, t, HI[t], 0, P)
+    quant("win", N4, P, "h4")
     cp(R("offt"), R("v6"))
+    pick("c4", 0, "win", C1, WIN, "off4")
     gather("v", R("spr", 2 * P, 3 * P), R("cst"), "offt")
-    mm(4, "uu", 0, "c4", 0, P)
+    mm(0, "uu", 0, "c4", 0, P)
     dma("y", T.oc[:, :], view(R("c4q")), [R("c4q")], [])
-    cp(R("ysb", 2 * P, 3 * P), PS(4, 0, P), "s")
+    cp(R("ysb", 2 * P, 3 * P), PS(0, 0, P), "s")
     dma("s", T.y[:, 2 * P:3 * P], ap(R("ysb", 2 * P, 3 * P)), [R("ysb", 2 * P, 3 * P)], [])
     for k in range(4):
         dma("y", T.osc[4 * k:4 * k + 4, :], T.c4s[32 * k:32 * k + 4, :], [R("c4s")], [])

@@ -6,7 +6,7 @@ X0 = NL - 2
 NX = P - X0
 V0 = P - 128
 XW = 2 * NX + 2
-BIG = 1.0e29
+BIG, GATE = 1.0e29, 2.0 ** 80
 CODE, PLANE, F, BF, I32, U16 = "float8_e4m3fn_x4", "uint8", "float32", "bfloat16", "int32", "uint16"
 CN, C1, C2, CL, CX, N4, S3, WIN = 64, 128, 352, 560, 752, 896, 1056, 1184
 C3, NE, N1, N2, N12, N3, WN = 512, 704, 768, 864, 1026, 1092, 1158
@@ -25,26 +25,51 @@ SCRATCH = {}
 for _n, _w in (("wt", 1024), ("uu", 128), ("uab", 256), ("win", WIN), ("wn", WN), ("pool", P), ("pland", P),
                ("left", P), ("c4", P)):
     SCRATCH.update(_pair(_n, _w))
-SCRATCH.update(_f(BF, hx=896, h2=4 * XW, hu=512, hv=8, huab=1024, he=8 * NL, hc=4 * XW, h3x=512, h4=640, ones=128,
-                  keep=192, tmod=192, mr=256, mb=256, sb=256, spw=768))
-SCRATCH.update(_f(F, msk=192, mskx=NX, a1d=NL, sl=192, ax=XW, sx=XW, ma=416, sa=416, mc=192, sc=192, md=80, sd=80,
-                  me=64, se=64, mf=P, sf=P, junk=64, s1x=NX, wr=P, ysb=3 * P, spr=3 * P, cst=8, cle=48,
-                  cgt=48, msg1=14, msg3=6, land1=14, land3=6, msg2=20, land2=20))
+SCRATCH.update(_f(BF, hx=896, h2=4 * XW, hu=512, hv=8, huab=1024, he=8 * NL, hc=4 * XW, h3x=512, h4=640, hl=512,
+                  ones=128, keep=192, tmod=192, mr=256, mb=256, sb=256, spw=768))
+SCRATCH.update(_f(F, msk=192, mskx=NX, a1d=NL, sl=192, ax=NX, sx=NX, ma=416, sa=416, mc=192, sc=192, md=80, sd=80,
+                  me=192, se=192, fx=36, fy=32, mf=P, sf=P, junk=128, s1x=NX, wr=P, ysb=3 * P, spr=3 * P, cst=8, cle=48,
+                  cgt=48, msg1=14, msg3=18, land1=14, land3=18, msg2=15, land2=15))
 SMALL, _at = {}, [0]
-for _n, _w in dict(d0=30, c0=24, c1=24, e0=30, e1=30, wg=P + 16, s3=10, cr=80, qf=1, q3=1, pw=10, pw5=10, ph=1,
-                   k63=1, k64=6, jw=10, t0=10, t1=10, t2=10, xm=1, gg=18, xx=12, yy=12, gt=12, a1w=12, a2f=10,
-                   zz=12, j16=16, sg=16, nn=1, u1=6, s2p=10, pe=4, s1p=10, da1=30, db1=30, so=30, sp=30, co=36, sh=16,
-                   th0=8, df=1, pb=1, az=12, g5=1, v0=5, u6=5, v1=10, v2=10, v3=10, v4=10, v5=10, v6=10,
-                   eo=30).items():
+for _n, _w in dict(d0=30, c0=24, c1=24, e0=30, e1=30, f5=36, wg=P + 16, s3=10, cr=80, qf=1, q3=1, pw=10, pw5=10, ph=1,
+                   k64=6, jw=10, t0=10, t1=10, t2=10, xm=1, gg=18, xx=12, yy=12, gt=12, a1w=12, a2f=10, zz=12, j16=16,
+                   sg=16, nn=1, u1=6, s2p=10, thr=10, pe=4, s1p=10, da1=30, db1=30, so=30, sp=30, co=36, sh=16, th6=6,
+                   e15=1, kt=1, ka=1, k5e=1, k5n=1, d2e=1, d2n=1, da=1, at=1, a0=1, a1=1, f4=8, nr=1, nq=1, ab=12,
+                   b3w=12, g5=1, v0=5, u6=5, v1=10, v2=10, v3=10, v4=10, v5=10, v6=10, eo=30).items():
     SMALL[_n] = (_at[0], _w)
     _at[0] += _w
 SCRATCH.update(_f(F, small=_at[0]))
 SCRATCH.update(_f(I32, qi=1, qj=1, ci=10, cj=10))
-SCRATCH.update(_f(U16, off3=10, offp=10, offl=10, offk=10, off4=10, offs=10, offt=10))
+SCRATCH.update(_f(U16, offa=6, offb=6, offp=10, offl=10, offk=10, off4=10, offs=10, offt=10))
 for _b in range(8):
     SCRATCH["ps%d" % _b] = ("psum", [128, 512], F)
 ARR = ["an1q", "an1s", "an2q", "an2s", "an3q", "an3s", "an12q", "an12s", "am1", "am2", "am3", "apq", "aps"]
 SEMAPHORES = ["cg"] + ARR + ["sent"] + ["d%d" % i for i in range(16)] + ["cv", "cs", "ct"]
+
+ISSUE = {
+    0: ('(0(7(9(1(3(2(4(8(:(;(5(<(=(6)D)@(>(?(@(N(K(C(B(L(I(J)I(M(H(G(R(F(P)5(Q(U)6(O(A(E)2(W(D)U)3(T)1)C)7)0)?)B'
+        ')<)=):)>)E)G)F)S)9)T)H)4(V)L)J)N*8)8)V)R);)W)M*0)K)A*4*;(S)Q)O*<)P*?*C*=*@*D*>*A*H*B*:*2*G*P*E*7*I*1*R*N'
+        '*6*L*F+9*O*3*W*Q*9+:+0*U+1*S*J+2+?+5*T+6+3*V+J+4*K+E+=+<+8*5+C+U+@+7+V+D,@+B+I+H,1+R,7+L+T*M+S,2+>+G,3,5'
+        ',9,4+M+W,:,6+A,8,;+O,E+K,<+P,F,H,A,0,C-V,I+F,J,G,=+N,L,K,N-W,>-=+Q,M,V,D,?,O,P,U-:+;,Q,B-6,R-0,W,S-1,T-;'
+        '-7-9-2-4-3-5-8-B-<-D-A.0-C->-F-?.1-@-E-G-H.2-I-J.3-K-M-N.7-O-P.4-S-R-Q.6.5.:-L-U.D.8-T.?.;.@.A.9.B.<.F.G'
+        '.>.H.I.K.J.=.C.V.W.N/0.E.U.O/3/1/2.L.T.M/9/4/5/6/:.P/7/;/8.Q/</@/=.R/A/>/?.S/D/B/C/E/F/H/G/I/K/J/N/O/P/Q'
+        '/R/L/M'),
+    1: ('(0(7(9(1(3(2(4(8(:(;(5(<(=(6)D)@(>(?(@(N(K(C(B(L(I(J(M(G(H(R(F(P)5(Q(U)6(O(A(E)2(W(D)Q)3(T)1)C)7)0)?)B)<'
+        ')=):)>)E)H)O)9)F)P)J)4*3(V)R)I)N)G)S)8)A)W(S);)M)K)L*6*7*:*>*8*;*?*9*<*C*=*5)U*B*J*@*2*D)T*L*H*1*F*A+3*I'
+        ')V*Q*K*4+4*R*O*S*M*E*T+7*W*N+0*U*P+B*V+=+6*0+2+M+;+8+N+1+<,8+:+A+@+Q+J+W+D+L*G+K+R+S+?+U+T,1+O+E+V,2,0+9'
+        ',3+G,=+C,4+H,>,@,9+P,;-M,A+>,B,?,5+F,D,C,F-N,6-4+I,E,N,<,7,G,H,M-1,:+5,I,U,J,P,O,K,Q,L-2,V-0,R,S-9,T,W-;'
+        '-3-8-:-O-=-5-6-<-P-7->-?-@-Q-A-B-R-D-E-F-V-G-J-S-I-H-U.1-T-C-L.;-K-W.2.6.7.0.8.3.9.=.5.>.?.@.B.4.A.:.M.N'
+        '.E.O.<.L.F.R.P.Q.C.K.D/0.S.T.U/1.G.V/2.W.H/3/7/4.I/8/5/6.J/;/9/:/</=/?/>/@/B/A/E/F/G/H/I/C/D'),
+    3: ('(0(7(9(1(3(2(4(8(:(;(5(<(=(6)D)@(>(?(@(N(K(C(B(L(I(J)F(M(H(G(R(F(P)5(Q(U)6(O(A(E)2(W(D)R)3(T)1)C)7)0)?)B'
+        ')<)=):)>)E)I)P)9)G)Q)K)4*=(V)S)J)O)H)T)8)A*9*0);)N(S)L)U*@)M)V*4*A*2*D*H*B*E*I*C*3*F*M*G*?*7*L*T)W*J*N*<'
+        '*V*R*6*P*1+4*S*;+>*U*K+3*8*>+?+1+5+6*W+7*O+B+0+:+8+;+2+9+M+H+A*:+=,0+F*5+C,1+<+G,G+E+L+K,7+U,=+O+W*Q+V,8'
+        ',9+J,;,:,?,6+P,2,@,<+D,5,A+R,>,L,4+N,C,B+S,M,O,H,Q,R,P+I.7,3,S,J,T+Q,D,N,V.8-0,U+T,E,W-F-8,K,F-1-2-7,I-C'
+        '+@-3-?-4-:-9-5-;-6-D-@-B-<-=-K->-A-M-E-J-L.9-O-G-H-N.:-I-P-Q-R.;-S-T.<-V-W.0.@.1.4.=.3.2.?.C.>-U.6.M.5.A'
+        '.D.H.I.B.J.K.E.O.G.P.Q.R.T.S.F/5/9.L/:.W/;/</0.N/8/?/=/>.U.V/7/E/@/A/1/6/F/B/C/G/2/L/D/H/3/I/M/J/4/K/N/P'
+        '/O/Q/R/T/S/U/W/V02030405060001'),
+}
+ISSUE[2] = ISSUE[1]
+ORDER = {r: [(ord(s[i]) - 40) * 40 + ord(s[i + 1]) - 48 for i in range(0, len(s), 2)] for r, s in ISSUE.items()}
 
 
 def rank_program(g, core, T, topo):
@@ -99,13 +124,24 @@ def rank_program(g, core, T, topo):
             for r in rs:
                 log.setdefault(r[0], []).append((r[1], r[2], r[3], ev, wr, tag))
 
+    prog = []
+
     def op(q, fn, reads, writes):
+        prog.append((q, lambda: op_(q, fn, reads, writes), reads, writes))
+
+    def dma(q, out, in_, reads, writes):
+        prog.append((q, lambda: dma_(q, out, in_, reads, writes), reads, writes))
+
+    def send(k, dst, src, sem):
+        prog.append(("g", lambda: send_(k, dst, src, sem), [src], []))
+
+    def op_(q, fn, reads, writes):
         order(q, reads, writes)
         count[own[q]] += 1
         fn().then_inc(T.sem[own[q]], 1)
         note(q, q, (own[q], count[own[q]]), reads, writes)
 
-    def dma(q, out, in_, reads, writes):
+    def dma_(q, out, in_, reads, writes):
         order(q, reads, writes)
         s = "d%d" % dmas[0]
         dmas[0] += 1
@@ -119,7 +155,7 @@ def rank_program(g, core, T, topo):
     def view(r):
         return ap(r).bitcast(dt.uint8) if SCRATCH[r[0]][2] == CODE else ap(r)
 
-    def send(k, dst, src, sem):
+    def send_(k, dst, src, sem):
         order("g", [src], [])
         to = peer(k)
         rid, pid = topo.addr(to)[:2]
@@ -196,17 +232,13 @@ def rank_program(g, core, T, topo):
             mm(banks[t], "wt", 512 + 128 * t, mv, ma, w, False, True)
 
     def relu(q, h, ha, t, bank, a, b):
-        o, i = R(h, 4 * ha + t, 4 * (ha + b - a), 4), PS(bank, a, b)
-        if q == "v":
-            ts(o, i, 0.0, A.max, 0.05, A.mult)
-        else:
-            act(o, i, 0.05, None, ACT.Relu)
+        act(R(h, 4 * ha + t, 4 * (ha + b - a), 4), PS(bank, a, b), 0.05, None, ACT.Relu)
 
-    def pick(dst, da, src, sa, sb, off):
-        o, i, l = R(dst + "q", da, da + P), R(src + "q", sa, sb), R(off)
+    def pick(dst, da, src, sa, sb, off, w=P):
+        o, i, l = R(dst + "q", da, da + w), R(src + "q", sa, sb), R(off, 0, w // 16)
         op("v", lambda: g.vector.tensor_copy(ap(o).bitcast(dt.uint32), ap(i).bitcast(dt.uint32).indirect(ap(l))),
            [i, l], [o])
-        o2, i2 = R(dst + "s", da, da + P), R(src + "s", sa, sb)
+        o2, i2 = R(dst + "s", da, da + w), R(src + "s", sa, sb)
         op("s", lambda: g.scalar.activation(ap(o2), ap(i2).indirect(ap(l)), ACT.Copy), [i2, l], [o2])
 
     def gather(q, o, win, off):
@@ -233,7 +265,7 @@ def rank_program(g, core, T, topo):
     x1 = 2 * last
     x0 = 2 - x1
     PE = P - x1
-    LO, HI, XB = (0, 1, 2, 3), (4, 5, 6, 7), (1, 2, 3, 0)
+    LO, HI = (0, 1, 2, 3), (4, 5, 6, 7)
 
     def cells(k, buf, a, w, at, s, early=0, cut=0):
         for x in "qs":
@@ -267,8 +299,6 @@ def rank_program(g, core, T, topo):
     fill(R("ones"), 1.0)
     ts(R("pw"), R("t0"), R("qf"), A.add)
     fill(R("h3x", 0, 4 * (128 - NX)), 0.0)
-    if last:
-        fill(R("he", 4 * X0, 4 * NL), 0.0)
 
     quant("win", CN, P, "hx")
     cells(1, "wn", NE, P, CN, "an1", d, d)
@@ -285,11 +315,14 @@ def rank_program(g, core, T, topo):
     cp(R("h2", 4 * NX, 4 * NX + 8), R("hx", 4 * CAPP, 4 * CAPP + 8), "s")
     cp(R("h2", 4 * NX + 8, 4 * XW), R("hx", 4 * P - 8, 4 * (P + CAPP)), "s")
     mm(7, "uab", 0, "win", C1, P)
-    lefts(LO, "win", CN, PE)
+    lefts(LO, "win", CN, 128)
     quant("wn", 0, P, "hx", CAPP)
     mask("ma", 0, PS(7, 0, P), 0)
     cp(R("a1d"), PS(7, 0, NL), "s")
-    lefts(HI, "win", C1, 128, (0, 1))
+    cp(R("hl", 0, 128), R("hx", 512, 4 * P), "s")
+    cp(R("hl", 128, 512), R("hx", 4 * CAPP, 4 * P), "s")
+    quant("wn", 384, 128, "hl")
+    lefts(HI, "wn", 384, 128)
     act(R("ph"), R("qf"), 1.0, 0.5)
     act(R("sh"), R("j16"), -1.0, R("qf"), ACT.Sign)
     act(R("sg"), R("j16"), -1.0, R("ph"), ACT.Sign)
@@ -321,139 +354,157 @@ def rank_program(g, core, T, topo):
     if d:
         act(R("g5"), R("xm"), -BIG)
     if last:
-        cp(R("mskx", 0, 2), R("msk", X0 % 16, X0 % 16 + 2), "s")
-        act(R("k63"), R("pw", 5, 6), -1.0, CAPP - 1.0)
-        act(R("c0", 1, 2), R("xm"), float(D1X - D1L), float(D1L))
-        act(R("c0", 4, 5), R("xm"), 0.0, -float(D2L))
-        act(R("c1", 4, 5), R("xm"), 0.0, float(D2L))
-        act(R("pb"), R("pw", 5, 6), 1.0, float(N4 - C1))
-        for a in (2, 5):
-            cp(R("c1", a, a + 1), R("pw", 5, 6), "s")
+        ts(R("e15"), R("qf"), 15.0, A.is_equal)
+        act(R("kt"), R("e15"), float(CAPP - NL))
+        act(R("ka"), R("e15"), float(NL - CAPP), R("k64", 5, 6))
+        act(R("da"), R("xm"), float(D1X - D1L), float(D1L))
+        act(R("k5e"), R("e15"), -float(D2L + D1X))
+        act(R("k5n"), R("xm"), float(D1L - D1X), -float(D1L + D2L))
+        act(R("k5n"), R("e15"), float(D2L + D1X), R("k5n"))
+        act(R("d2e"), R("e15"), float(D2L))
+        act(R("d2n"), R("e15"), -float(D2L), float(D2L))
     act(R("cle", 0, 48, 3), R("sg"), 1.0, None, ACT.Relu)
     act(R("cgt", 0, 48, 3), R("sg"), -1.0, None, ACT.Relu)
     for i in (1, 2):
         act(R("cle", i, 48, 3), R("sh"), 256.0 ** i)
         act(R("cgt", i, 48, 3), R("sh"), -256.0 ** i, 256.0 ** i)
-    act(R("da1", 0, 30, 3), R("t2"), 1.0, float(N1 - C3))
-    act(R("da1", 1, 30, 3), R("t2"), 0.0, -float(N2 - C3))
-    act(R("da1", 2, 30, 3), R(jw), 1.0, float(N2 - C3))
-    act(R("db1", 1, 30, 3), R("pw"), 0.0, -1.0)
-    act(R("db1", 2, 30, 3), R("pw"), 1.0 / 512, 1.0)
+    act(R("da1", 0, 30, 3), R("t2"), -1.0, float(N2 - N1))
+    act(R("da1", 1, 30, 3), R("t2"), 1.0, float(N1 - C3))
+    cp(R("da1", 2, 30, 3), R(jw), "s")
+    act(R("db1", 2, 30, 3), R("pw"), 1.0 / 512)
 
-    mm(7, "uab", 128, "wn", NE, PE)
-    rights(LO, "wn", NE, PE)
-    tt(R("sl", 0, NL - x1), PS(7, CAPP, PE), R("a1d", 0, NL - x1), A.add)
-    mask("ma", 256, PS(7, CAPP + d, PE), 0)
-    if d:
-        mask("ma", 415, PS(7, CAPP, CAPP + 1), 15)
-    squeeze("sa", "ma", 256, 336)
-    lefts(HI, "win", C1, 128, (2, 3))
+    rights(LO, "wn", NE, 128)
     for t in range(4):
         relu("s", "h2", 2, t, t, 0, CAPP)
     for t in range(4):
-        relu("s", "he", 0, t, t, CAPP, PE)
+        relu("s", "he", 0, t, t, CAPP, 128)
     quant("win", C2, XW, "h2")
+    mm(0, "uab", 128, "wn", NE, PE)
+    tt(R("sl", 0, NL - x1), PS(0, CAPP, PE), R("a1d", 0, NL - x1), A.add)
+    mask("ma", 256, PS(0, CAPP + d, PE), 0)
+    if d:
+        mask("ma", 415, PS(0, CAPP, CAPP + 1), 15)
+    mask("me", 128, PS(0, d, CAPP + d), 0)
+    squeeze("sa", "ma", 256, 336)
     cells(1, "wn", N12 - 2, NX + 2, C2 - 2, "an12")
-    cells(3, "wn", N3, NX, C1 + X0, "an3")
 
-    mm(0, "uab", 128, "wn", N2 - x1, 128)
-    rights(HI, "wn", N2, 128)
-    mm(1, "uab", 0, "win", C2, XW)
-    tt(R("sl", NL, 2 * NL), PS(0, x1, NL + x1), R("a1d"), A.add)
+    mm(1, "uab", 128, "wn", N2 - x1, P + x1)
+    rights(HI, "wn", N2 - 32, 128)
+    mm(2, "uab", 0, "win", C2, 128)
+    mm(3, "uab", 128, "win", C2, 128)
+    tt(R("sl", NL, 2 * NL), PS(1, x1, NL + x1), R("a1d"), A.add)
     if last:
-        tt(R("sl", X0, NL), PS(0, 0, 2), R("a1d", X0, NL), A.add)
+        tt(R("sl", X0, NL), PS(1, 0, 2), R("a1d", X0, NL), A.add)
     tt(R("mr", NL, 2 * NL), R("sl", NL, 2 * NL), R("sl", 0, NL), A.is_gt)
     for t in range(4):
-        relu("s", "he", NL, t, HI[t], 0, NL)
+        relu("s", "he", CAPP, t, HI[t], 0, 128)
     scan(R("mr", 0, NL), R("ones", 0, NL), R("mr", NL, 2 * NL), A.add, A.subtract)
     mask("mb", NL, R("mr", NL, 2 * NL), 0)
     mask("mb", 0, R("mr", 0, NL), 0)
     quant("win", CL, 2 * NL, "he")
-    mask("ma", P, PS(0, d + x1, NL + d + x1), 0)
-    mask("me", 0, PS(1, 2, NX), 0)
-    cp(R("ax"), PS(1, 0, XW), "s")
-    lefts(XB, "win", C2, XW, (1, 2))
-    mm(5, "uab", 0, "win", CL, 2 * NL)
-    lefts(XB, "win", C2, XW, (3, 0))
+    mask("ma", P, PS(1, d + x1, NL + d + x1), 0)
+    squeeze("sa", "ma", P, 256)
+    for a in (0, 6):
+        cp(R("b3w", a, a + 6 - d), W("sa", P, 6 - d), "s")
+        if d:
+            act(R("b3w", a + 5, a + 6), W("sa", P + 80, 1), 1.0, R("g5"))
+    mask("me", 0, PS(2, 2, NX), 0)
+    cp(R("ax"), PS(2, 0, NX), "s")
+    tt(R("sx"), PS(1, X0 + x1, P + x1), R("ax"), A.add)
+    mask("me", 64, PS(3, 2 + d, NX + d), 0)
+    lefts(LO, "win", C2, XW, (0,))
+    mm(4, "uab", 0, "win", CL, 2 * NL)
+    mm(5, "uab", 0, "win", C1 + V0, 128, True, False)
+    lefts(LO, "win", C2, XW, (1, 2, 3))
     squeeze("sb", "mb", 0, 2 * NL)
     squeeze("se", "me", 0, 64)
-    mm(4, "uab", 128, "wn", N2 + X0, XW)
-    rights(XB, "wn", N2 + X0, XW)
-    cw, mw = W("sb", 0, 6), W("sb", NL, 6)
+    squeeze("se", "me", 64, 192)
+    mm(5, "uab", 128, "wn", N3 - 128, 128, False, True)
+    rights(LO, "wn", N2 + X0, XW)
+    mm(6, "uab", 128, "wn", N3 - 128, 128)
+    mw = W("sb", NL, 6)
     m5 = W("sb", NL + 80, 1)
     act(R("gg", 6, 12), mw, BIG, -BIG)
     act(R("gg", 12, 18), mw, -BIG)
     act(R("gg", 0, 6), mw, -BIG)
     cp(R("msg1", 10, 14), W("se", 0, 4), "s")
     send(1, R("land1"), R("msg1"), "am1")
-    dma("y", ap(R("hu")), T.u[:, :], [R("wns", N12, N3)], [R("hu")])
-    act(R("c0", 7, 24, 3), mw, -float(D1L + D2L), float(D1L))
-    act(R("c1", 7, 24, 3), mw, float(D2L))
+    act(R("c0", 7, 24 - 3 * last, 3), W("sb", NL, 6 - last), -float(D1L + D2L), float(D1L))
+    act(R("c1", 7, 24 - 3 * last, 3), W("sb", NL, 6 - last), float(D2L))
     if last:
-        act(R("th0", 0, 1), W("sb", 80, 1), 1.0, m5)
-        act(R("th0", 1, 2), R("th0", 0, 1), 1.0, R("k63"))
-    mask("mc", 0, PS(5, 0, 2 * NL), 0)
-    tt(R("u1"), R("k64"), mw, A.mult)
+        act(R("at"), m5, R("ka"), W("sb", 80, 1))
+        act(R("a0"), m5, R("k5n"), R("da"))
+        act(R("a1"), m5, R("d2n"))
+    mask("mc", 0, PS(4, 0, 2 * NL), 0)
     squeeze("sc", "mc", 0, 2 * NL)
-    tt(R("th0", 2, 8), cw, R("u1"), A.add)
+    for c in range(6):
+        act(R("msg3", c, c + 1), W("sb", NL + 16 * c, 1), R("k64", c, c + 1), W("sb", 16 * c, 1))
     tt(R("xx"), R("a1w"), R("gg", 6, 18), A.add)
+    tt(R("yy"), W("sc", 0, 12), R("gg", 0, 12), A.add)
+    tt(R("msg3", 6, 18), R("yy"), R("xx"), A.max)
+    send(1, R("land3"), R("msg3"), "am3")
+    if last:
+        cp(R("th6", 0, 5), R("msg3", 0, 5), "s")
+    tt(R("f4"), R("land1", 6, 14), W("se", 64, 8), A.add)
+    tt(R("f5", 0, 4), R("f4", 0, 4), R("f4", 4, 8), A.is_lt)
+    scan(R("fx"), R("ones", 0, 36), R("f5"))
+    cells(3, "wn", N3, NX, C1 + X0, "an3")
+    dma("y", ap(R("hu")), T.u[:, :], [R("land3")], [R("hu")])
 
     for t in (0, 1):
-        relu("s", "hc", 0, t, XB[t], 0, XW)
-    tt(R("sx"), PS(4, 0, XW), R("ax"), A.add)
-    tt(R("yy"), W("sc", 0, 12), R("gg", 0, 12), A.add)
-    tt(R("mr", NL + X0 + x0, 256), R("sx", x0, NX), R("sx", NX + 2 + x0, XW), A.is_gt)
-    tt(R("az"), R("yy"), R("xx"), A.max)
-    act(R("junk"), R("mr", 2 * NL, 256), None, None, ACT.Identity, R("nn"))
-    relu("s", "hc", 0, 2, XB[2], 0, XW)
-    tt(R("mb", NL + X0 + x0, 256), R("mr", NL + X0 + x0, 256), R("mskx", x0, NX), A.mult)
-    ts(R("c1", 6 - 3 * x1, 24, 3), R("th0", 2 - x1, 8), R("nn"), A.is_le)
-    squeeze("sb", "mb", 176 if last else 192, 256)
-    act(R("gt", 0, 6), R("c1", 6, 24, 3), BIG, -BIG)
-    act(R("gt", 6, 12), R("c1", 6, 24, 3), -BIG)
-    relu("s", "hc", 0, 3, XB[3], 0, XW)
-    scan(R("co", 6 - 3 * x1, 24), R("c0", 6 - 3 * x1, 24), R("c1", 6 - 3 * x1, 24))
+        relu("s", "hc", 0, t, t, 0, XW)
+    tt(R("mr", NL + X0 + x0, 256), PS(5, 128 - NX + x0, 128), R("sx", x0, NX), A.is_lt)
+    act(R("junk", 0, 64), R("mr", 2 * NL, 256), None, None, ACT.Identity, R("nn"))
+    relu("s", "hc", 0, 2, 2, 0, XW)
+    if last:
+        m95 = R("mr", 2 * NL - 1, 2 * NL)
+        ts(R("th6", 5, 6), m95, R("kt"), A.mult, R("at"), A.add)
+        act(R("c0", 22, 23), m95, R("k5e"), R("a0"))
+        act(R("c1", 22, 23), m95, R("d2e"), R("a1"))
+    tt(R("mb", 2 * NL, 256), R("mr", 2 * NL, 256), R("mskx", 2, NX), A.mult)
+    ts(R("c1", 6, 24, 3), R("th6") if last else R("msg3", 0, 6), R("nn"), A.is_le)
+    squeeze("sb", "mb", 192, 256)
+    relu("s", "hc", 0, 3, 3, 0, XW)
+    scan(R("co", 6, 24), R("c0", 6, 24), R("c1", 6, 24))
+    cp(R("offa", 0, 5), R("co", 8, 21, 3))
     tt(R("co", 26, 36, 3), W("sb", 2 * NL, 4), R("pe"), A.add)
-    if last:
-        tt(R("df"), R("co", 5, 6), R("co", 2, 3), A.subtract)
-    tt(R("zz"), R("az"), R("gt"), A.add)
-    if last:
-        ts(R("co", 23, 24), m5, R("df"), A.mult, R("co", 2, 3), A.add)
-        tt(R("msg3"), R("zz", 0, 6), R("zz", 6, 12), A.max)
-        cp(R("off3"), R("co", 8, 36, 3))
-    else:
-        cp(R("off3"), R("co", 8, 36, 3))
-        tt(R("msg3"), R("zz", 0, 6), R("zz", 6, 12), A.max)
-    send(1, R("land3"), R("msg3"), "am3")
+    pick("wn", C3, "win", C1, CX, "offa", 80)
+    mm(7, "uab", 128, "wn", C3 - 48, 128)
+    op("v", lambda: g.vector.transpose(ap(R("fy")), ap(R("fx", 4, 36))), [R("fx")], [R("fy")])
+    act(R("junk", 80, 96), R("fy", 0, 16), -GATE, -GATE / 32, ACT.Identity, R("nr"))
+    act(R("junk", 96, 112), R("fy", 0, 16), GATE, GATE / 32, ACT.Identity, R("nq"))
     quant("win", CX, XW, "hc")
-    pick("wn", C3, "win", C1, CX + XW, "off3")
-    squeeze("sa", "ma", P, 256)
-    mask("ma", 256 + X0 - d, PS(4, NX + 2, XW), X0 - d)
-    mm(2, "uab", 128, "wn", C3, P)
-    mm(1, "uab", 0, "wn", C3 + V0, 128)
+    cp(R("offb", 0, 5), R("co", 23, 36, 3))
+    pick("wn", C3 + 80, "win", C1, CX + XW, "offb", 80)
+    mask("mf", 0, PS(7, 48 + d, 128), 0)
+    if d:
+        mask("mf", P - 1, PS(7, 48, 49), 15)
+    squeeze("sf", "mf", 0, 80 - 16 * d)
+    act(R("gt", 0, 6), R("land3", 0, 6), GATE, R("nr"), ACT.Relu)
+    act(R("gt", 6, 12), R("land3", 0, 6), -GATE, R("nq"), ACT.Relu)
+    mask("ma", 256 + X0 - d, PS(6, 128 - NX, 128), X0 - d)
+    mm(4, "uab", 128, "wn", C3 + V0, 128)
+    mm(5, "uab", 0, "wn", C3 + V0, 128)
     cp(R("a2f", 0, 6), R("land1", 0, 6), "s")
     cp(R("a2f", 6, 10), R("land1", 10, 14), "s")
     squeeze("sa", "ma", 336, 416)
-    if d:
-        act(W("sa", P + 80, 1), W("sa", P + 80, 1), 1.0, R("g5"))
     cp(R("e1", 2, 12, 3), R("co", 26, 36, 3), "s")
     cp(R("e1", 14, 30, 3), R("co", 8, 24, 3), "s")
-    cp(R("s1x"), PS(1, 128 - NX, 128), "s")
+    cp(R("s1x"), PS(5, 128 - NX, 128), "s")
     act(R("e1", 1, 12, 3), W("sb", 2 * NL, 4), -1.0, float(N4 - C1 - D1X))
-    act(R("e1", 13, 30 - 3 * last, 3), R("co", 7, 24 - 3 * last, 3), -1.0, float(N4 - C1))
-    if last:
-        act(R("e1", 28, 29), R("co", 23, 24), -1.0, R("pb"))
-    mask("mf", 0, PS(2, d, P), 0)
-    if d:
-        mask("mf", P - 1, PS(2, 0, 1), 15)
+    act(R("e1", 13, 30, 3), R("co", 7, 24, 3), -1.0, float(N4 - C1))
+    mask("mf", 80 - d, PS(4, 48, 128), 80 - d)
+    tt(R("ab"), R("land3", 6, 18), R("b3w"), A.add)
+    tt(R("zz"), R("ab"), R("gt"), A.subtract)
     tt(R("s2p"), R("a2f"), W("sa", 256, 10), A.add)
-    squeeze("sf", "mf", 0, P)
-    tt(R("s3", 0, 6), R("land3"), W("sa", P, 6), A.add)
+    tt(R("s3", 0, 6), R("zz", 0, 6), R("zz", 6, 12), A.max)
+    squeeze("sf", "mf", 80 - 16 * d, P)
     tt(R("s1p"), R("land1", 0, 10), W("sf", 0, 10), A.add)
+    tt(R("thr"), R("s3"), R("s2p"), A.max)
+    tt(R("d0", 1, 30, 3), R("s3"), R("s2p"), A.is_gt)
+    tt(R("d0", 2, 30, 3), R("s1p"), R("thr"), A.is_lt)
+    tt(R("msg2", 10, 15), R("s1p", 5, 10), R("s2p", 5, 10), A.max)
     cp(R("offs"), R("e1", 2, 30, 3))
-    tt(R("msg2", 10, 20), R("s1p"), R("s2p"), A.max)
-    tt(R("d0", 1, 30, 3), R("s1p"), R("s2p"), A.is_lt)
-    tt(R("d0", 2, 30, 3), R("s3"), R("msg2", 10, 20), A.is_le)
     scan(R("sp"), R("d0"), R("db1"))
     scan(R("so"), R("d0"), R("da1"))
     cp(R("msg2", 0, 10), R("sp", 2, 30, 3), "s")
@@ -465,17 +516,17 @@ def rank_program(g, core, T, topo):
     iota(R("spr", 0, CAPP), [[0, CAPP]], 1)
     iota(R("spr", CAPP, P), [[0, NL]])
 
-    mm(0, "uab", 128, "wn", N3 + NX - 128, 128)
-    lefts(HI, "wn", C3 + V0, 128)
-    rights(HI, "wn", N3 + NX - 128, 128)
+    mm(6, "uab", 128, "wn", N3 + NX - 128, 128)
+    lefts(LO, "wn", C3 + V0, 128)
+    rights(LO, "wn", N3 + NX - 128, 128)
     quant("wn", 256 + X0, 128, "h2")
-    tt(R("cr", 80 - NX + x0, 80), R("s1x", x0, NX), PS(0, 128 - NX + x0, 128), A.add)
+    tt(R("cr", 80 - NX + x0, 80), R("s1x", x0, NX), PS(6, 128 - NX + x0, 128), A.add)
     quant("uu", 0, 128, "hu")
-    mm(1, "uu", 0, "win", C1, 128)
-    mm(2, "uu", 0, "win", C2, 128)
-    mm(3, "uu", 0, "wn", C3, P)
+    mm(7, "uu", 0, "win", C1, 128)
+    mm(4, "uu", 0, "win", C2, 128)
+    mm(5, "uu", 0, "wn", C3, P)
     for t in range(4):
-        relu("s", "h3x", 128 - NX, t, HI[t], 128 - NX, 128)
+        relu("s", "h3x", 128 - NX, t, t, 128 - NX, 128)
     gather("s", R("spr", P, 2 * P), R("spw"), "offs")
     c0 = 0 if last else 16
     mask("md", c0, R("cr", c0, 80), 0)
@@ -484,19 +535,19 @@ def rank_program(g, core, T, topo):
 
     ts(R("offl"), R("land2", 0, 10), 512.0, A.mult)
     if last:
-        tt(R("u6"), W("sd", 0, 5), R("land2", 15, 20), A.is_gt)
+        tt(R("u6"), W("sd", 0, 5), R("land2", 10, 15), A.is_gt)
     else:
-        tt(R("e1", 0, 12, 3), W("sd", 16, 4), R("land2", 16, 20), A.is_gt)
+        tt(R("e1", 0, 12, 3), W("sd", 16, 4), R("land2", 11, 15), A.is_gt)
+    nc = 6 - last
+    tt(R("v0"), R("land2", 5, 10), R("pw5", 5, 10), A.subtract)
     pick("left", 0, "wn", 0, C3 + P, "offl")
-    lefts(HI, "left", 0, P)
-    rights(HI, "pland", 0, P)
+    lefts(LO, "left", 0, P)
+    rights(LO, "pland", 0, P)
     if last:
         cp(R("e1", 0, 12, 3), R("u6", 1, 5), "s")
         cp(R("e1", 27, 28), R("u6", 0, 1), "s")
-    cp(R("ysb", CAPP, P), PS(1, 0, NL), "s")
-    cp(R("ysb", 0, CAPP), PS(2, 2, NX), "s")
-    nc = 6 - last
-    tt(R("v0"), R("land2", 5, 10), R("pw5", 5, 10), A.subtract)
+    cp(R("ysb", CAPP, P), PS(7, 0, NL), "s")
+    cp(R("ysb", 0, CAPP), PS(4, 2, NX), "s")
     tt(R("v1", 4, 4 + nc), R("land2", 0, nc), R("pw5", 0, nc), A.subtract)
     tt(R("v1", 0, 4), R("v0", 1, 5), R("u6", 1, 5) if last else R("e1", 0, 12, 3), A.max)
     if last:
@@ -508,8 +559,8 @@ def rank_program(g, core, T, topo):
     act(R("v3"), R("v1"), -2.0, 1.0, ACT.Relu)
     act(R("v4"), R("v1"), -2.0 * step, 2.0 * step + 1.0 / 65536)
     act(R("v5"), R("v1"), 2.0, 1.0)
-    cp(R("ysb", P, P + CAPP), PS(3, NL, P), "s")
-    cp(R("ysb", P + CAPP, 2 * P), PS(3, 0, NL), "s")
+    cp(R("ysb", P, P + CAPP), PS(5, NL, P), "s")
+    cp(R("ysb", P + CAPP, 2 * P), PS(5, 0, NL), "s")
     dma("y", T.y[:, 0:2 * P], ap(R("ysb", 0, 2 * P)), [R("ysb", 0, 2 * P), R("plands")], [])
     scan(R("sf"), R("wg", 0, P), R("wr"), A.add)
     tt(R("v2"), R("v3"), R("v4"), A.max)
@@ -518,22 +569,23 @@ def rank_program(g, core, T, topo):
     ts(R("e0", 2, 30, 3), R("cj"), CAPP + 0.5, A.is_lt)
     scan(R("eo"), R("e0"), R("e1"))
     tt(R("v6"), R("v5"), R("e0", 2, 30, 3), A.mult)
+    for t in range(4):
+        relu("s", "h4", 0, t, t, 0, P)
     cp(R("off4"), R("eo", 2, 30, 3))
-    relu("v", "h4", 0, 3, HI[3], 0, P)
-    for t in range(3):
-        relu("s", "h4", 0, t, HI[t], 0, P)
     quant("win", N4, P, "h4")
     cp(R("offt"), R("v6"))
     pick("c4", 0, "win", C1, WIN, "off4")
     gather("v", R("spr", 2 * P, 3 * P), R("cst"), "offt")
-    mm(0, "uu", 0, "c4", 0, P)
+    mm(6, "uu", 0, "c4", 0, P)
     dma("y", T.oc[:, :], view(R("c4q")), [R("c4q")], [])
-    cp(R("ysb", 2 * P, 3 * P), PS(0, 0, P), "s")
+    cp(R("ysb", 2 * P, 3 * P), PS(6, 0, P), "s")
     dma("s", T.y[:, 2 * P:3 * P], ap(R("ysb", 2 * P, 3 * P)), [R("ysb", 2 * P, 3 * P)], [])
     for k in range(4):
         dma("y", T.osc[4 * k:4 * k + 4, :], T.c4s[32 * k:32 * k + 4, :], [R("c4s")], [])
     dma("y", T.sp[0:1, :], T.spr[0:1, :], [R("spr")], [])
 
+    for i in ORDER.get(rank, range(len(prog))):
+        prog[i][1]()
     for k in SEMAPHORES:
         if count[k]:
             wait("g", (k, count[k]))

@@ -2,15 +2,13 @@ from concourse.mybir import dt, AluOpType, ActivationFunctionType
 
 P, CAPP = 160, 64
 NL = P - CAPP
-X0 = NL - 2
-NX = P - X0
 V0 = P - 128
-XW = 2 * NX + 2
 BIG, GATE = 1.0e29, 2.0 ** 80
 CODE, PLANE, F, BF, I32, U16 = "float8_e4m3fn_x4", "uint8", "float32", "bfloat16", "int32", "uint16"
-CN, C1, C2, CL, CX, N4, S3, WIN = 64, 128, 352, 560, 752, 896, 1056, 1184
-C3, NE, N1, N2, N12, N3, WN = 512, 704, 768, 864, 1026, 1092, 1158
-D1L, D2L, D2X, D1X = CL - C1, CL + NL - C1, CX - X0 - C1, CX + NX + 2 - X0 - C1
+CN, C1, C2, CL, CX, WIN = 64, 128, 352, 560, 752, 896
+LB, C3, NE, N1, N2, N3, N4, S3, WN = 32, 544, 736, 800, 1056, 1216, 672, 1376, 1504
+HE = P + CAPP + 2
+D1L, D2L = CL - C1, CL + NL - C1
 
 
 def _pair(name, n):
@@ -22,53 +20,49 @@ def _f(dtype, **kw):
 
 
 SCRATCH = {}
-for _n, _w in (("wt", 1024), ("uu", 128), ("uab", 256), ("win", WIN), ("wn", WN), ("pool", P), ("pland", P),
+for _n, _w in (("wt", 1024), ("uu", 128), ("uab", 256), ("win", WIN + P + 2), ("wn", WN), ("pool", P), ("pland", P),
                ("left", P), ("c4", P)):
     SCRATCH.update(_pair(_n, _w))
-SCRATCH.update(_f(BF, hx=896, h2=4 * XW, hu=512, hv=8, huab=1024, he=8 * NL, hc=4 * XW, h3x=512, h4=640, hl=512,
-                  ones=128, keep=192, tmod=192, mr=256, mb=256, sb=256, spw=768))
-SCRATCH.update(_f(F, msk=192, mskx=NX, a1d=NL, sl=192, ax=NX, sx=NX, ma=416, sa=416, mc=192, sc=192, md=80, sd=80,
-                  me=192, se=192, fx=36, fy=32, mf=P, sf=P, junk=128, s1x=NX, wr=P, ysb=3 * P, spr=3 * P, cst=8, cle=48,
-                  cgt=48, msg1=14, msg3=18, land1=14, land3=18, msg2=15, land2=15))
+SCRATCH.update(_f(BF, hx=4 * (HE + 322), hu=512, hv=8, huab=1024, h4=640, ones=P, keep=192, tmod=256,
+                  rst=P, cle=768, cgt=768, cst=769, spw=WIN - C1, hold=256, geq=CAPP, nle=NL, cum=NL + 2, cw=NL, cx=NL, fr=66, nfe=CAPP, fx=CAPP, fy=CAPP))
+SCRATCH.update(_f(F, msk=192, a1d=NL, sl=NL, sx=66, sxe=CAPP, eb0=CAPP, sq=CAPP, ma=416, sa=416, mc=192,
+                  sc=192, md=80, sd=80, me=64, se=64, tr=128, tb=64, ga=P, mf=P, sf=P, junk=192, wr=P, ysb=3 * P, spr=3 * P,
+                  spx=80, msg1=18, msg3=18, land1=18, land3=18, msg2=5, land2=5))
 SMALL, _at = {}, [0]
-for _n, _w in dict(d0=30, c0=24, c1=24, e0=30, e1=30, f5=36, wg=P + 16, s3=10, cr=80, qf=1, q3=1, pw=10, pw5=10, ph=1,
-                   k64=6, jw=10, t0=10, t1=10, t2=10, xm=1, gg=18, xx=12, yy=12, gt=12, a1w=12, a2f=10, zz=12, j16=16,
-                   sg=16, nn=1, u1=6, s2p=10, thr=10, pe=4, s1p=10, da1=30, db1=30, so=30, sp=30, co=36, sh=16, th6=6,
-                   e15=1, kt=1, ka=1, k5e=1, k5n=1, d2e=1, d2n=1, da=1, at=1, a0=1, a1=1, f4=8, nr=1, nq=1, ab=12,
-                   b3w=12, g5=1, v0=5, u6=5, v1=10, v2=10, v3=10, v4=10, v5=10, v6=10, eo=30).items():
+for _n, _w in dict(d0=30, c0=18, c1=18, e0=20, e1=20, wg=P + 16, z0=24, z1=24, qf=1, q3=1, pw=10, pw5=10,
+                   k64=6, jw=10, t0=10, t1=10, t2=10, xx=6, yy=12, aw=12, nf=18, zz=24,
+                   nb=1, thr=10, s1p=10, da1=30, db1=30, so=30, sp=30, co=18, t5=1,
+                   e15=1, kt=1, k5e=1, d2e=1, da=1, a0=1, a1=1, f4=8, yz=12, nr=1, nq=1,
+                   b3w=12, g5=1, v0=5, u6=5, v1=10, v2=10, v3=10, v4=10, v5=10, v6=10, v7=10, eo=20).items():
     SMALL[_n] = (_at[0], _w)
     _at[0] += _w
 SCRATCH.update(_f(F, small=_at[0]))
 SCRATCH.update(_f(I32, qi=1, qj=1, ci=10, cj=10))
-SCRATCH.update(_f(U16, offa=6, offb=6, offp=10, offl=10, offk=10, off4=10, offs=10, offt=10))
+SCRATCH.update(_f(U16, offa=10, offb=6, offp=10, offq=10, offl=10, offk=10, off4=10, offt=10))
 for _b in range(8):
     SCRATCH["ps%d" % _b] = ("psum", [128, 512], F)
-ARR = ["an1q", "an1s", "an2q", "an2s", "an3q", "an3s", "an12q", "an12s", "am1", "am2", "am3", "apq", "aps"]
+ARR = ["an1q", "an1s", "an2q", "an2s", "an3q", "an3s", "an12q", "an12s", "am1", "am2", "am3", "am4", "apq", "aps"]
 SEMAPHORES = ["cg"] + ARR + ["sent"] + ["d%d" % i for i in range(16)] + ["cv", "cs", "ct"]
+RQ = dict(e="svsv", l="svsv", n="ssss", x="ssss", y="ssss", z="ssss", w="ssss", o="yyyy", th="s", sx="s", s2="vv", one=0)
 
 ISSUE = {
-    0: ('(0(7(9(1(3(2(4(8(:(;(5(<(=(6)D)@(>(?(@(N(K(C(B(L(I(J)I(M(H(G(R(F(P)5(Q(U)6(O(A(E)2(W(D)U)3(T)1)C)7)0)?)B'
-        ')<)=):)>)E)G)F)S)9)T)H)4(V)L)J)N*8)8)V)R);)W)M*0)K)A*4*;(S)Q)O*<)P*?*C*=*@*D*>*A*H*B*:*2*G*P*E*7*I*1*R*N'
-        '*6*L*F+9*O*3*W*Q*9+:+0*U+1*S*J+2+?+5*T+6+3*V+J+4*K+E+=+<+8*5+C+U+@+7+V+D,@+B+I+H,1+R,7+L+T*M+S,2+>+G,3,5'
-        ',9,4+M+W,:,6+A,8,;+O,E+K,<+P,F,H,A,0,C-V,I+F,J,G,=+N,L,K,N-W,>-=+Q,M,V,D,?,O,P,U-:+;,Q,B-6,R-0,W,S-1,T-;'
-        '-7-9-2-4-3-5-8-B-<-D-A.0-C->-F-?.1-@-E-G-H.2-I-J.3-K-M-N.7-O-P.4-S-R-Q.6.5.:-L-U.D.8-T.?.;.@.A.9.B.<.F.G'
-        '.>.H.I.K.J.=.C.V.W.N/0.E.U.O/3/1/2.L.T.M/9/4/5/6/:.P/7/;/8.Q/</@/=.R/A/>/?.S/D/B/C/E/F/H/G/I/K/J/N/O/P/Q'
-        '/R/L/M'),
-    1: ('(0(7(9(1(3(2(4(8(:(;(5(<(=(6)D)@(>(?(@(N(K(C(B(L(I(J(M(G(H(R(F(P)5(Q(U)6(O(A(E)2(W(D)Q)3(T)1)C)7)0)?)B)<'
-        ')=):)>)E)H)O)9)F)P)J)4*3(V)R)I)N)G)S)8)A)W(S);)M)K)L*6*7*:*>*8*;*?*9*<*C*=*5)U*B*J*@*2*D)T*L*H*1*F*A+3*I'
-        ')V*Q*K*4+4*R*O*S*M*E*T+7*W*N+0*U*P+B*V+=+6*0+2+M+;+8+N+1+<,8+:+A+@+Q+J+W+D+L*G+K+R+S+?+U+T,1+O+E+V,2,0+9'
-        ',3+G,=+C,4+H,>,@,9+P,;-M,A+>,B,?,5+F,D,C,F-N,6-4+I,E,N,<,7,G,H,M-1,:+5,I,U,J,P,O,K,Q,L-2,V-0,R,S-9,T,W-;'
-        '-3-8-:-O-=-5-6-<-P-7->-?-@-Q-A-B-R-D-E-F-V-G-J-S-I-H-U.1-T-C-L.;-K-W.2.6.7.0.8.3.9.=.5.>.?.@.B.4.A.:.M.N'
-        '.E.O.<.L.F.R.P.Q.C.K.D/0.S.T.U/1.G.V/2.W.H/3/7/4.I/8/5/6.J/;/9/:/</=/?/>/@/B/A/E/F/G/H/I/C/D'),
-    3: ('(0(7(9(1(3(2(4(8(:(;(5(<(=(6)D)@(>(?(@(N(K(C(B(L(I(J)F(M(H(G(R(F(P)5(Q(U)6(O(A(E)2(W(D)R)3(T)1)C)7)0)?)B'
-        ')<)=):)>)E)I)P)9)G)Q)K)4*=(V)S)J)O)H)T)8)A*9*0);)N(S)L)U*@)M)V*4*A*2*D*H*B*E*I*C*3*F*M*G*?*7*L*T)W*J*N*<'
-        '*V*R*6*P*1+4*S*;+>*U*K+3*8*>+?+1+5+6*W+7*O+B+0+:+8+;+2+9+M+H+A*:+=,0+F*5+C,1+<+G,G+E+L+K,7+U,=+O+W*Q+V,8'
-        ',9+J,;,:,?,6+P,2,@,<+D,5,A+R,>,L,4+N,C,B+S,M,O,H,Q,R,P+I.7,3,S,J,T+Q,D,N,V.8-0,U+T,E,W-F-8,K,F-1-2-7,I-C'
-        '+@-3-?-4-:-9-5-;-6-D-@-B-<-=-K->-A-M-E-J-L.9-O-G-H-N.:-I-P-Q-R.;-S-T.<-V-W.0.@.1.4.=.3.2.?.C.>-U.6.M.5.A'
-        '.D.H.I.B.J.K.E.O.G.P.Q.R.T.S.F/5/9.L/:.W/;/</0.N/8/?/=/>.U.V/7/E/@/A/1/6/F/B/C/G/2/L/D/H/3/I/M/J/4/K/N/P'
-        '/O/Q/R/T/S/U/W/V02030405060001'),
+    0: '(0(@(4(1(2(3(8(5(6(?(9(<(7(;)H)O(S(A(I(=(K(N(M(E(O(H)M*4)N(J)K)@)>*5(L(B)P(R)I(C)R(:)B*1)J)A)E(Q)Q)W)G*0(P(D)F*2)C)0)S(>(U)D*3)L(W(G)6(T*6)5)7(V(F)1-U)2)?)3)=)4-T*7):*:)T)9*8*9)<)8*;*B*>*<*F*=*R*E*D*Q)U*O)V*?*P*C*K*A*H+4*G+3*I*S*T+2*J*U+1*@*L+Q+U+P+7+5*M,1+6+8+T*N*V+L+N,4*W+M+:+S+O+9+W+0+E,B+;,6+=+B+F+<,7,@+>,9+C,5,C+?,:+A+D+@,F,3+G,E+R,H,8,D+H,I+V,J,A,G,0,;+I,K,Q,T,S,U,<,L,R,2+K,V,P,M-;,O+J-<,N,=,?,>,W-4-0-3-=-2->-1-?-8-5.0-A.2-@-6.3-C.7.1-B.4-9.6.5-7-V-E-W-:-D-G-F-H-I-J-L-K-M);-N-Q-P-O.?.8.A.B-S.9.>.;.C.@.:-R.=.<.J.L.N.W.K.M.E.F.G/0.P/7.R/4/5/1.Q.D/3.T/2.U/6.V/9.O.S/8/?/@/:/A/>/;.H.I/</=/C/B/D/F/E/G/M/I/H/O/N/L/P/J/K',
+    1: '(8(0(5(1(2(3(4(6(=(?(9)I(7(@(<(Q(A(N(J(>(H(K(D)@(I(L(M)Q)U);)?)T(G)S(R)=)J(;(B(O)L(P)M)F)V)D)R(:)C)9)>)G(C)5)4(V(F(S(T(W)6(U(E)0)1-H)8)3)<)A)2-G*0)O)P)W*2*1)7*4*3*:*6*H*5*;*<*>)N*I*7)B*F)E)H*G*B*=*9*?*R*J*@*S*K*A*L*Q*8*P*C+H*V+L*T+D*W*U*M+P+J*D+N*N+1+G*E+C+0+S+<*O+R,7+2,<+E+K+4+I+=+3+M+7+F,6+U+8+:+6+;+5+V+9+>,0,=,:,8+?,1,>,;,?,5+Q+T+@,@,H,2,F+W,9,A+A,3,M+O,I,E,J,B,G+B-0,4,D,K,C,L,Q,W,P,O)K-1,T,N-K-2-7-N-3,R-5-8-4,U-6,S-O-R-9-L-P,V-I-M-;-J-:-Q-<-=):-?->-@-A-D-C-B.2-V.4.6-F-T.1.0.3.5-W-U-E-S.:.;.>.?.=.J.A.K.@.O.Q.P.L.E.R.D.N.M.C.G.8.T.9.H.I.S.<.B.F.7/2.U/3/4.V/1.W/0/5/6/7/9/8/:/A/@/;/</C/?/B/=/>',
+    2: '(8(0(4(1(2(3(5(6(;(9(=)G(7(<(:)I(R(A)@(J):(H(M(D(L(G(N(@(K(I(B)J(?(P)K(>)L)H)U)=(Q)A)E(O)B)F)D)M)>)C(C)8)S)Q(U)T)V)6)?(W)R(F(S)4(T)5(V(E)0)1-H)<)3);-G)O)W)N)P*2*0*1)7*3*:*6*4*>*5*I*;*<*H)2*G*7*F*=*?*B*9*@*J*S*K*R*A*P+I*Q*L*8*C+H*V+L*T*D*U*W+D*E*M+M+E+J*N+C+1+P+0+S*O+<+Q+F+2,0+T,7+4+=,:+:+6,1+3,;+8+;+5+7+U+9+>,H,5+V,=,8+N+?,>+W,?,6,9,I+G,2+@,@+K+R,J,F,3,A,<,G+A,K+O,E,B-0+B,D,W,M,4,L,C,P,O,Q-1,T-7-N-2,N-K-3-I-M-5,R-L-4,U-6-J-P-8-Q,V-O-R-9,S-;-:-<-=)9-?->-@-A-D-C-B.1-T.5-F-V.3.6-S.0.2-U.4-W-E.:.;.8.9.>.?.=.J.A.K.@.<.P.O.Q.L.D.R.C.N.M.B.T.H.F.S.G.E.I.U/3.7/1.V/2/4.W/0/5/6/7/9/8/:/;/</C/@/A/?/B/=/>',
+    3: '(5(=(0(1(2(3(:(6(8(@(4(Q(7(9(?(A(H(R(;(L(<(D(N(I(J(K)=(>)D*2)V)K*4(M)L(G)A)C)I)O*3)J)>*1)B(B)Q*9):)P(P)?*0)E(C)W)N(O(T(W)9)4(F)6*7*8)F(V*6)H(S*5)5(U(E)0.3)1)<.2)3)2*:)G*=)8*;*<);)7*>*E*A)U*?*I*@*T*F)M*R)R*G*S*B)S*J*H*U*Q*D*K+6*M+4*L)T+5+S*V+9*C+T+3+W*N*W+:,0+7*O,3+8)@+<+N*P+;+O+0,6+U+P,1+1+=,4+Q+G,D+2+@,<+?+B,8+A,B+>+H+C,9,C+D,E,@+F,H,5+R+E,7,A+I,:,J,I,L,F,K+V+J,M,;-2,O,G,Q-3,P+K,W,N-0,2-7-5-1+M,R-B,V-A+L,S-4,U-C-6,T-:-9-;-E,=->.4-8.8,?.7,>-D-<-F-?.;-G-I.<.6-H.:-=.5.9-@.=-K-L-M-J-N-O-P-R-Q-S-T-W-V-U.F.?.I.1.>.D.@.K.G.A.J.0.E.V.C.U.B.T/9/;/0/=/</:.W/A/B.O/>/3/D/4/@/?/2/7.Q/F.P/6/C/8.M/E/1/5.N/M/G/L.L/N/H/K.R/I.H.S/J/O/P/Q/S/R/T0203/U0401/V05/W00',
 }
-ISSUE[2] = ISSUE[1]
+ISSUE = {
+    0: '(4(?(0(;(1(2(5(7(3(6(8(=)H(:)I)O(@(<)9(A)K)@(J(D)J)M(L(M(N(B(H(K*3);)N(R(G(I):)>(P)Q(C*0)R(F*4)A)W*2)P(>(E(9)L(S.6)8(Q)S*1*5.7)=(O)?)F)G)0)C)4)1(U(T)<(W)3(V)D)T*8*9*7*:*<)5*C*=)7*;)6*B*O*>*D*P)V*R*F*?+1*Q*E+2+4*H*K+3*I*A*T)2)E*J*U*@*G)U*6*L*S+5+Q+U*V+R*M+7+6+N*W+P*N,1+T+8+V+M+E+O,4+0+:,2+9,0,B+F+L+S+;+W,5,:,H,7,6,F+=+?+<+@+B+A,J+C+>,8,D,I+D,@,C,A,3+G,9,;,E,K,R,G+H,L,U,?,Q,T,S+I-8-6,M-;-7,P-F+K,V-E+J,N,O,W-4,>,=-3-5,<-2-0-G->-<-=-1-H-I-?-9-:-B-@-K-N.=-M-J-L.<-A.@.A-C.9-O.;.?-D.>-P.B)B.:-Q-R-S-U-V-T.0-W.1.2.3.D.L.C.J.K.N.E.I.5.F.4.8.U.O.G.H.V/0.W/:.P/9/;/=/</C/3/2/A/4/?/@/>/E/7/8/D/1/5/L/6/M/F/J/K/G/B.R.S/H.Q/I/O/N/P.T/Q/R/S.M/U/T0301000402/V/W',
+    1: '(9(4(0(1)H(2(6(>(3(;(8(=(:(5)?(?(P(F(L)8(J(@(H(I(B(K(E(G)D(N)I(7)K(Q(<(A)J)7(D);(C)S)L)G(M-O)E)9-P)<(O)>)A(V)B)=(W)R)U)P):(S)@)2)1(T)6)0)4(R(U*0)V*1)W)5*2)3*4*5*9*E*;*F*3)Q)M)N*H*:*G*=*O*6*P*<*R*>*Q)F)O*?)C*A*@*8*J*S*K*7*I*B+I+G+K*L*T*U+H*C+F+D*M+O+B*V+L+;*D+J+E+R*W+0+P+T*N+N+1,6+<+M+C+U+7+2+9+6+3,4+5,7,<+8+4,0,1,:+W+S,=,9+=,5,E+:,>,?+V+>,8,N-@,Q,2,R,W+Q,@,G,I,S,H-8,F+?,3,O,;,A,D-9+A,J+@,B,C,K,V,P-:-2-0-1,L-<-;,U-3,T-5,M-T-=-?->)T-4-6-B-A-7-C-F-E.0-D-W-R-V-H-G.3.2-S-I-U.1-J-K-L.5.:.;.<.6-N.7-M.F-Q.4.8.G.9.I.R.V.U.T.S.C.H.=/2/0/1.W.L.A/3.B.M/6.>/4.K/5.Q.P.O.J/7/>.@.N/=/8/</;/9/:.D/?/@.E/A/B/C/D.?/J/E/F/I/M/L/K/G/H',
+    2: '(;(4(0(1(2(7(6(3(8)G(:(5(?(P)?(F(J);(H(E(L(G(B(K)E(I)8(@)L)F(=)I(N(9(>)A)7(Q(A)6)C(D)<)D(C(<-O)9(M-P)Q)J(O)P)>)H)B(V)=)K(W(T)T)R):(R(U)0)1)@)2(S)N)M)O*1*0)V)W*5)5*<*4)4*2)3*9*H*3*;*G*E*=*6*R*F*:*Q*O*?*A*P*@*8*>*I*7*J*B*K*S+G+K*U+I+M*C*L*T*V+H+D*D+L+O+B*M+Q*W+C+0+E+R+;+P*N+1,6+T+S+U+<+3+2+5+F+6,5+7+4+8+9+W,<+J+:,7+=+V,>,8,=,9,0+>,E,4,:,I,?,;,F,1,U,W,G,N+?,P+N,@,H-8+A,J,2,O+@,3,T,A,Q,D-9,K,B,C-:-0-1,L,S,R-@-2-<-;-5,V,M-U-R-3-T-V-=-?->)U)S-6-4-B-A-7-C-F-D-E.2-S.0-G-H-W.1.3-I-J-K-L.5.:.7.<.=.;.6-N.4.8-M.9.F-Q.A.G.H.I.R.?.S.U.V.T.L.K/1.M/0/2.W.Q.@.O/6.P/5.J/>.N/</7/=/4/3/;/8.C.B.D/9/:/@.E/?/A/B/C/D.>/K/E/F/J/M/I/L/G/H',
+    3: '(4)H(0(1(7(2(5(3(6(8*2(=(:(;(<)?)T*0)I*8(?(L(F(I)7(J(P(K)>(H)G(B)U(E*1(@);(G(9)F(>)E)6(N)O(A)M)B(D)J(C)<(Q)8)P.;*4*3)A(O(M.<)C)V)L)N)=(V)D)9(U(W(T)@)3)2):(S)0)1(R*7*6*9)S*:*;*<*=*D)4*>)5*E*?*S*F*Q*@)Q)W*5*H*G*P*R+5*A*I+3*T*J+2*K+4*L)R)K*C*U+8*V*B+6+R+V+S*M+W+9*W+7,2*N+T+:+M+;+0,0+O+N*O,3,5+<+F+P+1,7+>,B+=,4+B+?+C,@+D+@+A,C,?,A+G+Q,;,6,G+E+U+H,8,I,H,K,D+I,:,1-1,<,9,J,F,L,N,E,V-2+J,M,P,O-6+K-:-J-A-0-K,W+L-=,Q-9,=,>-?-8-4-@-<-L,R,U-3-5-M,S,T-B-C-7-N-;-D->-G-S-R.@-P-Q-O.B-E.C.A-H-T.G-F.>.F-I.D-U.?.E.0-W-V.2.1.3.5.4.6.7.8.I.Q.H.S.P.J.:.K.T.W.9.=.L/6/9/:/;/H/8.N/F.O/G.U/I/D/E/>.V/0/=/</J/K/L/B/7/M/A/@/P/?00/C/Q/W.M/V/R/O01/N/3/S/1/4/2.R/T/U03/5020405060709080>0=0@0<0?0:0;',
+}
+ISSUE = {
+    0: '(5(;(0(1(2)M(4(3(7(6(?(8(>(:(@(N(L*4(<(I(H)O)I(G(D)K)N(R(J(M*5(K)W)A*1*3(A)J(B)P(P):)S)=(C(S(O(F)H(E)E(9)L.7(Q)C)0.6)B)@)R)1*0)?)F)G)8)2);)3(V)<)5)D(U(T)>)9)4)T(W*:*7*8*9*>)7*E*;)6*B(=*P*<*R*=*C*D*Q)V*F*O+2*?+4*G+3*S*H+1*I*K)Q*A*T*J*6)U+S+7*@*U+5+Q+W*L+U+8*V+6*M+R+9+L+N*W+M+:+P*N+E,3,1+T+O+;,6+0,4+F,7+=+C+<,B+?+B+A+@+>,0,5,C,A,@,:+D,F+G,9,H,E,Q+V+H,8,T,J,I,D,;,G,S,2,U+I,K,R+K-0+J,V,L-;,=-4,W-5-8,?-6,>,<-7-3-F,M,P-E-<,O-G,N-=-1-I-H->-2-N-B-L-J-:.;-M-K-9*2.<.=-?.?-@-O.@-C.>-A.9.B-P.A-D.:-Q-R-S-U-V-T.0-W.1.2.3.D.M.F.J.K.E.5.C.H.4.G.U.8.V/0/9/:/=/</;.L.W/A/?/@/>/2.I/C.R/3/E.P.Q/4/D/6/7/8/1/F/K/5/L/G/M.O/B/J/H.S.N/I/N/O.T/P/Q/R/S/U/T0403010002/V/W',
+    1: '(;(4(0(1(2(9(5(3(7(6(8(=)H(>(?(F(L(@(J(G(H)8(B(P(K(E(I)G)6(:)K)I(<)9(N(A)J)P)?)S)F)L(D)7)U)Q)T(C)<);(Q-P(O(M-O)A)B)=(V)C(W)D)E)4):(U)1(T)@(R)2)N(S)V*1)W*0*2*9)5*5)>)3)M*3*F*:*G*4*;*=*<)0)O*H*E*P*6*Q*>*?*I*R*@*O*J)R*8*A*U*K*7+H*S+L+G*B+K*V*L*T*C+I+D+M*W*M+O+B+0+F*D+;+C+E+P+J+Q+1+R+T*N,0+<+3+9+2+6+N,6+4+7+S,5+5+8,:,4+U+:,7+=,<+V,H,>,8+>+W,9,=,;,I,E,F,1+?,?,G+A,J,L,T,W+@,V,O,Q,@,K-9,A,D-8-0-1,B,C-:,3,M,2,U,R-@-5-;-A-<-2-?,S,N-T,P-U->-6-=-3.0-R-B.1-7-S-4-W-C.3-F-V.2-D-E-G-H-I-J-K-L.5.=.7.>.<.6.;.:-N.4.8-M.9-Q.F.G.H.I.V.A.R.B.U.S.T.K.L/1.M/0/2.W/6.Q/3.P/5.O.J/>.N/=/7.@/</4/;/8.C.D.?/9/:/@.E/?/A/B/C/D/J/E/F/K/I/M/L/G/H',
+    2: '(5(;(0(1(2(7(4(3(6(=)F(8(9)H(P(?(:(@)9)?(<(L(B)7(J(G(F(E(H(K(I)6(N)J)Q)I)8(A);(D(Q)T(O(C)B-P)C)<(M)=-O)@)K)P)>(V)E(W):)2(T)1)D)0)U(R(S)M)L)4(U)V)W*0*1*2*9)5*3)3*:*4*H*;*E*5*=*<*G*F*R*6*>*O*I*?*Q*@*P(>*A)N*8*J*U*K*7*S+G)R)O+K+H*B+L*V*L*T+O*C+C+0+I*W*M+F+D+B*D+;+P+M+R+1+E+S*N+<+3+4+2+9+Q,6+8+7+5+T+6,5+J,0+:,:+=,;,<+W+N,9+>,>+U,=+V,L,4,H,8,1,7+?,?,G,I+@,M,F+A,E,@,P-9,W,V,3,U,O-8,2,A,D,J,K-:,B,C-0-1-A-@-<)G-;,Q,T,R-?,N-5-=-2->,S)S)A-T-R-U-6-V-B-3-S.2-7.0-C.1-4-W.3-F-D-E-G-H-I-J-K-L.5.:.7.<.=.;.6-N.4.9-M.8-Q.F.G.H.I.T.C.S.A.V.B.R.U.D.@.K/4.L.W.J/0.E/1/2.N.O.P/5.M/;/6.Q/3/</=/7/>/8/9/:/@/?/A/B/C/D.?.>/E/K/F/J/L/M/I/G/H',
+    3: '(=(4(0*2(1(7(2(5(3(6(8(;)F(:(>)?(?(P(L(F(@(J(K(H(G(I(B(<(E*1)9)>(N*6)M)G)7);*8)N(Q)U)T)8(A)J)H(D)@)E(C)<.;(O)L)K*5)A)B.<*0(M)W)P*3)V)=(V(W*7)4)6(R):(U)1(T(S)2*9*<*;*:*=*D)3*@)5*?*F*>*4)I)0*H*E*Q*P*A*S*R*G*I+3*J*T+2*K+5*L*C+4(9*U)O*B+Q+8)R)C*V+6+U+R)S+V*M+9*W,1)Q+7*N,2+T+:,0+O+0+M+;+S*O+F+N+W+P+<,4,5,7+1,C+G,;+>+=+C+@+A+B+?,?,H+D,B,A,6,3,@,G,:+E+H,F,I,9,K-1,E+I,8-6,D,J,M,N,L-0-2,<+J,P,O,W,V+K-7-;-=-9-8->-A-?-4+L,Q-J,=-K,R,U-3-5-L,S,T-B-C-R)D,>-N-D-M-<-:-@-G-Q-S.@-P-O.B-E.D.A-H.E-T-F.>.F-I.C-U.?.G.0-W-V.2.1.3.5.4.6.7.8.I.P.K.N.R.V.Q.J.W.:.H.S.M.9.L.=/6/3/1/9/8/7/:/;/D.O/F/4/G/E/H/I/?/O/0/=/</J/K/L/A/M/C/@/P/>/W/B/Q01/V/R/N00.T/2/S/T/5/U030204050607.U0<08090>0=0@0?0:0;',
+}
 ORDER = {r: [(ord(s[i]) - 40) * 40 + ord(s[i + 1]) - 48 for i in range(0, len(s), 2)] for r, s in ISSUE.items()}
 
 
@@ -202,8 +196,8 @@ def rank_program(g, core, T, topo):
     def fill(o, c):
         op("v", lambda: g.vector.memset(ap(o), c), [], [o])
 
-    def scan(o, a, b, op0=A.mult, op1=A.add):
-        op("v", lambda: g.vector.tensor_tensor_scan(ap(o), ap(a), ap(b), 0.0, op0, op1), [a, b], [o])
+    def scan(o, a, b, op0=A.mult, op1=A.add, first=0.0):
+        op("v", lambda: g.vector.tensor_tensor_scan(ap(o), ap(a), ap(b), first, op0, op1), [a, b], [o])
 
     def iota(o, pattern, base=0, cm=0):
         if SCRATCH[o[0]][2] == I32:
@@ -223,8 +217,8 @@ def rank_program(g, core, T, topo):
         o = PS(bank, 0, w)
         op("t", lambda: g.tensor.matmul_mx(ap(o), ap(rd[0]), ap(rd[1]), ap(rd[2]), ap(rd[3]), start, stop), rd, [o])
 
-    def lefts(banks, mv, ma, w, which=range(4)):
-        for t in which:
+    def lefts(banks, mv, ma, w):
+        for t in range(4):
             mm(banks[t], "wt", 128 * t, mv, ma, w, True, False)
 
     def rights(banks, mv, ma, w):
@@ -232,17 +226,24 @@ def rank_program(g, core, T, topo):
             mm(banks[t], "wt", 512 + 128 * t, mv, ma, w, False, True)
 
     def relu(q, h, ha, t, bank, a, b):
-        act(R(h, 4 * ha + t, 4 * (ha + b - a), 4), PS(bank, a, b), 0.05, None, ACT.Relu)
+        o = R(h, 4 * ha + t, 4 * (ha + b - a), 4)
+        if q == "s":
+            act(o, PS(bank, a, b), 0.05, None, ACT.Relu)
+        else:
+            ts(o, PS(bank, a, b), 0.05, A.mult, 0.0, A.max)
 
-    def pick(dst, da, src, sa, sb, off, w=P):
-        o, i, l = R(dst + "q", da, da + w), R(src + "q", sa, sb), R(off, 0, w // 16)
+    def turn(o, i):
+        op("v", lambda: g.vector.transpose(ap(o), ap(i)), [i], [o])
+
+    def pick(dst, da, src, sa, sb, off, w=P, k=0):
+        o, i, l = R(dst + "q", da, da + w), R(src + "q", sa, sb), R(off, k, k + w // 16)
         op("v", lambda: g.vector.tensor_copy(ap(o).bitcast(dt.uint32), ap(i).bitcast(dt.uint32).indirect(ap(l))),
            [i, l], [o])
         o2, i2 = R(dst + "s", da, da + w), R(src + "s", sa, sb)
         op("s", lambda: g.scalar.activation(ap(o2), ap(i2).indirect(ap(l)), ACT.Copy), [i2, l], [o2])
 
-    def gather(q, o, win, off):
-        l = R(off)
+    def gather(q, o, win, off, k=10, a=0):
+        l = R(off, a, k)
         if q == "v":
             op("v", lambda: g.vector.tensor_copy(ap(o), ap(win).indirect(ap(l))), [win, l], [o])
         else:
@@ -262,326 +263,364 @@ def rank_program(g, core, T, topo):
     d = shift[1]
     last = (rank + 1) // n
     jw = "jw" if d else "pw"
-    x1 = 2 * last
-    x0 = 2 - x1
-    PE = P - x1
+    xs = NL - 2 * last
+    nx = P - xs
+    o12 = 2 * last
+    D1X = CX + CAPP - xs - C1
+    ea = 5 if last else 6
+    eb = 5 if last or d else 6
     LO, HI = (0, 1, 2, 3), (4, 5, 6, 7)
 
-    def cells(k, buf, a, w, at, s, early=0, cut=0):
+    def cells(k, a, w, at, s):
         for x in "qs":
-            b = at + shift[k] - early
-            send(-k, R(buf + x, a - early, a + w - cut), R("win" + x, b, at + shift[k] + w - cut), s + x)
+            send(-k, R("wn" + x, a, a + w), R("win" + x, at, at + w), s + x)
 
-    for k, buf, a, w, s in ((1, "wn", NE - last, P, "an1"), (2, "wn", N2 - last, P + last, "an2"),
-                            (3, "wn", N3, NX, "an3"), (1, "wn", N12 - 2, NX + 2, "an12")):
-        lands(k, R(buf + "q", a, a + w), s + "q")
-        lands(k, R(buf + "s", a, a + w), s + "s")
+    for k, a, w, s in ((1, NE, P, "an1"), (2, N2, P, "an2"), (3, N3, nx, "an3"), (1, N1 + NL, nx, "an12")):
+        lands(k, R("wnq", a, a + w), s + "q")
+        lands(k, R("wns", a, a + w), s + "s")
     lands(-1, R("land1"), "am1")
     lands(-1, R("land3"), "am3")
     lands(1, R("land2"), "am2")
+    lands(1, R("offl"), "am4")
     lands(1, R("plandq"), "apq")
     lands(1, R("plands"), "aps")
 
     dma("y", ap(R("hx", 0, 4 * P)), T.x[:, :], [], [R("hx", 0, 4 * P)])
     dma("y", ap(R("hv")), T.u[:, 0:8], [], [R("hv")])
-    dma("y", ap(R("wts")), T.ws[:, :], [], [R("wts")])
     dma("y", view(R("wtq")), T.wc[:, :], [], [R("wtq")])
+    dma("y", ap(R("wts")), T.ws[:, :], [], [R("wts")])
 
     iota(R("qi"), [[0, 1]], 0, 1)
     iota(R("t0"), [[16, 10]])
-    iota(R("tmod"), [[0, 12], [1, 16]])
-    iota(R("j16"), [[1, 16]])
-    iota(R("cst"), [[1, 8]])
-    fill(R("small", 0, SMALL["wg"][0] + 16), 0.0)
+    iota(R("tmod"), [[0, 16], [1, 16]])
+    fill(R("small", 0, SMALL["z0"][0]), 0.0)
     ts(R("qj"), R("qi"), 15, A.bitwise_and)
-    fill(R("small", SMALL["s3"][0], SMALL["qf"][0]), -BIG)
+    fill(R("small", SMALL["z0"][0], SMALL["qf"][0]), -BIG)
     cp(R("qf"), R("qj"))
     fill(R("ones"), 1.0)
     ts(R("pw"), R("t0"), R("qf"), A.add)
-    fill(R("h3x", 0, 4 * (128 - NX)), 0.0)
+    fill(R("cum", 0, 2), 0.0)
+    fill(R("eb0"), BIG)
 
+    if d:
+        fill(R("hx", 4 * P, 4 * P + 8), 0.0)
+        quant("win", WIN, P + 2, "hx")
     quant("win", CN, P, "hx")
-    cells(1, "wn", NE, P, CN, "an1", d, d)
     quant("win", CN + P, 128, "hx")
-    cells(2, "wn", N2, P, C1, "an2", int((rank - 2) % n == n - 1))
-    cp(R("hx", 4 * P, 4 * (P + CAPP)), R("hx", 0, 4 * CAPP), "s")
+    cells(1, NE, P, WIN + 1 if d else CN, "an1")
+    cells(2, N2, P, C1 + shift[2], "an2")
     for t in range(4):
-        ts(R("huab", t, 512, 4), R("ones"), R("hv", t, t + 1), A.mult)
-        act(R("huab", 512 + t, 1024, 4), R("ones"), 0.0, R("hv", 4 + t, 5 + t))
-    ts(R("msk"), R("tmod"), R("qf"), A.is_equal)
+        ts(R("huab", t, 512, 4), R("ones", 0, 128), R("hv", t, t + 1), A.mult)
+        act(R("huab", 512 + t, 1024, 4), R("ones", 0, 128), 0.0, R("hv", 4 + t, 5 + t))
+    ts(R("msk"), R("tmod", 0, 192), R("qf"), A.is_equal)
     quant("uab", 0, 256, "huab")
-    ts(R("keep"), R("tmod"), 0.0, A.not_equal)
-    cp(R("h2", 0, 8), R("hx", 4 * P - 8, 4 * P), "s")
-    cp(R("h2", 4 * NX, 4 * NX + 8), R("hx", 4 * CAPP, 4 * CAPP + 8), "s")
-    cp(R("h2", 4 * NX + 8, 4 * XW), R("hx", 4 * P - 8, 4 * (P + CAPP)), "s")
+    ts(R("keep"), R("tmod", 0, 192), 0.0, A.not_equal)
+    cp(R("hx", 4 * (HE - 2), 4 * HE), R("hx", 4 * CAPP, 4 * CAPP + 8), "s")
     mm(7, "uab", 0, "win", C1, P)
-    lefts(LO, "win", CN, 128)
-    quant("wn", 0, P, "hx", CAPP)
+    lefts(LO, "win", CN, P)
     mask("ma", 0, PS(7, 0, P), 0)
+    turn(R("tr", 0, 64), PS(7, NL, P))
+    cp(R("msg1", 14, 16), R("tr", 0, 64, 32), "s")
     cp(R("a1d"), PS(7, 0, NL), "s")
-    cp(R("hl", 0, 128), R("hx", 512, 4 * P), "s")
-    cp(R("hl", 128, 512), R("hx", 4 * CAPP, 4 * P), "s")
-    quant("wn", 384, 128, "hl")
-    lefts(HI, "wn", 384, 128)
-    act(R("ph"), R("qf"), 1.0, 0.5)
-    act(R("sh"), R("j16"), -1.0, R("qf"), ACT.Sign)
-    act(R("sg"), R("j16"), -1.0, R("ph"), ACT.Sign)
-    act(R("pw5"), R("pw"), 1.0 / 512)
-    act(R("q3"), R("qf"), 3.0)
-    quant("wn", 256, 128, "hx", CAPP)
+    lefts(HI, "win", C1, 128)
+    quant("win", C2 - V0, 128, "hx", V0)
+    quant("wn", LB - V0, 128, "hx", V0)
+    quant("wn", LB + NL, 128, "hx")
+    if not RQ["one"]:
+        quant("wn", C3 - 128, 128, "hx")
     squeeze("sa", "ma", 0, P)
-    fill(R("c0", 2, 24, 3), 1.0)
-    fill(R("e0", 1, 30, 3), float(S3 - V0 - N4))
-    ts(R("mskx"), R("msk", X0 % 16, X0 % 16 + NX), float(D2X - D1X), A.mult)
+    ts(R("hold"), R("tmod"), R("qf"), A.is_le, 1024.0, A.mult)
+    ts(R("geq"), R("tmod", 0, CAPP), R("qf"), A.not_equal, -BIG, A.mult)
+    act(R("rst"), R("keep", 0, P), 2 * BIG, -BIG)
+    act(R("pw5"), R("pw"), 1.0, 512.0)
+    act(R("cst", 0, 1), R("qf"), 0.0)
+    for i in range(3):
+        ts(R("cle", 256 * i, 256 * i + 256), R("tmod"), R("qf"), A.is_le, 256.0 ** i, A.mult)
+        act(R("cgt", 256 * i, 256 * i + 256), R("hold"), -256.0 ** i / 1024, 256.0 ** i)
+    fill(R("c0", 2, 18, 3), 1.0)
+    fill(R("e0", 1, 20, 2), float(S3 - V0 - N4))
     if d:
         ts(R("t1"), R("pw"), P - 1.5, A.is_gt, -float(P), A.mult)
         act(R("jw"), R("pw"), 1.0, 1.0)
         tt(R("jw"), R("jw"), R("t1"), A.add)
     if d or last:
-        ts(R("xm"), R("pw", 5, 6), X0 - 0.5, A.is_gt)
-    ts(R("sh"), R("sh"), 0.75, A.mult, 0.75, A.add)
-    fill(R("db1"), 0.5)
-    ts(R("t2"), R(jw), X0 - 0.5, A.is_gt, float(N12 - X0 - N1), A.mult)
-    ts(R("sh"), R("sh"), 1.0, A.min)
-    for a, b, c in ((0, D1L, 0.0), (D1L, D2L, 1.0), (D2L, CX + NX - C1, 2.0), (CX + NX - C1, 768, 1.0)):
-        fill(R("spw", a, b), c)
+        fill(R("db1"), 256.0)
+        cp(R("db1", 2, 30, 3), R("pw"), "s")
+    if last:
+        ts(R("t2"), R("pw"), NL - 1.5, A.is_gt, float(o12), A.mult)
+        act(R("da1", 1, 30, 3), R("t2"), 1.0, float(N1 - C3))
+        act(R("da1", 0, 30, 3), R("t2"), -1.0, float(N2 - N1))
+    else:
+        fill(R("da1"), float(N2 - N1))
+    for a, b, c in ((0, D1L, 0.0), (D1L, D2L, 1.0), (D2L, CX + CAPP - C1, 2.0), (CX + CAPP - C1, WIN - C1, 1.0)):
+        act(R("spw", a, b), R("huab", 0, b - a), 0.0, c)
     cp(R("msg1", 0, 10), W("sa", 0, 10), "s")
     for a in (0, 6):
-        cp(R("a1w", a, a + 6), W("sa", 0, 6), "s")
+        cp(R("aw", a, a + 6), W("sa", 0, 6), "s")
     act(R("k64"), R("pw", 0, 6), -1.0, float(CAPP))
-    cp(R("c1", 8, 24, 3), R("pw", 0, 6), "s")
-    act(R("pe"), R("pw", 6, 10), 1.0, float(D1X))
-    if d:
-        act(R("g5"), R("xm"), -BIG)
-    if last:
+    cp(R("c1", 2, 18, 3), R("pw", 0, 6), "s")
+    act(R("eb0", 0, CAPP, 16), R("pw", 6, 10), -1.0 / nx, -D1X / nx)
+    cp(R("e1", 1, 8, 2), R("pw", 6, 10), "s")
+    cp(R("e1", 9, 20, 2), R("pw", 0, 6), "s")
+    if d or last:
         ts(R("e15"), R("qf"), 15.0, A.is_equal)
-        act(R("kt"), R("e15"), float(CAPP - NL))
-        act(R("ka"), R("e15"), float(NL - CAPP), R("k64", 5, 6))
-        act(R("da"), R("xm"), float(D1X - D1L), float(D1L))
-        act(R("k5e"), R("e15"), -float(D2L + D1X))
-        act(R("k5n"), R("xm"), float(D1L - D1X), -float(D1L + D2L))
-        act(R("k5n"), R("e15"), float(D2L + D1X), R("k5n"))
-        act(R("d2e"), R("e15"), float(D2L))
-        act(R("d2n"), R("e15"), -float(D2L), float(D2L))
-    act(R("cle", 0, 48, 3), R("sg"), 1.0, None, ACT.Relu)
-    act(R("cgt", 0, 48, 3), R("sg"), -1.0, None, ACT.Relu)
-    for i in (1, 2):
-        act(R("cle", i, 48, 3), R("sh"), 256.0 ** i)
-        act(R("cgt", i, 48, 3), R("sh"), -256.0 ** i, 256.0 ** i)
-    act(R("da1", 0, 30, 3), R("t2"), -1.0, float(N2 - N1))
-    act(R("da1", 1, 30, 3), R("t2"), 1.0, float(N1 - C3))
-    cp(R("da1", 2, 30, 3), R(jw), "s")
-    act(R("db1", 2, 30, 3), R("pw"), 1.0 / 512)
-
-    rights(LO, "wn", NE, 128)
-    for t in range(4):
-        relu("s", "h2", 2, t, t, 0, CAPP)
-    for t in range(4):
-        relu("s", "he", 0, t, t, CAPP, 128)
-    quant("win", C2, XW, "h2")
-    mm(0, "uab", 128, "wn", NE, PE)
-    tt(R("sl", 0, NL - x1), PS(0, CAPP, PE), R("a1d", 0, NL - x1), A.add)
-    mask("ma", 256, PS(0, CAPP + d, PE), 0)
     if d:
-        mask("ma", 415, PS(0, CAPP, CAPP + 1), 15)
-    mask("me", 128, PS(0, d, CAPP + d), 0)
-    squeeze("sa", "ma", 256, 336)
-    cells(1, "wn", N12 - 2, NX + 2, C2 - 2, "an12")
-
-    mm(1, "uab", 128, "wn", N2 - x1, P + x1)
-    rights(HI, "wn", N2 - 32, 128)
-    mm(2, "uab", 0, "win", C2, 128)
-    mm(3, "uab", 128, "win", C2, 128)
-    tt(R("sl", NL, 2 * NL), PS(1, x1, NL + x1), R("a1d"), A.add)
+        act(R("g5"), R("e15"), -BIG)
     if last:
-        tt(R("sl", X0, NL), PS(1, 0, 2), R("a1d", X0, NL), A.add)
-    tt(R("mr", NL, 2 * NL), R("sl", NL, 2 * NL), R("sl", 0, NL), A.is_gt)
+        fill(R("sl", NL - 1, NL), BIG)
+        act(R("kt"), R("e15"), float(CAPP - NL))
+        act(R("da"), R("e15"), (D1X - D1L) / 2.0, D1L / 2.0)
+        act(R("k5e"), R("e15"), -(D1X + D2L) / 2.0)
+        act(R("d2e"), R("e15"), (D2L - D1X) / 2.0)
+        ts(R("md", 0, 15), R("msk", 0, 15), -BIG, A.mult)
+    cp(R("da1", 2, 30, 3), R(jw), "s")
+
+    rights(LO, "wn", NE, P)
     for t in range(4):
-        relu("s", "he", CAPP, t, HI[t], 0, 128)
-    scan(R("mr", 0, NL), R("ones", 0, NL), R("mr", NL, 2 * NL), A.add, A.subtract)
-    mask("mb", NL, R("mr", NL, 2 * NL), 0)
-    mask("mb", 0, R("mr", 0, NL), 0)
-    quant("win", CL, 2 * NL, "he")
-    mask("ma", P, PS(1, d + x1, NL + d + x1), 0)
-    squeeze("sa", "ma", P, 256)
+        relu(RQ["e"][t], "hx", P, t, t, 0, CAPP)
+    quant("win", C2 + V0 + 2 * d, 128, "hx", NL + 2 * d)
+    cells(1, N1 + NL, CAPP + 2 * d, C2 + NL - d, "an12")
+    for t in range(4):
+        relu(RQ["l"][t], "hx", HE, t, t, CAPP, P)
+    mm(0, "uab", 128, "wn", N1 - V0, 128)
+    mm(1, "uab", 0, "win", C1, 128, True, False)
+    tt(R("sl", 0, NL - last), PS(0, V0, 128 - last), R("a1d", 0, NL - last), A.add)
+    mask("ma", 256, PS(0, V0 + d, 128 - last), 0)
+    if d:
+        mask("ma", 415, PS(0, V0, V0 + 1), 15)
+    mm(2, "uab", 0, "win", C2 + V0, 128)
+    mask("me", 0, PS(2, CAPP, 128), 0)
+    squeeze("se", "me", 0, 64)
+    cp(R("msg1", 10, 14), W("se", 0, 4), "s")
+
+    rights(HI, "wn", N2, 128)
+    mm(1, "uab", 128, "wn", N2, 128, False, True)
+    mm(3, "uab", 0, "win", C2 + V0, 128, True, False)
+    mm(3, "uab", 128, "wn", N2 + V0, 128, False, True)
+    turn(R("tr", 64, 128), PS(3, CAPP, 128))
+    cp(R("msg1", 16, 18), R("tr", 64, 128, 32), "s")
+    send(1, R("land1"), R("msg1"), "am1")
+    for t in range(4):
+        relu(RQ["n"][t], "hx", HE + NL, t, HI[t], 0, NL)
+    quant("win", CL, 2 * NL, "hx", HE)
+    mm(0, "uab", 0, "win", CL, 2 * NL)
+    tt(R("nle"), PS(1, 0, NL), R("sl"), A.is_le)
+    scan(R("cum", 2, 2 + NL), R("ones", 0, NL), R("nle"))
+    scan(R("cw"), R("hold", 0, NL), R("cum", 2, 2 + NL), A.add, A.min)
+    scan(R("cx"), R("hold", 0, NL), R("cum", 1, 1 + NL), A.add, A.min)
+    ff = R("nf", 6, 12)
+    tt(ff, W("cw", 0, 6), W("cx", 0, 6), A.is_equal)
+    for a in (0, 12):
+        act(R("nf", a, a + 6), ff, -1.0, 1.0)
+    if RQ["th"] == "v":
+        tt(R("xx"), ff, R("k64"), A.mult)
+        tt(R("msg3", 0, 6), W("cw", 0, 6), R("xx"), A.add)
+    else:
+        for c in range(6):
+            act(R("msg3", c, c + 1), R("nf", 6 + c, 7 + c), R("k64", c, c + 1), W("cw", 16 * c, 1))
+    tt(R("yy"), R("aw"), R("nf", 6, 18), A.mult)
+    mask("mc", 0, PS(0, 0, 2 * NL), 0)
+    squeeze("sc", "mc", 0, 2 * NL)
+    tt(R("yz"), W("sc", 0, 12), R("nf", 0, 12), A.mult)
+    tt(R("msg3", 6, 18), R("yz"), R("yy"), A.add)
+    send(1, R("land3"), R("msg3"), "am3")
+    x3 = NL - 2 * ((rank - 3) % n == n - 1)
+    cells(3, N3, P - x3, C1 + x3 + shift[3], "an3")
+
+    mm(2, "uab", 128, "wn", N2, 128)
+    mm(1, "uab", 128, "win", C2 + V0 + 2 * d, 128)
+    tt(R("sxe"), PS(3, CAPP, 128), R("geq"), A.add)
+    cp(R("sx", 0, nx), PS(3, xs - V0, 128), RQ["sx"])
+    lefts(HI, "win", C2 + V0, 128)
+    rights(HI, "wn", N2 + V0, 128)
+    for t in range(4):
+        relu(RQ["x"][t], "hx", HE + 2 * NL, t, HI[t], CAPP, 128)
+    mm(5, "uab", 0, "win", C1 + V0, 128, True, False)
+    turn(R("tb"), PS(1, CAPP - d, 128 - d))
+    mask("ma", P, PS(2, d, NL + d), 0)
+    lefts(LO, "win", C1 + V0, 128)
+    squeeze("sa", "ma", P, 256 + 16 * eb)
     for a in (0, 6):
         cp(R("b3w", a, a + 6 - d), W("sa", P, 6 - d), "s")
         if d:
             act(R("b3w", a + 5, a + 6), W("sa", P + 80, 1), 1.0, R("g5"))
-    mask("me", 0, PS(2, 2, NX), 0)
-    cp(R("ax"), PS(2, 0, NX), "s")
-    tt(R("sx"), PS(1, X0 + x1, P + x1), R("ax"), A.add)
-    mask("me", 64, PS(3, 2 + d, NX + d), 0)
-    lefts(LO, "win", C2, XW, (0,))
-    mm(4, "uab", 0, "win", CL, 2 * NL)
-    mm(5, "uab", 0, "win", C1 + V0, 128, True, False)
-    lefts(LO, "win", C2, XW, (1, 2, 3))
-    squeeze("sb", "mb", 0, 2 * NL)
-    squeeze("se", "me", 0, 64)
-    squeeze("se", "me", 64, 192)
-    mm(5, "uab", 128, "wn", N3 - 128, 128, False, True)
-    rights(LO, "wn", N2 + X0, XW)
-    mm(6, "uab", 128, "wn", N3 - 128, 128)
-    mw = W("sb", NL, 6)
-    m5 = W("sb", NL + 80, 1)
-    act(R("gg", 6, 12), mw, BIG, -BIG)
-    act(R("gg", 12, 18), mw, -BIG)
-    act(R("gg", 0, 6), mw, -BIG)
-    cp(R("msg1", 10, 14), W("se", 0, 4), "s")
-    send(1, R("land1"), R("msg1"), "am1")
-    act(R("c0", 7, 24 - 3 * last, 3), W("sb", NL, 6 - last), -float(D1L + D2L), float(D1L))
-    act(R("c1", 7, 24 - 3 * last, 3), W("sb", NL, 6 - last), float(D2L))
+    act(R("c0", 1, 18 - 3 * last, 3), R("nf", 6, 12 - last), -(D1L + D2L) / 2.0, D1L / 2.0)
+    act(R("c1", 1, 18 - 3 * last, 3), R("nf", 6, 12 - last), (D2L - D1L) / 2.0, D1L / 2.0)
     if last:
-        act(R("at"), m5, R("ka"), W("sb", 80, 1))
-        act(R("a0"), m5, R("k5n"), R("da"))
-        act(R("a1"), m5, R("d2n"))
-    mask("mc", 0, PS(4, 0, 2 * NL), 0)
-    squeeze("sc", "mc", 0, 2 * NL)
-    for c in range(6):
-        act(R("msg3", c, c + 1), W("sb", NL + 16 * c, 1), R("k64", c, c + 1), W("sb", 16 * c, 1))
-    tt(R("xx"), R("a1w"), R("gg", 6, 18), A.add)
-    tt(R("yy"), W("sc", 0, 12), R("gg", 0, 12), A.add)
-    tt(R("msg3", 6, 18), R("yy"), R("xx"), A.max)
-    send(1, R("land3"), R("msg3"), "am3")
-    if last:
-        cp(R("th6", 0, 5), R("msg3", 0, 5), "s")
-    tt(R("f4"), R("land1", 6, 14), W("se", 64, 8), A.add)
-    tt(R("f5", 0, 4), R("f4", 0, 4), R("f4", 4, 8), A.is_lt)
-    scan(R("fx"), R("ones", 0, 36), R("f5"))
-    cells(3, "wn", N3, NX, C1 + X0, "an3")
-    dma("y", ap(R("hu")), T.u[:, :], [R("land3")], [R("hu")])
+        act(R("a0"), R("nf", 11, 12), -(D1L + D2L) / 2.0, R("da"))
+        act(R("a1"), R("nf", 11, 12), (D2L - D1L) / 2.0, R("da"))
 
-    for t in (0, 1):
-        relu("s", "hc", 0, t, t, 0, XW)
-    tt(R("mr", NL + X0 + x0, 256), PS(5, 128 - NX + x0, 128), R("sx", x0, NX), A.is_lt)
-    act(R("junk", 0, 64), R("mr", 2 * NL, 256), None, None, ACT.Identity, R("nn"))
-    relu("s", "hc", 0, 2, 2, 0, XW)
+    v12 = N1 + o12 + V0
+    mm(5, "uab", 128, "wn", v12, 128, False, True)
+    rights(LO, "wn", v12, 128)
+    mm(7, "uab", 128, "wn", v12, 128)
+    tt(R("fr", 0, nx), PS(5, xs - V0, 128), R("sx", 0, nx), A.is_lt)
+    act(R("junk", 0, CAPP), R("fr", nx - CAPP, nx), 1.0, 1.0 / 128, ACT.Identity, R("nb"))
+    tt(R("nfe"), PS(5, CAPP, 128), R("sxe"), A.is_lt)
     if last:
-        m95 = R("mr", 2 * NL - 1, 2 * NL)
-        ts(R("th6", 5, 6), m95, R("kt"), A.mult, R("at"), A.add)
-        act(R("c0", 22, 23), m95, R("k5e"), R("a0"))
-        act(R("c1", 22, 23), m95, R("d2e"), R("a1"))
-    tt(R("mb", 2 * NL, 256), R("mr", 2 * NL, 256), R("mskx", 2, NX), A.mult)
-    ts(R("c1", 6, 24, 3), R("th6") if last else R("msg3", 0, 6), R("nn"), A.is_le)
-    squeeze("sb", "mb", 192, 256)
-    relu("s", "hc", 0, 3, 3, 0, XW)
-    scan(R("co", 6, 24), R("c0", 6, 24), R("c1", 6, 24))
-    cp(R("offa", 0, 5), R("co", 8, 21, 3))
-    tt(R("co", 26, 36, 3), W("sb", 2 * NL, 4), R("pe"), A.add)
-    pick("wn", C3, "win", C1, CX, "offa", 80)
-    mm(7, "uab", 128, "wn", C3 - 48, 128)
-    op("v", lambda: g.vector.transpose(ap(R("fy")), ap(R("fx", 4, 36))), [R("fx")], [R("fy")])
-    act(R("junk", 80, 96), R("fy", 0, 16), -GATE, -GATE / 32, ACT.Identity, R("nr"))
-    act(R("junk", 96, 112), R("fy", 0, 16), GATE, GATE / 32, ACT.Identity, R("nq"))
-    quant("win", CX, XW, "hc")
-    cp(R("offb", 0, 5), R("co", 23, 36, 3))
-    pick("wn", C3 + 80, "win", C1, CX + XW, "offb", 80)
-    mask("mf", 0, PS(7, 48 + d, 128), 0)
-    if d:
-        mask("mf", P - 1, PS(7, 48, 49), 15)
-    squeeze("sf", "mf", 0, 80 - 16 * d)
-    act(R("gt", 0, 6), R("land3", 0, 6), GATE, R("nr"), ACT.Relu)
-    act(R("gt", 6, 12), R("land3", 0, 6), -GATE, R("nq"), ACT.Relu)
-    mask("ma", 256 + X0 - d, PS(6, 128 - NX, 128), X0 - d)
-    mm(4, "uab", 128, "wn", C3 + V0, 128)
-    mm(5, "uab", 0, "wn", C3 + V0, 128)
-    cp(R("a2f", 0, 6), R("land1", 0, 6), "s")
-    cp(R("a2f", 6, 10), R("land1", 10, 14), "s")
-    squeeze("sa", "ma", 336, 416)
-    cp(R("e1", 2, 12, 3), R("co", 26, 36, 3), "s")
-    cp(R("e1", 14, 30, 3), R("co", 8, 24, 3), "s")
-    cp(R("s1x"), PS(5, 128 - NX, 128), "s")
-    act(R("e1", 1, 12, 3), W("sb", 2 * NL, 4), -1.0, float(N4 - C1 - D1X))
-    act(R("e1", 13, 30, 3), R("co", 7, 24, 3), -1.0, float(N4 - C1))
-    mask("mf", 80 - d, PS(4, 48, 128), 80 - d)
-    tt(R("ab"), R("land3", 6, 18), R("b3w"), A.add)
-    tt(R("zz"), R("ab"), R("gt"), A.subtract)
-    tt(R("s2p"), R("a2f"), W("sa", 256, 10), A.add)
-    tt(R("s3", 0, 6), R("zz", 0, 6), R("zz", 6, 12), A.max)
-    squeeze("sf", "mf", 80 - 16 * d, P)
-    tt(R("s1p"), R("land1", 0, 10), W("sf", 0, 10), A.add)
-    tt(R("thr"), R("s3"), R("s2p"), A.max)
-    tt(R("d0", 1, 30, 3), R("s3"), R("s2p"), A.is_gt)
-    tt(R("d0", 2, 30, 3), R("s1p"), R("thr"), A.is_lt)
-    tt(R("msg2", 10, 15), R("s1p", 5, 10), R("s2p", 5, 10), A.max)
-    cp(R("offs"), R("e1", 2, 30, 3))
-    scan(R("sp"), R("d0"), R("db1"))
+        f95 = R("fr", 1, 2)
+        act(R("t5"), f95, R("kt"), R("msg3", 5, 6))
+        ts(R("c0", 16, 17), f95, R("k5e"), A.mult, R("a0"), A.add)
+        ts(R("c1", 16, 17), f95, R("d2e"), A.mult, R("a1"), A.add)
+        act(R("c1", 15, 16), R("t5"), -1.0, R("nb"), ACT.Sign)
+    act(R("c1", 0, 18 - 3 * last, 3), R("msg3", 0, 6 - last), -1.0, R("nb"), ACT.Sign)
+    scan(R("co"), R("c0"), R("c1"))
+    one = RQ["one"]
+    if one:
+        cp(R("offa", 0, 6), R("co", 2, 18, 3))
+    else:
+        cp(R("offa", 0, ea), R("co", 2, 3 * ea, 3))
+        pick("wn", C3, "win", C1, CX, "offa", 16 * ea)
+    dma("y", ap(R("hu")), T.u[:, :], [R("co")], [R("hu")])
+    for t in range(4):
+        relu(RQ["y"][t], "hx", HE + 256, t, t, xs - V0, 128)
+    scan(R("sq"), R("eb0"), R("nfe"), A.min)
+    if last and not one:
+        cp(R("offb", 0, 1), R("co", 17, 18))
+    ts(R("offa", 6, 10) if one else R("offb", last, last + 4), W("sq", 0, 4), -float(nx), A.mult, 0.25, A.add)
+    quant("win", CX, nx + CAPP, "hx", HE + 2 * NL)
+    lo = NL - d - last
+    mask("ma", 256 + lo, PS(7, NL - V0 - last, 128), lo)
+    squeeze("sa", "ma", 256 + 16 * eb, 416)
+    for c in range(10):
+        act(R("ga", 16 * c, 16 * c + 16), R("geq", 0, 16), 1.0, R("land1", c, c + 1))
+
+    def score(a, src):
+        tt(R("mf", a, a + src[2] - src[1]), src, R("ga", a, a + src[2] - src[1]), A.add)
+
+    def most(a, b):
+        scan(R("sf", a, b), R("rst", 0, b - a), R("mf", a, b), A.min, A.max)
+
+    if one:
+        pick("wn", C3, "win", C1, WIN, "offa")
+        mm(4, "uab", 128, "wn", C3, P)
+        score(0, PS(4, d, P))
+        if d:
+            score(P - 1, PS(4, 0, 1))
+        most(0, P)
+    else:
+        pick("wn", C3 + 16 * ea, "win", C1, WIN, "offb", P - 16 * ea)
+        va = 16 * ea - 128
+        mm(4, "uab", 128, "wn", C3 + va, 128)
+        score(0, PS(4, d - va, 128))
+        if d:
+            score(P - 1, PS(4, -va, 1 - va))
+        most(0, 16 * eb)
+        mm(6, "uab", 128, "wn", C3 + V0, 128)
+        score(16 * ea - d, PS(6, 16 * ea - V0, 128))
+        most(16 * eb, P)
+    for b in (0, 1):
+        ts(R("fx", 32 * b, 32 * b + 32), R("tb", 32 * b, 32 * b + 32), R("land1", 14 + b, 15 + b), A.add,
+           R("land1", 16 + b, 17 + b), A.is_lt)
+    turn(R("fy"), R("fx"))
+    act(R("junk", 64, 128), R("fy"), -GATE, -GATE / 128, ACT.Identity, R("nr"))
+    act(R("junk", 128, 192), R("fy"), GATE, GATE / 128, ACT.Identity, R("nq"))
+    act(R("z0", 1, 12, 2), R("land3", 0, 6), -GATE, R("nq"))
+    act(R("z0", 13, 24, 2), R("land3", 0, 6), GATE, R("nr"))
+    tt(R("z1", 0, 24, 2), R("land3", 6, 18), R("b3w"), A.add)
+    if RQ["s2"][0] == "v":
+        tt(R("z1", 13, 24, 2), R("land1", 0, 6), W("sa", 256, 6), A.add)
+    else:
+        for c in range(6):
+            act(R("z1", 13 + 2 * c, 14 + 2 * c), W("sa", 256 + 16 * c, 1), 1.0, R("land1", c, c + 1))
+    if RQ["s2"][1] == "v":
+        tt(R("thr", 6, 10), R("land1", 10, 14), W("sa", 256 + NL, 4), A.add)
+    else:
+        for c in range(6, 10):
+            act(R("thr", c, c + 1), W("sa", 256 + 16 * c, 1), 1.0, R("land1", 4 + c, 5 + c))
+    scan(R("zz"), R("z0"), R("z1"), A.min, A.max)
+    tt(R("thr", 0, 6), R("zz", 1, 12, 2), R("zz", 13, 24, 2), A.max)
+    tt(R("d0", 1, 18, 3), R("thr", 0, 6), R("z1", 13, 24, 2), A.is_gt)
+    tt(R("d0", 2, 30, 3), W("sf", 0, 10), R("thr"), A.is_lt)
+    tt(R("msg2", 1 - d, 5), W("sf", 96 - 16 * d, 4 + d), R("thr", 6 - d, 10), A.max)
+    send(-1, R("land2", 1 - d, 5), R("msg2", 1 - d, 5), "am2")
     scan(R("so"), R("d0"), R("da1"))
-    cp(R("msg2", 0, 10), R("sp", 2, 30, 3), "s")
+    if d or last:
+        scan(R("sp"), R("d0"), R("db1"))
+        cp(R("offq"), R("sp", 2, 30, 3))
     cp(R("offp"), R("so", 2, 30, 3))
     pick("pool", 0, "wn", C3, N3, "offp")
-    send(-1, R("land2"), R("msg2"), "am2")
+    send(-1, R("offl"), R("offq" if d or last else "offp"), "am4")
     send(-1, R("plandq"), R("poolq"), "apq")
     send(-1, R("plands"), R("pools"), "aps")
     iota(R("spr", 0, CAPP), [[0, CAPP]], 1)
     iota(R("spr", CAPP, P), [[0, NL]])
+    iota(R("cst", 1, 769), [[1, 3], [0, 256]], 1)
 
-    mm(6, "uab", 128, "wn", N3 + NX - 128, 128)
+    v3 = N3 + nx - 128
+    mm(5, "uab", 0, "wn", C3 + V0, 128, True, False)
+    mm(5, "uab", 128, "wn", v3, 128, False, True)
     lefts(LO, "wn", C3 + V0, 128)
-    rights(LO, "wn", N3 + NX - 128, 128)
-    quant("wn", 256 + X0, 128, "h2")
-    tt(R("cr", 80 - NX + x0, 80), R("s1x", x0, NX), PS(6, 128 - NX + x0, 128), A.add)
-    quant("uu", 0, 128, "hu")
-    mm(7, "uu", 0, "win", C1, 128)
-    mm(4, "uu", 0, "win", C2, 128)
-    mm(5, "uu", 0, "wn", C3, P)
-    for t in range(4):
-        relu("s", "h3x", 128 - NX, t, t, 128 - NX, 128)
-    gather("s", R("spr", P, 2 * P), R("spw"), "offs")
+    rights(LO, "wn", v3, 128)
+    quant("wn", LB + 256, P, "hx", CAPP)
     c0 = 0 if last else 16
-    mask("md", c0, R("cr", c0, 80), 0)
-    quant("win", S3, 128, "h3x")
+    mask("md", 16 - last, PS(5, CAPP - last, 128), 16 - last)
     squeeze("sd", "md", c0, 80)
-
-    ts(R("offl"), R("land2", 0, 10), 512.0, A.mult)
-    if last:
-        tt(R("u6"), W("sd", 0, 5), R("land2", 10, 15), A.is_gt)
+    quant("uu", 0, 128, "hu")
+    mm(7, "uu", 0, "win", C2, P)
+    mm(4, "uu", 0, "wn", C3, P)
+    for t in range(4):
+        relu(RQ["z"][t], "hx", HE + 2 * NL - nx, t, t, xs - V0, 128)
+    gather("s", R("spr", P + CAPP, P + CAPP + 16 * (6 if one else ea)), R("spw"), "offa", 6 if one else ea)
+    if one:
+        gather("s", R("spr", P, P + CAPP), R("spw"), "offa", 10, 6)
+        if last:
+            pick("wn", S3 - NL, "win", C1, WIN, "offa", 32, 4)
+    elif last:
+        gather("s", R("spx"), R("spw"), "offb", 5)
+        cp(R("spr", 2 * P - 16, 2 * P), R("spx", 0, 16), "s")
+        cp(R("spr", P, P + CAPP), R("spx", 16, 80), "s")
+        pick("wn", S3 - 80, "win", C1, WIN, "offb", 16)
     else:
-        tt(R("e1", 0, 12, 3), W("sd", 16, 4), R("land2", 11, 15), A.is_gt)
+        gather("s", R("spr", P, P + CAPP), R("spw"), "offb", 4)
+    quant("wn", S3, 128, "hx", HE + CAPP)
+    for w, b in ((0, 7), (1, 4)):
+        cp(R("ysb", w * P, w * P + CAPP), PS(b, NL, P), "s")
+        cp(R("ysb", w * P + CAPP, w * P + P), PS(b, 0, NL), "s")
+    dma("y", T.y[:, 0:2 * P], ap(R("ysb", 0, 2 * P)), [R("ysb", 0, 2 * P), R("plands")], [])
+
+    if last:
+        tt(R("u6"), W("sd", 0, 5), R("land2"), A.is_gt)
+        cp(R("e1", 0, 8, 2), R("u6", 1, 5), "s")
+        cp(R("e1", 18, 19), R("u6", 0, 1), "s")
+        tt(R("v0"), R("u6"), R("pw5", 5, 10), A.mult)
+    else:
+        tt(R("e1", 0, 8, 2), W("sd", 16, 4), R("land2", 1, 5), A.is_gt)
+        tt(R("v0", 1, 5), R("e1", 0, 8, 2), R("pw5", 6, 10), A.mult)
     nc = 6 - last
-    tt(R("v0"), R("land2", 5, 10), R("pw5", 5, 10), A.subtract)
-    pick("left", 0, "wn", 0, C3 + P, "offl")
+    pick("left", 0, "wn", LB, C3 + P, "offl")
     lefts(LO, "left", 0, P)
     rights(LO, "pland", 0, P)
+    cp(R("offk", 4, 4 + nc), R("offl", 0, nc))
+    for c in range(4):
+        ts(R("offk", c, c + 1), R("offl", 6 + c, 7 + c), R("v0", 1 + c, 2 + c), A.max)
     if last:
-        cp(R("e1", 0, 12, 3), R("u6", 1, 5), "s")
-        cp(R("e1", 27, 28), R("u6", 0, 1), "s")
-    cp(R("ysb", CAPP, P), PS(7, 0, NL), "s")
-    cp(R("ysb", 0, CAPP), PS(4, 2, NX), "s")
-    tt(R("v1", 4, 4 + nc), R("land2", 0, nc), R("pw5", 0, nc), A.subtract)
-    tt(R("v1", 0, 4), R("v0", 1, 5), R("u6", 1, 5) if last else R("e1", 0, 12, 3), A.max)
-    if last:
-        tt(R("v1", 9, 10), R("v0", 0, 1), R("u6", 0, 1), A.max)
-    ts(R("offk"), R("v1"), 2.0, A.mult, R("q3"), A.add)
-    step = 1.0 / 256 - 1.0 / 65536
+        ts(R("offk", 9, 10), R("offl", 5, 6), R("v0", 0, 1), A.max)
     gather("v", R("wr"), R("cle"), "offk")
     gather("s", R("wg", 16, P + 16), R("cgt"), "offk")
-    act(R("v3"), R("v1"), -2.0, 1.0, ACT.Relu)
-    act(R("v4"), R("v1"), -2.0 * step, 2.0 * step + 1.0 / 65536)
-    act(R("v5"), R("v1"), 2.0, 1.0)
-    cp(R("ysb", P, P + CAPP), PS(5, NL, P), "s")
-    cp(R("ysb", P + CAPP, 2 * P), PS(5, 0, NL), "s")
-    dma("y", T.y[:, 0:2 * P], ap(R("ysb", 0, 2 * P)), [R("ysb", 0, 2 * P), R("plands")], [])
-    scan(R("sf"), R("wg", 0, P), R("wr"), A.add)
+    ts(R("v3"), R("offk"), 255.5, A.is_lt, 1.0 / 65536, A.max)
+    ts(R("v4"), R("offk"), 511.5, A.is_lt, 1.0 / 256, A.mult)
+    ts(R("v5"), R("offk"), 1.0, A.add, 1.0 / 128, A.mult)
+    scan(R("eo"), R("e0"), R("e1"))
+    scan(R("sf"), R("wg", 0, P), R("wr"), A.add, A.add, -(CAPP + 1.0) * (1 + 256 + 65536))
     tt(R("v2"), R("v3"), R("v4"), A.max)
     tt(R("ci"), W("sf", 0, 10), R("v2"), A.mult)
-    ts(R("cj"), R("ci"), 255, A.bitwise_and)
-    ts(R("e0", 2, 30, 3), R("cj"), CAPP + 0.5, A.is_lt)
-    scan(R("eo"), R("e0"), R("e1"))
-    tt(R("v6"), R("v5"), R("e0", 2, 30, 3), A.mult)
+    ts(R("cj"), R("ci"), N4 - C3, A.bitwise_and)
+    tt(R("v7"), R("cj"), R("eo", 1, 20, 2), A.add)
+    tt(R("v6"), R("cj"), R("v5"), A.mult)
     for t in range(4):
-        relu("s", "h4", 0, t, t, 0, P)
-    cp(R("off4"), R("eo", 2, 30, 3))
-    quant("win", N4, P, "h4")
+        relu(RQ["w"][t], "h4", 0, t, t, 0, P)
+    cp(R("off4"), R("v7"))
+    quant("wn", N4, P, "h4")
     cp(R("offt"), R("v6"))
-    pick("c4", 0, "win", C1, WIN, "off4")
+    pick("c4", 0, "wn", C3, WN, "off4")
     gather("v", R("spr", 2 * P, 3 * P), R("cst"), "offt")
     mm(6, "uu", 0, "c4", 0, P)
     dma("y", T.oc[:, :], view(R("c4q")), [R("c4q")], [])
     cp(R("ysb", 2 * P, 3 * P), PS(6, 0, P), "s")
     dma("s", T.y[:, 2 * P:3 * P], ap(R("ysb", 2 * P, 3 * P)), [R("ysb", 2 * P, 3 * P)], [])
     for k in range(4):
-        dma("y", T.osc[4 * k:4 * k + 4, :], T.c4s[32 * k:32 * k + 4, :], [R("c4s")], [])
+        dma(RQ["o"][k], T.osc[4 * k:4 * k + 4, :], T.c4s[32 * k:32 * k + 4, :], [R("c4s")], [])
     dma("y", T.sp[0:1, :], T.spr[0:1, :], [R("spr")], [])
 
     for i in ORDER.get(rank, range(len(prog))):

from concourse.mybir import dt, AluOpType, ActivationFunctionType

P, CAPP = 160, 64
NL = P - CAPP
V0 = P - 128
BIG, GATE = 1.0e29, 2.0 ** 80
CODE, PLANE, F, BF, I32, U16 = "float8_e4m3fn_x4", "uint8", "float32", "bfloat16", "int32", "uint16"
CN, C1, C2, CL, CX, WIN = 64, 128, 352, 560, 752, 896
LB, C3, NE, N1, N2, N3, N4, S3, WN = 32, 544, 736, 800, 1056, 1216, 672, 1376, 1504
HE = P + CAPP + 2
D1L, D2L = CL - C1, CL + NL - C1


def _pair(name, n):
    return {name + "q": ("sbuf", [128, n], CODE), name + "s": ("sbuf", [128, n], PLANE)}


def _f(dtype, **kw):
    return {k: ("sbuf", [128, n], dtype) for k, n in kw.items()}


SCRATCH = {}
for _n, _w in (("wt", 1024), ("uu", 128), ("uab", 256), ("win", WIN + P + 2), ("wn", WN), ("pool", P), ("pland", P),
               ("left", P), ("c4", P)):
    SCRATCH.update(_pair(_n, _w))
SCRATCH.update(_f(BF, hx=4 * (HE + 322), hu=512, hv=8, huab=1024, h4=640, ones=P, keep=192, tmod=256,
                  rst=P, cle=768, cgt=768, cst=769, spw=WIN - C1, hold=256, geq=CAPP, nle=NL, cum=NL + 2, cw=NL, cx=NL, fr=66, nfe=CAPP, fx=CAPP, fy=CAPP))
SCRATCH.update(_f(F, msk=192, a1d=NL, sl=NL, sx=66, sxe=CAPP, eb0=CAPP, sq=CAPP, ma=416, sa=416, mc=192,
                  sc=192, md=80, sd=80, me=64, se=64, tr=128, tb=64, ga=P, mf=P, sf=P, junk=192, wr=P, ysb=3 * P, spr=3 * P,
                  spx=80, msg1=18, msg3=18, land1=18, land3=18, msg2=5, land2=5))
SMALL, _at = {}, [0]
for _n, _w in dict(d0=30, c0=18, c1=18, e0=20, e1=20, wg=P + 16, z0=24, z1=24, qf=1, q3=1, pw=10, pw5=10,
                   k64=6, jw=10, t0=10, t1=10, t2=10, xx=6, yy=12, aw=12, nf=18, zz=24,
                   nb=1, thr=10, s1p=10, da1=30, db1=30, so=30, sp=30, co=18, t5=1,
                   e15=1, kt=1, k5e=1, d2e=1, da=1, a0=1, a1=1, f4=8, yz=12, nr=1, nq=1,
                   b3w=12, g5=1, v0=5, u6=5, v1=10, v2=10, v3=10, v4=10, v5=10, v6=10, v7=10, eo=20).items():
    SMALL[_n] = (_at[0], _w)
    _at[0] += _w
SCRATCH.update(_f(F, small=_at[0]))
SCRATCH.update(_f(I32, qi=1, qj=1, ci=10, cj=10))
SCRATCH.update(_f(U16, offa=10, offb=6, offp=10, offq=10, offl=10, offk=10, off4=10, offt=10))
for _b in range(8):
    SCRATCH["ps%d" % _b] = ("psum", [128, 512], F)
ARR = ["an1q", "an1s", "an2q", "an2s", "an3q", "an3s", "an12q", "an12s", "am1", "am2", "am3", "am4", "apq", "aps"]
SEMAPHORES = ["cg"] + ARR + ["sent"] + ["d%d" % i for i in range(16)] + ["cv", "cs", "ct"]
RQ = dict(e="svsv", l="svsv", n="ssss", x="ssss", y="ssss", z="ssss", w="ssss", o="yyyy", th="s", sx="s", s2="vv", one=0)

ISSUE = {
    0: '(0(@(4(1(2(3(8(5(6(?(9(<(7(;)H)O(S(A(I(=(K(N(M(E(O(H)M*4)N(J)K)@)>*5(L(B)P(R)I(C)R(:)B*1)J)A)E(Q)Q)W)G*0(P(D)F*2)C)0)S(>(U)D*3)L(W(G)6(T*6)5)7(V(F)1-U)2)?)3)=)4-T*7):*:)T)9*8*9)<)8*;*B*>*<*F*=*R*E*D*Q)U*O)V*?*P*C*K*A*H+4*G+3*I*S*T+2*J*U+1*@*L+Q+U+P+7+5*M,1+6+8+T*N*V+L+N,4*W+M+:+S+O+9+W+0+E,B+;,6+=+B+F+<,7,@+>,9+C,5,C+?,:+A+D+@,F,3+G,E+R,H,8,D+H,I+V,J,A,G,0,;+I,K,Q,T,S,U,<,L,R,2+K,V,P,M-;,O+J-<,N,=,?,>,W-4-0-3-=-2->-1-?-8-5.0-A.2-@-6.3-C.7.1-B.4-9.6.5-7-V-E-W-:-D-G-F-H-I-J-L-K-M);-N-Q-P-O.?.8.A.B-S.9.>.;.C.@.:-R.=.<.J.L.N.W.K.M.E.F.G/0.P/7.R/4/5/1.Q.D/3.T/2.U/6.V/9.O.S/8/?/@/:/A/>/;.H.I/</=/C/B/D/F/E/G/M/I/H/O/N/L/P/J/K',
    1: '(8(0(5(1(2(3(4(6(=(?(9)I(7(@(<(Q(A(N(J(>(H(K(D)@(I(L(M)Q)U);)?)T(G)S(R)=)J(;(B(O)L(P)M)F)V)D)R(:)C)9)>)G(C)5)4(V(F(S(T(W)6(U(E)0)1-H)8)3)<)A)2-G*0)O)P)W*2*1)7*4*3*:*6*H*5*;*<*>)N*I*7)B*F)E)H*G*B*=*9*?*R*J*@*S*K*A*L*Q*8*P*C+H*V+L*T+D*W*U*M+P+J*D+N*N+1+G*E+C+0+S+<*O+R,7+2,<+E+K+4+I+=+3+M+7+F,6+U+8+:+6+;+5+V+9+>,0,=,:,8+?,1,>,;,?,5+Q+T+@,@,H,2,F+W,9,A+A,3,M+O,I,E,J,B,G+B-0,4,D,K,C,L,Q,W,P,O)K-1,T,N-K-2-7-N-3,R-5-8-4,U-6,S-O-R-9-L-P,V-I-M-;-J-:-Q-<-=):-?->-@-A-D-C-B.2-V.4.6-F-T.1.0.3.5-W-U-E-S.:.;.>.?.=.J.A.K.@.O.Q.P.L.E.R.D.N.M.C.G.8.T.9.H.I.S.<.B.F.7/2.U/3/4.V/1.W/0/5/6/7/9/8/:/A/@/;/</C/?/B/=/>',
    2: '(8(0(4(1(2(3(5(6(;(9(=)G(7(<(:)I(R(A)@(J):(H(M(D(L(G(N(@(K(I(B)J(?(P)K(>)L)H)U)=(Q)A)E(O)B)F)D)M)>)C(C)8)S)Q(U)T)V)6)?(W)R(F(S)4(T)5(V(E)0)1-H)<)3);-G)O)W)N)P*2*0*1)7*3*:*6*4*>*5*I*;*<*H)2*G*7*F*=*?*B*9*@*J*S*K*R*A*P+I*Q*L*8*C+H*V+L*T*D*U*W+D*E*M+M+E+J*N+C+1+P+0+S*O+<+Q+F+2,0+T,7+4+=,:+:+6,1+3,;+8+;+5+7+U+9+>,H,5+V,=,8+N+?,>+W,?,6,9,I+G,2+@,@+K+R,J,F,3,A,<,G+A,K+O,E,B-0+B,D,W,M,4,L,C,P,O,Q-1,T-7-N-2,N-K-3-I-M-5,R-L-4,U-6-J-P-8-Q,V-O-R-9,S-;-:-<-=)9-?->-@-A-D-C-B.1-T.5-F-V.3.6-S.0.2-U.4-W-E.:.;.8.9.>.?.=.J.A.K.@.<.P.O.Q.L.D.R.C.N.M.B.T.H.F.S.G.E.I.U/3.7/1.V/2/4.W/0/5/6/7/9/8/:/;/</C/@/A/?/B/=/>',
    3: '(5(=(0(1(2(3(:(6(8(@(4(Q(7(9(?(A(H(R(;(L(<(D(N(I(J(K)=(>)D*2)V)K*4(M)L(G)A)C)I)O*3)J)>*1)B(B)Q*9):)P(P)?*0)E(C)W)N(O(T(W)9)4(F)6*7*8)F(V*6)H(S*5)5(U(E)0.3)1)<.2)3)2*:)G*=)8*;*<);)7*>*E*A)U*?*I*@*T*F)M*R)R*G*S*B)S*J*H*U*Q*D*K+6*M+4*L)T+5+S*V+9*C+T+3+W*N*W+:,0+7*O,3+8)@+<+N*P+;+O+0,6+U+P,1+1+=,4+Q+G,D+2+@,<+?+B,8+A,B+>+H+C,9,C+D,E,@+F,H,5+R+E,7,A+I,:,J,I,L,F,K+V+J,M,;-2,O,G,Q-3,P+K,W,N-0,2-7-5-1+M,R-B,V-A+L,S-4,U-C-6,T-:-9-;-E,=->.4-8.8,?.7,>-D-<-F-?.;-G-I.<.6-H.:-=.5.9-@.=-K-L-M-J-N-O-P-R-Q-S-T-W-V-U.F.?.I.1.>.D.@.K.G.A.J.0.E.V.C.U.B.T/9/;/0/=/</:.W/A/B.O/>/3/D/4/@/?/2/7.Q/F.P/6/C/8.M/E/1/5.N/M/G/L.L/N/H/K.R/I.H.S/J/O/P/Q/S/R/T0203/U0401/V05/W00',
}
ISSUE = {
    0: '(4(?(0(;(1(2(5(7(3(6(8(=)H(:)I)O(@(<)9(A)K)@(J(D)J)M(L(M(N(B(H(K*3);)N(R(G(I):)>(P)Q(C*0)R(F*4)A)W*2)P(>(E(9)L(S.6)8(Q)S*1*5.7)=(O)?)F)G)0)C)4)1(U(T)<(W)3(V)D)T*8*9*7*:*<)5*C*=)7*;)6*B*O*>*D*P)V*R*F*?+1*Q*E+2+4*H*K+3*I*A*T)2)E*J*U*@*G)U*6*L*S+5+Q+U*V+R*M+7+6+N*W+P*N,1+T+8+V+M+E+O,4+0+:,2+9,0,B+F+L+S+;+W,5,:,H,7,6,F+=+?+<+@+B+A,J+C+>,8,D,I+D,@,C,A,3+G,9,;,E,K,R,G+H,L,U,?,Q,T,S+I-8-6,M-;-7,P-F+K,V-E+J,N,O,W-4,>,=-3-5,<-2-0-G->-<-=-1-H-I-?-9-:-B-@-K-N.=-M-J-L.<-A.@.A-C.9-O.;.?-D.>-P.B)B.:-Q-R-S-U-V-T.0-W.1.2.3.D.L.C.J.K.N.E.I.5.F.4.8.U.O.G.H.V/0.W/:.P/9/;/=/</C/3/2/A/4/?/@/>/E/7/8/D/1/5/L/6/M/F/J/K/G/B.R.S/H.Q/I/O/N/P.T/Q/R/S.M/U/T0301000402/V/W',
    1: '(9(4(0(1)H(2(6(>(3(;(8(=(:(5)?(?(P(F(L)8(J(@(H(I(B(K(E(G)D(N)I(7)K(Q(<(A)J)7(D);(C)S)L)G(M-O)E)9-P)<(O)>)A(V)B)=(W)R)U)P):(S)@)2)1(T)6)0)4(R(U*0)V*1)W)5*2)3*4*5*9*E*;*F*3)Q)M)N*H*:*G*=*O*6*P*<*R*>*Q)F)O*?)C*A*@*8*J*S*K*7*I*B+I+G+K*L*T*U+H*C+F+D*M+O+B*V+L+;*D+J+E+R*W+0+P+T*N+N+1,6+<+M+C+U+7+2+9+6+3,4+5,7,<+8+4,0,1,:+W+S,=,9+=,5,E+:,>,?+V+>,8,N-@,Q,2,R,W+Q,@,G,I,S,H-8,F+?,3,O,;,A,D-9+A,J+@,B,C,K,V,P-:-2-0-1,L-<-;,U-3,T-5,M-T-=-?->)T-4-6-B-A-7-C-F-E.0-D-W-R-V-H-G.3.2-S-I-U.1-J-K-L.5.:.;.<.6-N.7-M.F-Q.4.8.G.9.I.R.V.U.T.S.C.H.=/2/0/1.W.L.A/3.B.M/6.>/4.K/5.Q.P.O.J/7/>.@.N/=/8/</;/9/:.D/?/@.E/A/B/C/D.?/J/E/F/I/M/L/K/G/H',
    2: '(;(4(0(1(2(7(6(3(8)G(:(5(?(P)?(F(J);(H(E(L(G(B(K)E(I)8(@)L)F(=)I(N(9(>)A)7(Q(A)6)C(D)<)D(C(<-O)9(M-P)Q)J(O)P)>)H)B(V)=)K(W(T)T)R):(R(U)0)1)@)2(S)N)M)O*1*0)V)W*5)5*<*4)4*2)3*9*H*3*;*G*E*=*6*R*F*:*Q*O*?*A*P*@*8*>*I*7*J*B*K*S+G+K*U+I+M*C*L*T*V+H+D*D+L+O+B*M+Q*W+C+0+E+R+;+P*N+1,6+T+S+U+<+3+2+5+F+6,5+7+4+8+9+W,<+J+:,7+=+V,>,8,=,9,0+>,E,4,:,I,?,;,F,1,U,W,G,N+?,P+N,@,H-8+A,J,2,O+@,3,T,A,Q,D-9,K,B,C-:-0-1,L,S,R-@-2-<-;-5,V,M-U-R-3-T-V-=-?->)U)S-6-4-B-A-7-C-F-D-E.2-S.0-G-H-W.1.3-I-J-K-L.5.:.7.<.=.;.6-N.4.8-M.9.F-Q.A.G.H.I.R.?.S.U.V.T.L.K/1.M/0/2.W.Q.@.O/6.P/5.J/>.N/</7/=/4/3/;/8.C.B.D/9/:/@.E/?/A/B/C/D.>/K/E/F/J/M/I/L/G/H',
    3: '(4)H(0(1(7(2(5(3(6(8*2(=(:(;(<)?)T*0)I*8(?(L(F(I)7(J(P(K)>(H)G(B)U(E*1(@);(G(9)F(>)E)6(N)O(A)M)B(D)J(C)<(Q)8)P.;*4*3)A(O(M.<)C)V)L)N)=(V)D)9(U(W(T)@)3)2):(S)0)1(R*7*6*9)S*:*;*<*=*D)4*>)5*E*?*S*F*Q*@)Q)W*5*H*G*P*R+5*A*I+3*T*J+2*K+4*L)R)K*C*U+8*V*B+6+R+V+S*M+W+9*W+7,2*N+T+:+M+;+0,0+O+N*O,3,5+<+F+P+1,7+>,B+=,4+B+?+C,@+D+@+A,C,?,A+G+Q,;,6,G+E+U+H,8,I,H,K,D+I,:,1-1,<,9,J,F,L,N,E,V-2+J,M,P,O-6+K-:-J-A-0-K,W+L-=,Q-9,=,>-?-8-4-@-<-L,R,U-3-5-M,S,T-B-C-7-N-;-D->-G-S-R.@-P-Q-O.B-E.C.A-H-T.G-F.>.F-I.D-U.?.E.0-W-V.2.1.3.5.4.6.7.8.I.Q.H.S.P.J.:.K.T.W.9.=.L/6/9/:/;/H/8.N/F.O/G.U/I/D/E/>.V/0/=/</J/K/L/B/7/M/A/@/P/?00/C/Q/W.M/V/R/O01/N/3/S/1/4/2.R/T/U03/5020405060709080>0=0@0<0?0:0;',
}
ISSUE = {
    0: '(5(;(0(1(2)M(4(3(7(6(?(8(>(:(@(N(L*4(<(I(H)O)I(G(D)K)N(R(J(M*5(K)W)A*1*3(A)J(B)P(P):)S)=(C(S(O(F)H(E)E(9)L.7(Q)C)0.6)B)@)R)1*0)?)F)G)8)2);)3(V)<)5)D(U(T)>)9)4)T(W*:*7*8*9*>)7*E*;)6*B(=*P*<*R*=*C*D*Q)V*F*O+2*?+4*G+3*S*H+1*I*K)Q*A*T*J*6)U+S+7*@*U+5+Q+W*L+U+8*V+6*M+R+9+L+N*W+M+:+P*N+E,3,1+T+O+;,6+0,4+F,7+=+C+<,B+?+B+A+@+>,0,5,C,A,@,:+D,F+G,9,H,E,Q+V+H,8,T,J,I,D,;,G,S,2,U+I,K,R+K-0+J,V,L-;,=-4,W-5-8,?-6,>,<-7-3-F,M,P-E-<,O-G,N-=-1-I-H->-2-N-B-L-J-:.;-M-K-9*2.<.=-?.?-@-O.@-C.>-A.9.B-P.A-D.:-Q-R-S-U-V-T.0-W.1.2.3.D.M.F.J.K.E.5.C.H.4.G.U.8.V/0/9/:/=/</;.L.W/A/?/@/>/2.I/C.R/3/E.P.Q/4/D/6/7/8/1/F/K/5/L/G/M.O/B/J/H.S.N/I/N/O.T/P/Q/R/S/U/T0403010002/V/W',
    1: '(;(4(0(1(2(9(5(3(7(6(8(=)H(>(?(F(L(@(J(G(H)8(B(P(K(E(I)G)6(:)K)I(<)9(N(A)J)P)?)S)F)L(D)7)U)Q)T(C)<);(Q-P(O(M-O)A)B)=(V)C(W)D)E)4):(U)1(T)@(R)2)N(S)V*1)W*0*2*9)5*5)>)3)M*3*F*:*G*4*;*=*<)0)O*H*E*P*6*Q*>*?*I*R*@*O*J)R*8*A*U*K*7+H*S+L+G*B+K*V*L*T*C+I+D+M*W*M+O+B+0+F*D+;+C+E+P+J+Q+1+R+T*N,0+<+3+9+2+6+N,6+4+7+S,5+5+8,:,4+U+:,7+=,<+V,H,>,8+>+W,9,=,;,I,E,F,1+?,?,G+A,J,L,T,W+@,V,O,Q,@,K-9,A,D-8-0-1,B,C-:,3,M,2,U,R-@-5-;-A-<-2-?,S,N-T,P-U->-6-=-3.0-R-B.1-7-S-4-W-C.3-F-V.2-D-E-G-H-I-J-K-L.5.=.7.>.<.6.;.:-N.4.8-M.9-Q.F.G.H.I.V.A.R.B.U.S.T.K.L/1.M/0/2.W/6.Q/3.P/5.O.J/>.N/=/7.@/</4/;/8.C.D.?/9/:/@.E/?/A/B/C/D/J/E/F/K/I/M/L/G/H',
    2: '(5(;(0(1(2(7(4(3(6(=)F(8(9)H(P(?(:(@)9)?(<(L(B)7(J(G(F(E(H(K(I)6(N)J)Q)I)8(A);(D(Q)T(O(C)B-P)C)<(M)=-O)@)K)P)>(V)E(W):)2(T)1)D)0)U(R(S)M)L)4(U)V)W*0*1*2*9)5*3)3*:*4*H*;*E*5*=*<*G*F*R*6*>*O*I*?*Q*@*P(>*A)N*8*J*U*K*7*S+G)R)O+K+H*B+L*V*L*T+O*C+C+0+I*W*M+F+D+B*D+;+P+M+R+1+E+S*N+<+3+4+2+9+Q,6+8+7+5+T+6,5+J,0+:,:+=,;,<+W+N,9+>,>+U,=+V,L,4,H,8,1,7+?,?,G,I+@,M,F+A,E,@,P-9,W,V,3,U,O-8,2,A,D,J,K-:,B,C-0-1-A-@-<)G-;,Q,T,R-?,N-5-=-2->,S)S)A-T-R-U-6-V-B-3-S.2-7.0-C.1-4-W.3-F-D-E-G-H-I-J-K-L.5.:.7.<.=.;.6-N.4.9-M.8-Q.F.G.H.I.T.C.S.A.V.B.R.U.D.@.K/4.L.W.J/0.E/1/2.N.O.P/5.M/;/6.Q/3/</=/7/>/8/9/:/@/?/A/B/C/D.?.>/E/K/F/J/L/M/I/G/H',
    3: '(=(4(0*2(1(7(2(5(3(6(8(;)F(:(>)?(?(P(L(F(@(J(K(H(G(I(B(<(E*1)9)>(N*6)M)G)7);*8)N(Q)U)T)8(A)J)H(D)@)E(C)<.;(O)L)K*5)A)B.<*0(M)W)P*3)V)=(V(W*7)4)6(R):(U)1(T(S)2*9*<*;*:*=*D)3*@)5*?*F*>*4)I)0*H*E*Q*P*A*S*R*G*I+3*J*T+2*K+5*L*C+4(9*U)O*B+Q+8)R)C*V+6+U+R)S+V*M+9*W,1)Q+7*N,2+T+:,0+O+0+M+;+S*O+F+N+W+P+<,4,5,7+1,C+G,;+>+=+C+@+A+B+?,?,H+D,B,A,6,3,@,G,:+E+H,F,I,9,K-1,E+I,8-6,D,J,M,N,L-0-2,<+J,P,O,W,V+K-7-;-=-9-8->-A-?-4+L,Q-J,=-K,R,U-3-5-L,S,T-B-C-R)D,>-N-D-M-<-:-@-G-Q-S.@-P-O.B-E.D.A-H.E-T-F.>.F-I.C-U.?.G.0-W-V.2.1.3.5.4.6.7.8.I.P.K.N.R.V.Q.J.W.:.H.S.M.9.L.=/6/3/1/9/8/7/:/;/D.O/F/4/G/E/H/I/?/O/0/=/</J/K/L/A/M/C/@/P/>/W/B/Q01/V/R/N00.T/2/S/T/5/U030204050607.U0<08090>0=0@0?0:0;',
}
ORDER = {r: [(ord(s[i]) - 40) * 40 + ord(s[i + 1]) - 48 for i in range(0, len(s), 2)] for r, s in ISSUE.items()}


def rank_program(g, core, T, topo):
    rank = T.rank_of(core)
    if rank is None:
        return
    n = len(T.cores)
    A, ACT = AluOpType, ActivationFunctionType
    eng = {"v": g.vector, "s": g.scalar, "t": g.tensor, "g": g, "y": g.sync}
    own = {"v": "cv", "s": "cs", "t": "ct", "g": "cg"}
    count = {k: 0 for k in SEMAPHORES}
    known = {q: {} for q in eng}
    clock = {}
    log = {}
    dmas = [0]

    def R(name, a=0, b=None, s=1):
        if name in SMALL:
            at, w = SMALL[name]
            return ("small", at + a, at + (w if b is None else b), s)
        return (name, a, SCRATCH[name][1][1] if b is None else b, s)

    def ap(r):
        return T[r[0]][:, r[1]:r[2]] if r[3] == 1 else T[r[0]][:, r[1]:r[2]:r[3]]

    def wait(q, ev):
        if known[q].get(ev[0], 0) >= ev[1]:
            return
        eng[q].wait_ge(T.sem[ev[0]], ev[1])
        for k, v in list(clock.get(ev, {}).items()) + [ev]:
            if known[q].get(k, 0) < v:
                known[q][k] = v

    def order(q, reads, writes):
        need = {}
        for rs, wr in ((reads, False), (writes, True)):
            for r in rs:
                bank = r[0].startswith("ps")
                for (a, b, st, ev, w, oq) in log.get(r[0], []):
                    if bank:
                        if oq == q:
                            continue
                    elif b <= r[1] or a >= r[2] or (st > 1 and st == r[3] and (a - r[1]) % st) or not (w or wr):
                        continue
                    need[ev[0]] = max(need.get(ev[0], 0), ev[1])
        for k in sorted(need, key=lambda k: k == own.get(q)):
            wait(q, (k, need[k]))

    def note(q, tag, ev, reads, writes):
        clock[ev] = dict(known[q])
        for rs, wr in ((reads, False), (writes, True)):
            for r in rs:
                log.setdefault(r[0], []).append((r[1], r[2], r[3], ev, wr, tag))

    prog = []

    def op(q, fn, reads, writes):
        prog.append((q, lambda: op_(q, fn, reads, writes), reads, writes))

    def dma(q, out, in_, reads, writes):
        prog.append((q, lambda: dma_(q, out, in_, reads, writes), reads, writes))

    def send(k, dst, src, sem):
        prog.append(("g", lambda: send_(k, dst, src, sem), [src], []))

    def op_(q, fn, reads, writes):
        order(q, reads, writes)
        count[own[q]] += 1
        fn().then_inc(T.sem[own[q]], 1)
        note(q, q, (own[q], count[own[q]]), reads, writes)

    def dma_(q, out, in_, reads, writes):
        order(q, reads, writes)
        s = "d%d" % dmas[0]
        dmas[0] += 1
        count[s] = 16
        eng[q].dma_start(out, in_).then_inc(T.sem[s], 16)
        note(q, "dma", (s, 16), reads, writes)

    def peer(k):
        return T.cores[(rank + k) % n]

    def view(r):
        return ap(r).bitcast(dt.uint8) if SCRATCH[r[0]][2] == CODE else ap(r)

    def send_(k, dst, src, sem):
        order("g", [src], [])
        to = peer(k)
        rid, pid = topo.addr(to)[:2]
        g.remote_dma(view(dst), view(src), T.sem[sem], T.sem.sent, pid, rid, topo.mask(core, to))
        count["sent"] += len(topo.engines(core, to))

    def lands(k, r, sem):
        count[sem] = len(topo.engines(peer(k), core))
        log.setdefault(r[0], []).append((r[1], r[2], 1, (sem, count[sem]), True, "far"))

    def isr(x):
        return isinstance(x, tuple)

    def val(x):
        return ap(x) if isr(x) else x

    def tt(o, a, b, alu):
        op("v", lambda: g.vector.tensor_tensor(ap(o), ap(a), ap(b), alu), [a, b], [o])

    def ts(o, a, s1, op0, s2=None, op1=None):
        rd = [a] + [x for x in (s1, s2) if isr(x)]
        if op1 is None:
            op("v", lambda: g.vector.tensor_scalar(ap(o), ap(a), val(s1), None, op0), rd, [o])
        else:
            op("v", lambda: g.vector.tensor_scalar(ap(o), ap(a), val(s1), val(s2), op0, op1), rd, [o])

    def act(o, a, scale=None, bias=None, func=ACT.Identity, total=None):
        kw = {}
        if scale is not None:
            kw["scale"] = val(scale)
        if bias is not None:
            kw["bias"] = val(bias)
        if total is not None:
            kw["accum_out"] = ap(total)
        op("s", lambda: g.scalar.activation(ap(o), ap(a), func, **kw), [a] + [x for x in (scale, bias) if isr(x)],
           [o] + ([total] if total else []))

    def cp(o, a, q="v"):
        if q == "v":
            op("v", lambda: g.vector.tensor_copy(ap(o), ap(a)), [a], [o])
        else:
            act(o, a, None, None, ACT.Copy)

    def fill(o, c):
        op("v", lambda: g.vector.memset(ap(o), c), [], [o])

    def scan(o, a, b, op0=A.mult, op1=A.add, first=0.0):
        op("v", lambda: g.vector.tensor_tensor_scan(ap(o), ap(a), ap(b), first, op0, op1), [a, b], [o])

    def iota(o, pattern, base=0, cm=0):
        if SCRATCH[o[0]][2] == I32:
            op("g", lambda: g.iota(ap(o), pattern, base, cm), [], [o])
        else:
            op("g", lambda: g.iota(ap(o), pattern, base, cm, allow_small_or_imprecise_dtypes=True), [], [o])

    def quant(name, a, w, h, ha=0):
        q, s, i = R(name + "q", a, a + w), R(name + "s", a, a + w), R(h, 4 * ha, 4 * (ha + w))
        op("v", lambda: g.vector.quantize_mx(ap(q), ap(s), ap(i)), [i], [q, s])

    def PS(bank, a, b):
        return R("ps%d" % bank, a, b)

    def mm(bank, st, sa, mv, ma, w, start=True, stop=True):
        rd = [R(st + "q", sa, sa + 128), R(st + "s", sa, sa + 128), R(mv + "q", ma, ma + w), R(mv + "s", ma, ma + w)]
        o = PS(bank, 0, w)
        op("t", lambda: g.tensor.matmul_mx(ap(o), ap(rd[0]), ap(rd[1]), ap(rd[2]), ap(rd[3]), start, stop), rd, [o])

    def lefts(banks, mv, ma, w):
        for t in range(4):
            mm(banks[t], "wt", 128 * t, mv, ma, w, True, False)

    def rights(banks, mv, ma, w):
        for t in range(4):
            mm(banks[t], "wt", 512 + 128 * t, mv, ma, w, False, True)

    def relu(q, h, ha, t, bank, a, b):
        o = R(h, 4 * ha + t, 4 * (ha + b - a), 4)
        if q == "s":
            act(o, PS(bank, a, b), 0.05, None, ACT.Relu)
        else:
            ts(o, PS(bank, a, b), 0.05, A.mult, 0.0, A.max)

    def turn(o, i):
        op("v", lambda: g.vector.transpose(ap(o), ap(i)), [i], [o])

    def pick(dst, da, src, sa, sb, off, w=P, k=0):
        o, i, l = R(dst + "q", da, da + w), R(src + "q", sa, sb), R(off, k, k + w // 16)
        op("v", lambda: g.vector.tensor_copy(ap(o).bitcast(dt.uint32), ap(i).bitcast(dt.uint32).indirect(ap(l))),
           [i, l], [o])
        o2, i2 = R(dst + "s", da, da + w), R(src + "s", sa, sb)
        op("s", lambda: g.scalar.activation(ap(o2), ap(i2).indirect(ap(l)), ACT.Copy), [i2, l], [o2])

    def gather(q, o, win, off, k=10, a=0):
        l = R(off, a, k)
        if q == "v":
            op("v", lambda: g.vector.tensor_copy(ap(o), ap(win).indirect(ap(l))), [win, l], [o])
        else:
            op("s", lambda: g.scalar.activation(ap(o), ap(win).indirect(ap(l)), ACT.Copy), [win, l], [o])

    def mask(buf, a, src, pos):
        w = src[2] - src[1]
        tt(R(buf, a, a + w), src, R("msk", pos % 16, pos % 16 + w), A.mult)

    def squeeze(o, i, a, b):
        scan(R(o, a, b), R("keep", 0, b - a), R(i, a, b))

    def W(buf, a, c):
        return R(buf, a + 15, a + 16 * c, 16 if c > 1 else 1)

    shift = {k: (((rank - k) % n) + k) // n for k in (1, 2, 3)}
    d = shift[1]
    last = (rank + 1) // n
    jw = "jw" if d else "pw"
    xs = NL - 2 * last
    nx = P - xs
    o12 = 2 * last
    D1X = CX + CAPP - xs - C1
    ea = 5 if last else 6
    eb = 5 if last or d else 6
    LO, HI = (0, 1, 2, 3), (4, 5, 6, 7)

    def cells(k, a, w, at, s):
        for x in "qs":
            send(-k, R("wn" + x, a, a + w), R("win" + x, at, at + w), s + x)

    for k, a, w, s in ((1, NE, P, "an1"), (2, N2, P, "an2"), (3, N3, nx, "an3"), (1, N1 + NL, nx, "an12")):
        lands(k, R("wnq", a, a + w), s + "q")
        lands(k, R("wns", a, a + w), s + "s")
    lands(-1, R("land1"), "am1")
    lands(-1, R("land3"), "am3")
    lands(1, R("land2"), "am2")
    lands(1, R("offl"), "am4")
    lands(1, R("plandq"), "apq")
    lands(1, R("plands"), "aps")

    dma("y", ap(R("hx", 0, 4 * P)), T.x[:, :], [], [R("hx", 0, 4 * P)])
    dma("y", ap(R("hv")), T.u[:, 0:8], [], [R("hv")])
    dma("y", view(R("wtq")), T.wc[:, :], [], [R("wtq")])
    dma("y", ap(R("wts")), T.ws[:, :], [], [R("wts")])

    iota(R("qi"), [[0, 1]], 0, 1)
    iota(R("t0"), [[16, 10]])
    iota(R("tmod"), [[0, 16], [1, 16]])
    fill(R("small", 0, SMALL["z0"][0]), 0.0)
    ts(R("qj"), R("qi"), 15, A.bitwise_and)
    fill(R("small", SMALL["z0"][0], SMALL["qf"][0]), -BIG)
    cp(R("qf"), R("qj"))
    fill(R("ones"), 1.0)
    ts(R("pw"), R("t0"), R("qf"), A.add)
    fill(R("cum", 0, 2), 0.0)
    fill(R("eb0"), BIG)

    if d:
        fill(R("hx", 4 * P, 4 * P + 8), 0.0)
        quant("win", WIN, P + 2, "hx")
    quant("win", CN, P, "hx")
    quant("win", CN + P, 128, "hx")
    cells(1, NE, P, WIN + 1 if d else CN, "an1")
    cells(2, N2, P, C1 + shift[2], "an2")
    for t in range(4):
        ts(R("huab", t, 512, 4), R("ones", 0, 128), R("hv", t, t + 1), A.mult)
        act(R("huab", 512 + t, 1024, 4), R("ones", 0, 128), 0.0, R("hv", 4 + t, 5 + t))
    ts(R("msk"), R("tmod", 0, 192), R("qf"), A.is_equal)
    quant("uab", 0, 256, "huab")
    ts(R("keep"), R("tmod", 0, 192), 0.0, A.not_equal)
    cp(R("hx", 4 * (HE - 2), 4 * HE), R("hx", 4 * CAPP, 4 * CAPP + 8), "s")
    mm(7, "uab", 0, "win", C1, P)
    lefts(LO, "win", CN, P)
    mask("ma", 0, PS(7, 0, P), 0)
    turn(R("tr", 0, 64), PS(7, NL, P))
    cp(R("msg1", 14, 16), R("tr", 0, 64, 32), "s")
    cp(R("a1d"), PS(7, 0, NL), "s")
    lefts(HI, "win", C1, 128)
    quant("win", C2 - V0, 128, "hx", V0)
    quant("wn", LB - V0, 128, "hx", V0)
    quant("wn", LB + NL, 128, "hx")
    if not RQ["one"]:
        quant("wn", C3 - 128, 128, "hx")
    squeeze("sa", "ma", 0, P)
    ts(R("hold"), R("tmod"), R("qf"), A.is_le, 1024.0, A.mult)
    ts(R("geq"), R("tmod", 0, CAPP), R("qf"), A.not_equal, -BIG, A.mult)
    act(R("rst"), R("keep", 0, P), 2 * BIG, -BIG)
    act(R("pw5"), R("pw"), 1.0, 512.0)
    act(R("cst", 0, 1), R("qf"), 0.0)
    for i in range(3):
        ts(R("cle", 256 * i, 256 * i + 256), R("tmod"), R("qf"), A.is_le, 256.0 ** i, A.mult)
        act(R("cgt", 256 * i, 256 * i + 256), R("hold"), -256.0 ** i / 1024, 256.0 ** i)
    fill(R("c0", 2, 18, 3), 1.0)
    fill(R("e0", 1, 20, 2), float(S3 - V0 - N4))
    if d:
        ts(R("t1"), R("pw"), P - 1.5, A.is_gt, -float(P), A.mult)
        act(R("jw"), R("pw"), 1.0, 1.0)
        tt(R("jw"), R("jw"), R("t1"), A.add)
    if d or last:
        fill(R("db1"), 256.0)
        cp(R("db1", 2, 30, 3), R("pw"), "s")
    if last:
        ts(R("t2"), R("pw"), NL - 1.5, A.is_gt, float(o12), A.mult)
        act(R("da1", 1, 30, 3), R("t2"), 1.0, float(N1 - C3))
        act(R("da1", 0, 30, 3), R("t2"), -1.0, float(N2 - N1))
    else:
        fill(R("da1"), float(N2 - N1))
    for a, b, c in ((0, D1L, 0.0), (D1L, D2L, 1.0), (D2L, CX + CAPP - C1, 2.0), (CX + CAPP - C1, WIN - C1, 1.0)):
        act(R("spw", a, b), R("huab", 0, b - a), 0.0, c)
    cp(R("msg1", 0, 10), W("sa", 0, 10), "s")
    for a in (0, 6):
        cp(R("aw", a, a + 6), W("sa", 0, 6), "s")
    act(R("k64"), R("pw", 0, 6), -1.0, float(CAPP))
    cp(R("c1", 2, 18, 3), R("pw", 0, 6), "s")
    act(R("eb0", 0, CAPP, 16), R("pw", 6, 10), -1.0 / nx, -D1X / nx)
    cp(R("e1", 1, 8, 2), R("pw", 6, 10), "s")
    cp(R("e1", 9, 20, 2), R("pw", 0, 6), "s")
    if d or last:
        ts(R("e15"), R("qf"), 15.0, A.is_equal)
    if d:
        act(R("g5"), R("e15"), -BIG)
    if last:
        fill(R("sl", NL - 1, NL), BIG)
        act(R("kt"), R("e15"), float(CAPP - NL))
        act(R("da"), R("e15"), (D1X - D1L) / 2.0, D1L / 2.0)
        act(R("k5e"), R("e15"), -(D1X + D2L) / 2.0)
        act(R("d2e"), R("e15"), (D2L - D1X) / 2.0)
        ts(R("md", 0, 15), R("msk", 0, 15), -BIG, A.mult)
    cp(R("da1", 2, 30, 3), R(jw), "s")

    rights(LO, "wn", NE, P)
    for t in range(4):
        relu(RQ["e"][t], "hx", P, t, t, 0, CAPP)
    quant("win", C2 + V0 + 2 * d, 128, "hx", NL + 2 * d)
    cells(1, N1 + NL, CAPP + 2 * d, C2 + NL - d, "an12")
    for t in range(4):
        relu(RQ["l"][t], "hx", HE, t, t, CAPP, P)
    mm(0, "uab", 128, "wn", N1 - V0, 128)
    mm(1, "uab", 0, "win", C1, 128, True, False)
    tt(R("sl", 0, NL - last), PS(0, V0, 128 - last), R("a1d", 0, NL - last), A.add)
    mask("ma", 256, PS(0, V0 + d, 128 - last), 0)
    if d:
        mask("ma", 415, PS(0, V0, V0 + 1), 15)
    mm(2, "uab", 0, "win", C2 + V0, 128)
    mask("me", 0, PS(2, CAPP, 128), 0)
    squeeze("se", "me", 0, 64)
    cp(R("msg1", 10, 14), W("se", 0, 4), "s")

    rights(HI, "wn", N2, 128)
    mm(1, "uab", 128, "wn", N2, 128, False, True)
    mm(3, "uab", 0, "win", C2 + V0, 128, True, False)
    mm(3, "uab", 128, "wn", N2 + V0, 128, False, True)
    turn(R("tr", 64, 128), PS(3, CAPP, 128))
    cp(R("msg1", 16, 18), R("tr", 64, 128, 32), "s")
    send(1, R("land1"), R("msg1"), "am1")
    for t in range(4):
        relu(RQ["n"][t], "hx", HE + NL, t, HI[t], 0, NL)
    quant("win", CL, 2 * NL, "hx", HE)
    mm(0, "uab", 0, "win", CL, 2 * NL)
    tt(R("nle"), PS(1, 0, NL), R("sl"), A.is_le)
    scan(R("cum", 2, 2 + NL), R("ones", 0, NL), R("nle"))
    scan(R("cw"), R("hold", 0, NL), R("cum", 2, 2 + NL), A.add, A.min)
    scan(R("cx"), R("hold", 0, NL), R("cum", 1, 1 + NL), A.add, A.min)
    ff = R("nf", 6, 12)
    tt(ff, W("cw", 0, 6), W("cx", 0, 6), A.is_equal)
    for a in (0, 12):
        act(R("nf", a, a + 6), ff, -1.0, 1.0)
    if RQ["th"] == "v":
        tt(R("xx"), ff, R("k64"), A.mult)
        tt(R("msg3", 0, 6), W("cw", 0, 6), R("xx"), A.add)
    else:
        for c in range(6):
            act(R("msg3", c, c + 1), R("nf", 6 + c, 7 + c), R("k64", c, c + 1), W("cw", 16 * c, 1))
    tt(R("yy"), R("aw"), R("nf", 6, 18), A.mult)
    mask("mc", 0, PS(0, 0, 2 * NL), 0)
    squeeze("sc", "mc", 0, 2 * NL)
    tt(R("yz"), W("sc", 0, 12), R("nf", 0, 12), A.mult)
    tt(R("msg3", 6, 18), R("yz"), R("yy"), A.add)
    send(1, R("land3"), R("msg3"), "am3")
    x3 = NL - 2 * ((rank - 3) % n == n - 1)
    cells(3, N3, P - x3, C1 + x3 + shift[3], "an3")

    mm(2, "uab", 128, "wn", N2, 128)
    mm(1, "uab", 128, "win", C2 + V0 + 2 * d, 128)
    tt(R("sxe"), PS(3, CAPP, 128), R("geq"), A.add)
    cp(R("sx", 0, nx), PS(3, xs - V0, 128), RQ["sx"])
    lefts(HI, "win", C2 + V0, 128)
    rights(HI, "wn", N2 + V0, 128)
    for t in range(4):
        relu(RQ["x"][t], "hx", HE + 2 * NL, t, HI[t], CAPP, 128)
    mm(5, "uab", 0, "win", C1 + V0, 128, True, False)
    turn(R("tb"), PS(1, CAPP - d, 128 - d))
    mask("ma", P, PS(2, d, NL + d), 0)
    lefts(LO, "win", C1 + V0, 128)
    squeeze("sa", "ma", P, 256 + 16 * eb)
    for a in (0, 6):
        cp(R("b3w", a, a + 6 - d), W("sa", P, 6 - d), "s")
        if d:
            act(R("b3w", a + 5, a + 6), W("sa", P + 80, 1), 1.0, R("g5"))
    act(R("c0", 1, 18 - 3 * last, 3), R("nf", 6, 12 - last), -(D1L + D2L) / 2.0, D1L / 2.0)
    act(R("c1", 1, 18 - 3 * last, 3), R("nf", 6, 12 - last), (D2L - D1L) / 2.0, D1L / 2.0)
    if last:
        act(R("a0"), R("nf", 11, 12), -(D1L + D2L) / 2.0, R("da"))
        act(R("a1"), R("nf", 11, 12), (D2L - D1L) / 2.0, R("da"))

    v12 = N1 + o12 + V0
    mm(5, "uab", 128, "wn", v12, 128, False, True)
    rights(LO, "wn", v12, 128)
    mm(7, "uab", 128, "wn", v12, 128)
    tt(R("fr", 0, nx), PS(5, xs - V0, 128), R("sx", 0, nx), A.is_lt)
    act(R("junk", 0, CAPP), R("fr", nx - CAPP, nx), 1.0, 1.0 / 128, ACT.Identity, R("nb"))
    tt(R("nfe"), PS(5, CAPP, 128), R("sxe"), A.is_lt)
    if last:
        f95 = R("fr", 1, 2)
        act(R("t5"), f95, R("kt"), R("msg3", 5, 6))
        ts(R("c0", 16, 17), f95, R("k5e"), A.mult, R("a0"), A.add)
        ts(R("c1", 16, 17), f95, R("d2e"), A.mult, R("a1"), A.add)
        act(R("c1", 15, 16), R("t5"), -1.0, R("nb"), ACT.Sign)
    act(R("c1", 0, 18 - 3 * last, 3), R("msg3", 0, 6 - last), -1.0, R("nb"), ACT.Sign)
    scan(R("co"), R("c0"), R("c1"))
    one = RQ["one"]
    if one:
        cp(R("offa", 0, 6), R("co", 2, 18, 3))
    else:
        cp(R("offa", 0, ea), R("co", 2, 3 * ea, 3))
        pick("wn", C3, "win", C1, CX, "offa", 16 * ea)
    dma("y", ap(R("hu")), T.u[:, :], [R("co")], [R("hu")])
    for t in range(4):
        relu(RQ["y"][t], "hx", HE + 256, t, t, xs - V0, 128)
    scan(R("sq"), R("eb0"), R("nfe"), A.min)
    if last and not one:
        cp(R("offb", 0, 1), R("co", 17, 18))
    ts(R("offa", 6, 10) if one else R("offb", last, last + 4), W("sq", 0, 4), -float(nx), A.mult, 0.25, A.add)
    quant("win", CX, nx + CAPP, "hx", HE + 2 * NL)
    lo = NL - d - last
    mask("ma", 256 + lo, PS(7, NL - V0 - last, 128), lo)
    squeeze("sa", "ma", 256 + 16 * eb, 416)
    for c in range(10):
        act(R("ga", 16 * c, 16 * c + 16), R("geq", 0, 16), 1.0, R("land1", c, c + 1))

    def score(a, src):
        tt(R("mf", a, a + src[2] - src[1]), src, R("ga", a, a + src[2] - src[1]), A.add)

    def most(a, b):
        scan(R("sf", a, b), R("rst", 0, b - a), R("mf", a, b), A.min, A.max)

    if one:
        pick("wn", C3, "win", C1, WIN, "offa")
        mm(4, "uab", 128, "wn", C3, P)
        score(0, PS(4, d, P))
        if d:
            score(P - 1, PS(4, 0, 1))
        most(0, P)
    else:
        pick("wn", C3 + 16 * ea, "win", C1, WIN, "offb", P - 16 * ea)
        va = 16 * ea - 128
        mm(4, "uab", 128, "wn", C3 + va, 128)
        score(0, PS(4, d - va, 128))
        if d:
            score(P - 1, PS(4, -va, 1 - va))
        most(0, 16 * eb)
        mm(6, "uab", 128, "wn", C3 + V0, 128)
        score(16 * ea - d, PS(6, 16 * ea - V0, 128))
        most(16 * eb, P)
    for b in (0, 1):
        ts(R("fx", 32 * b, 32 * b + 32), R("tb", 32 * b, 32 * b + 32), R("land1", 14 + b, 15 + b), A.add,
           R("land1", 16 + b, 17 + b), A.is_lt)
    turn(R("fy"), R("fx"))
    act(R("junk", 64, 128), R("fy"), -GATE, -GATE / 128, ACT.Identity, R("nr"))
    act(R("junk", 128, 192), R("fy"), GATE, GATE / 128, ACT.Identity, R("nq"))
    act(R("z0", 1, 12, 2), R("land3", 0, 6), -GATE, R("nq"))
    act(R("z0", 13, 24, 2), R("land3", 0, 6), GATE, R("nr"))
    tt(R("z1", 0, 24, 2), R("land3", 6, 18), R("b3w"), A.add)
    if RQ["s2"][0] == "v":
        tt(R("z1", 13, 24, 2), R("land1", 0, 6), W("sa", 256, 6), A.add)
    else:
        for c in range(6):
            act(R("z1", 13 + 2 * c, 14 + 2 * c), W("sa", 256 + 16 * c, 1), 1.0, R("land1", c, c + 1))
    if RQ["s2"][1] == "v":
        tt(R("thr", 6, 10), R("land1", 10, 14), W("sa", 256 + NL, 4), A.add)
    else:
        for c in range(6, 10):
            act(R("thr", c, c + 1), W("sa", 256 + 16 * c, 1), 1.0, R("land1", 4 + c, 5 + c))
    scan(R("zz"), R("z0"), R("z1"), A.min, A.max)
    tt(R("thr", 0, 6), R("zz", 1, 12, 2), R("zz", 13, 24, 2), A.max)
    tt(R("d0", 1, 18, 3), R("thr", 0, 6), R("z1", 13, 24, 2), A.is_gt)
    tt(R("d0", 2, 30, 3), W("sf", 0, 10), R("thr"), A.is_lt)
    tt(R("msg2", 1 - d, 5), W("sf", 96 - 16 * d, 4 + d), R("thr", 6 - d, 10), A.max)
    send(-1, R("land2", 1 - d, 5), R("msg2", 1 - d, 5), "am2")
    scan(R("so"), R("d0"), R("da1"))
    if d or last:
        scan(R("sp"), R("d0"), R("db1"))
        cp(R("offq"), R("sp", 2, 30, 3))
    cp(R("offp"), R("so", 2, 30, 3))
    pick("pool", 0, "wn", C3, N3, "offp")
    send(-1, R("offl"), R("offq" if d or last else "offp"), "am4")
    send(-1, R("plandq"), R("poolq"), "apq")
    send(-1, R("plands"), R("pools"), "aps")
    iota(R("spr", 0, CAPP), [[0, CAPP]], 1)
    iota(R("spr", CAPP, P), [[0, NL]])
    iota(R("cst", 1, 769), [[1, 3], [0, 256]], 1)

    v3 = N3 + nx - 128
    mm(5, "uab", 0, "wn", C3 + V0, 128, True, False)
    mm(5, "uab", 128, "wn", v3, 128, False, True)
    lefts(LO, "wn", C3 + V0, 128)
    rights(LO, "wn", v3, 128)
    quant("wn", LB + 256, P, "hx", CAPP)
    c0 = 0 if last else 16
    mask("md", 16 - last, PS(5, CAPP - last, 128), 16 - last)
    squeeze("sd", "md", c0, 80)
    quant("uu", 0, 128, "hu")
    mm(7, "uu", 0, "win", C2, P)
    mm(4, "uu", 0, "wn", C3, P)
    for t in range(4):
        relu(RQ["z"][t], "hx", HE + 2 * NL - nx, t, t, xs - V0, 128)
    gather("s", R("spr", P + CAPP, P + CAPP + 16 * (6 if one else ea)), R("spw"), "offa", 6 if one else ea)
    if one:
        gather("s", R("spr", P, P + CAPP), R("spw"), "offa", 10, 6)
        if last:
            pick("wn", S3 - NL, "win", C1, WIN, "offa", 32, 4)
    elif last:
        gather("s", R("spx"), R("spw"), "offb", 5)
        cp(R("spr", 2 * P - 16, 2 * P), R("spx", 0, 16), "s")
        cp(R("spr", P, P + CAPP), R("spx", 16, 80), "s")
        pick("wn", S3 - 80, "win", C1, WIN, "offb", 16)
    else:
        gather("s", R("spr", P, P + CAPP), R("spw"), "offb", 4)
    quant("wn", S3, 128, "hx", HE + CAPP)
    for w, b in ((0, 7), (1, 4)):
        cp(R("ysb", w * P, w * P + CAPP), PS(b, NL, P), "s")
        cp(R("ysb", w * P + CAPP, w * P + P), PS(b, 0, NL), "s")
    dma("y", T.y[:, 0:2 * P], ap(R("ysb", 0, 2 * P)), [R("ysb", 0, 2 * P), R("plands")], [])

    if last:
        tt(R("u6"), W("sd", 0, 5), R("land2"), A.is_gt)
        cp(R("e1", 0, 8, 2), R("u6", 1, 5), "s")
        cp(R("e1", 18, 19), R("u6", 0, 1), "s")
        tt(R("v0"), R("u6"), R("pw5", 5, 10), A.mult)
    else:
        tt(R("e1", 0, 8, 2), W("sd", 16, 4), R("land2", 1, 5), A.is_gt)
        tt(R("v0", 1, 5), R("e1", 0, 8, 2), R("pw5", 6, 10), A.mult)
    nc = 6 - last
    pick("left", 0, "wn", LB, C3 + P, "offl")
    lefts(LO, "left", 0, P)
    rights(LO, "pland", 0, P)
    cp(R("offk", 4, 4 + nc), R("offl", 0, nc))
    for c in range(4):
        ts(R("offk", c, c + 1), R("offl", 6 + c, 7 + c), R("v0", 1 + c, 2 + c), A.max)
    if last:
        ts(R("offk", 9, 10), R("offl", 5, 6), R("v0", 0, 1), A.max)
    gather("v", R("wr"), R("cle"), "offk")
    gather("s", R("wg", 16, P + 16), R("cgt"), "offk")
    ts(R("v3"), R("offk"), 255.5, A.is_lt, 1.0 / 65536, A.max)
    ts(R("v4"), R("offk"), 511.5, A.is_lt, 1.0 / 256, A.mult)
    ts(R("v5"), R("offk"), 1.0, A.add, 1.0 / 128, A.mult)
    scan(R("eo"), R("e0"), R("e1"))
    scan(R("sf"), R("wg", 0, P), R("wr"), A.add, A.add, -(CAPP + 1.0) * (1 + 256 + 65536))
    tt(R("v2"), R("v3"), R("v4"), A.max)
    tt(R("ci"), W("sf", 0, 10), R("v2"), A.mult)
    ts(R("cj"), R("ci"), N4 - C3, A.bitwise_and)
    tt(R("v7"), R("cj"), R("eo", 1, 20, 2), A.add)
    tt(R("v6"), R("cj"), R("v5"), A.mult)
    for t in range(4):
        relu(RQ["w"][t], "h4", 0, t, t, 0, P)
    cp(R("off4"), R("v7"))
    quant("wn", N4, P, "h4")
    cp(R("offt"), R("v6"))
    pick("c4", 0, "wn", C3, WN, "off4")
    gather("v", R("spr", 2 * P, 3 * P), R("cst"), "offt")
    mm(6, "uu", 0, "c4", 0, P)
    dma("y", T.oc[:, :], view(R("c4q")), [R("c4q")], [])
    cp(R("ysb", 2 * P, 3 * P), PS(6, 0, P), "s")
    dma("s", T.y[:, 2 * P:3 * P], ap(R("ysb", 2 * P, 3 * P)), [R("ysb", 2 * P, 3 * P)], [])
    for k in range(4):
        dma(RQ["o"][k], T.osc[4 * k:4 * k + 4, :], T.c4s[32 * k:32 * k + 4, :], [R("c4s")], [])
    dma("y", T.sp[0:1, :], T.spr[0:1, :], [R("spr")], [])

    for i in ORDER.get(rank, range(len(prog))):
        prog[i][1]()
    for k in SEMAPHORES:
        if count[k]:
            wait("g", (k, count[k]))
